import numpy as np
import ml_dtypes


def mxq(x, axis, fmt="e4m3"):
    dtype, down = {"e4m3": (ml_dtypes.float8_e4m3fn, 7), "e5m2": (ml_dtypes.float8_e5m2, 14)}[fmt]
    v = np.moveaxis(np.asarray(x, np.float32).astype(ml_dtypes.bfloat16).astype(np.float64), axis, -1)
    blocks = v.reshape(v.shape[:-1] + (-1, 32))
    amax = np.abs(blocks).max(-1, keepdims=True)
    byte = np.maximum(np.where(amax > 0, np.frexp(amax)[1] - 1 + 127, 0) - down, 1)
    scale = np.exp2(byte - 127.0)
    codes = (blocks / scale).astype(np.float32).astype(dtype).astype(np.float64)
    return np.moveaxis((codes * scale).reshape(v.shape), -1, axis)


WIDE = False


def mx_kscale(k):
    if not WIDE:
        return np.ones(k)
    levels = np.array([10, -10, 5, -5, 0])
    if k % 512:
        return np.exp2(np.random.permutation(np.resize(levels, k // 32))).repeat(32)
    a = np.empty((k // 512, 16))
    for p in range(k // 512):
        a[p, :8] = np.random.permutation(np.resize(levels, 8))
        for g in range(8):
            far = levels[np.abs(levels - a[p, g]) >= 10]
            a[p, g + 8] = far[np.random.randint(len(far))]
    return np.exp2(a.ravel()).repeat(32)


def f64(x):
    return np.asarray(x).astype(np.float64)


def striped(idx):
    return np.tile(idx.reshape(-1, 16).T, (8, 1)).astype(np.uint16)


def unstriped(offs):
    return offs[:16].T.reshape(-1).astype(np.int64)


E2M1 = np.array([0.0, 0.5, 1.0, 1.5, 2.0, 3.0, 4.0, 6.0, -0.0, -0.5, -1.0, -1.5, -2.0, -3.0, -4.0, -6.0])


def pack_weight(w, fmt):
    k, n = w.shape
    w = f64(np.asarray(w, np.float32).astype(ml_dtypes.bfloat16)).reshape(k // 32, 32, n)
    amax = np.abs(w).max(1)
    if fmt == "e4m3":
        byte = np.frexp(amax)[1] - 1 + 127 - 7
    else:
        mant, ex = np.frexp(amax / 6.0)
        byte = np.where(mant > 0.5, ex, ex - 1) + 127
    byte = np.clip(np.where(amax > 0, byte, 1), 1, 254)
    scaled = (w * np.exp2(127.0 - byte)[:, None, :]).reshape(k, n).astype(np.float32)
    by_word = np.ascontiguousarray(scaled.reshape(k // 512, 128, 4, n).transpose(0, 1, 3, 2))
    if fmt == "e4m3":
        words = by_word.astype(ml_dtypes.float8_e4m3fn).view(np.uint8)
    else:
        c = by_word.astype(ml_dtypes.float4_e2m1fn).view(np.uint8) & 0xF
        words = (c[..., 0::2] | (c[..., 1::2] << 4)).reshape(k // 512, 128, 2 * n)
    return np.ascontiguousarray(words), np.ascontiguousarray(byte.astype(np.uint8).reshape(k // 512, 16, n))


def unpack_weight(words, scales, fmt):
    g, _, n = scales.shape
    words = np.ascontiguousarray(words).reshape(g, 128, n, -1)
    if fmt == "e4m3":
        vals = words.view(ml_dtypes.float8_e4m3fn).astype(np.float64)
    else:
        nib = np.empty((g, 128, n, 4), np.uint8)
        nib[..., 0::2] = words & 0xF
        nib[..., 1::2] = words >> 4
        vals = E2M1[nib]
    vals = vals * np.repeat(np.exp2(scales.astype(np.float64) - 127.0), 8, axis=1)[..., None]
    return vals.transpose(0, 1, 3, 2).reshape(g * 512, n)


def gelu(v):
    return 0.5 * v * (1.0 + np.tanh(np.sqrt(2.0 / np.pi) * (v + 0.044715 * v**3)))


def striped8(idx):
    return np.concatenate([v.reshape(-1, 16).T for v in idx]).astype(np.uint16)


def unstriped8(offs):
    return np.stack([offs[16 * g:16 * g + 16].T.reshape(-1) for g in range(8)]).astype(np.int64)


def runs(v, idx8):
    k = np.arange(v.shape[0])
    return v[k[:, None], idx8[k % 512 // 64]]


K, T, S, H, N = 1024, 2048, 1024, 1024, 256

def setup_inputs():
    n = np.random.standard_normal
    s = mx_kscale(K)[:, None]
    u = mx_kscale(H)[:, None]
    tab_words, tab_scales = pack_weight(n((K, T)) * s, "e4m3")
    offs = striped8(np.stack([np.random.permutation(T)[:S] for _ in range(8)]))
    w1 = n((K, H)) / np.sqrt(K) / s
    w2_words, w2_scales = pack_weight(n((K, H)) / np.sqrt(K) / s * u.T, "e2m1")
    quad = n(H) * u[:, 0]
    cons = n(H) * u[:, 0]
    w3_words, w3_scales = pack_weight(n((H, N)) / np.sqrt(H) / u, "e4m3")
    return {
        "tab_words": tab_words, "tab_scales": tab_scales,
        "offs": offs,
        "w1": w1.astype(np.float32),
        "w2_words": w2_words, "w2_scales": w2_scales,
        "quad": quad.astype(np.float32),
        "cons": cons.astype(np.float32),
        "w3_words": w3_words, "w3_scales": w3_scales,
    }

def reference(tab_words, tab_scales, offs, w1, w2_words, w2_scales, quad, cons, w3_words, w3_scales):
    v = runs(unpack_weight(tab_words, tab_scales, "e4m3"), unstriped8(offs))
    w1q = mxq(f64(w1), 0, "e4m3")
    w2 = unpack_weight(w2_words, w2_scales, "e2m1")
    w3 = unpack_weight(w3_words, w3_scales, "e4m3")
    x = w1q.T @ v
    b = w2.T @ v
    h = (f64(quad)[:, None] * x + b) * x + f64(cons)[:, None]
    hq = mxq(h, 0, "e4m3")
    return w3.T @ hq

@@ -1,0 +1,316 @@
+from contextlib import ExitStack
+
+import concourse.mybir as mybir
+
+K, T, S, H, N = 1024, 2048, 1024, 1024, 256
+FLOPS = 2 * (2 * K * H * S + H * N * S)
+
+F32 = mybir.dt.float32
+BF16 = mybir.dt.bfloat16
+I32 = mybir.dt.int32
+U32 = mybir.dt.uint32
+U16 = mybir.dt.uint16
+U8 = mybir.dt.uint8
+FP8X4 = mybir.dt.float8_e4m3fn_x4
+FP4X4 = mybir.dt.float4_e2m1fn_x4
+MULT = mybir.AluOpType.mult
+ADD = mybir.AluOpType.add
+IDENT = mybir.ActivationFunctionType.Identity
+
+P = 128
+PACK = 4
+KP = P * PACK
+NT = 512
+PASSES = K // KP
+BLOCKS = H // KP
+HALVES = S // NT
+E_ENGINE = ("v", "v", "s", "v", "v")
+CAST_ENGINE = "s"
+CAST_AT = ((0,), (1,), (2, 3), (4,), (5, 6), (7,))
+LAST_CHUNKS = ((0, 256), (256, 512))
+
+
+def tile_list_seawater_horner_surrogate_kernel(
+    tc, tab_words, tab_scales, offs, w1, w2_words, w2_scales, quad, cons, w3_words, w3_scales, out
+):
+    nc = tc.nc
+    with ExitStack() as ctx:
+        keep = ctx.enter_context(tc.tile_pool(name="keep", bufs=1))
+        ring = ctx.enter_context(tc.tile_pool(name="ring", bufs=2))
+        psum = ctx.enter_context(tc.psum_pool(name="psum", bufs=1))
+
+        offsets = keep.tile([P, S // 16], U16, name="offsets")
+        nc.sync.dma_start(offsets[:], offs)
+
+        ts_win = keep.tile([P, T], U8, name="ts_win", align_bytes=64)
+        nc.gpsimd.memset(ts_win[:].bitcast(I32), 0)
+        for a in range(PASSES):
+            nc.sync.dma_start(ts_win[4 * a : P : 8, :].bitcast(I32), tab_scales[a].bitcast(I32))
+
+        w2s_raw = keep.tile([P, PASSES, H], U8, name="w2s_raw", align_bytes=64)
+        nc.vector.memset(w2s_raw[:].rearrange("p a c -> p (a c)").bitcast(I32), 0)
+        for d in range(4):
+            nc.gpsimd.dma_start(
+                w2s_raw[32 * d : 32 * d + 4, :, :].bitcast(I32),
+                w2_scales[:, 4 * d : 4 * d + 4, :].rearrange("a r c -> r a c").bitcast(I32),
+            )
+        q_col = keep.tile([P, BLOCKS, PACK], F32, name="q_col")
+        c_col = keep.tile([P, BLOCKS, PACK], F32, name="c_col")
+
+        v_plane = []
+        for a in range(PASSES):
+            plane = keep.tile([P, S], U8, name=f"v_plane{a}", align_bytes=64)
+            nc.vector.memset(plane[:].bitcast(I32), 0)
+            v_plane.append(plane)
+
+        w2_raw = keep.tile([P, PASSES, H // 2], I32, name="w2_raw", align_bytes=64)
+        nc.sync.dma_start(w2_raw[:], w2_words.rearrange("a p c -> p a c").bitcast(I32))
+        tab_win = []
+        for a in range(PASSES):
+            win = keep.tile([P, T], I32, name="tab_win", tag=f"big{a}", align_bytes=64)
+            nc.sync.dma_start(win[:], tab_words[a].rearrange("p t i -> p (t i)").bitcast(I32))
+            tab_win.append(win)
+
+        def load_w1(a, b):
+            raw = keep.tile([P, PACK, KP], F32, name="w1_raw", tag=f"big{2 * (1 - b) + a}", align_bytes=64)
+            nc.sync.dma_start(
+                raw[:],
+                w1[a * KP : (a + 1) * KP, b * KP : (b + 1) * KP].rearrange("(p j) c -> p j c", j=PACK),
+            )
+            return raw
+
+        w1_raw = {(a, 0): load_w1(a, 0) for a in range(PASSES)}
+        nc.scalar.dma_start(q_col[:], quad.rearrange("(b p t) -> p b t", p=P, t=PACK))
+        nc.scalar.dma_start(c_col[:], cons.rearrange("(b p t) -> p b t", p=P, t=PACK))
+
+        ts_got = keep.tile([P, S], U8, name="ts_got", align_bytes=64)
+        nc.vector.tensor_copy(ts_got[:], ts_win[:].indirect(offsets[:]))
+        for a in range(PASSES):
+            for r in range(4):
+                eng = nc.scalar if r % 2 == 0 else nc.gpsimd
+                eng.dma_start(
+                    v_plane[a][r:P:32, :].bitcast(I32), ts_got[8 * r + 4 * a : P : 32, :].bitcast(I32)
+                )
+
+        w2p, w2sp = [], []
+
+        def permute_w2(b):
+            words = keep.tile([P, PASSES, PACK, 2 * P], U8, name=f"w2p{b}", align_bytes=64)
+            src = w2_raw[:].bitcast(U16)[:, :, b * KP : (b + 1) * KP]
+            nc.vector.tensor_copy(words[:].bitcast(U16), src.rearrange("p a (m t) -> p a t m", t=PACK))
+            scales = keep.tile([P, PASSES, PACK, P], U8, name=f"w2sp{b}", align_bytes=64)
+            ssrc = w2s_raw[:, :, b * KP : (b + 1) * KP]
+            nc.vector.tensor_copy(scales[:], ssrc.rearrange("p a (m t) -> p a t m", t=PACK))
+            w2p.append(words)
+            w2sp.append(scales)
+
+        permute_w2(0)
+
+        v_words = {}
+        for a in range(PASSES):
+            for s in range(HALVES):
+                got = keep.tile([P, NT], I32, name=f"v_words{a}{s}", align_bytes=64)
+                lists = offsets[:, s * (NT // 16) : (s + 1) * (NT // 16)]
+                nc.vector.tensor_copy(got[:].bitcast(U32), tab_win[a][:].bitcast(U32).indirect(lists))
+                v_words[a, s] = got
+
+        w1_codes = [keep.tile([P, PASSES, KP], U32, name=f"w1c{b}", align_bytes=64) for b in range(BLOCKS)]
+        w1_scales = [keep.tile([P, PASSES, KP], U8, name=f"w1s{b}", align_bytes=64) for b in range(BLOCKS)]
+        w1_bf = [keep.tile([P, PASSES, PACK * KP], BF16, name=f"w1b{b}", align_bytes=64) for b in range(BLOCKS)]
+
+        def cast_views(a, b):
+            dst = w1_bf[b][:, a, :].rearrange("p (t m j) -> p m j t", t=PACK, j=PACK)
+            src = w1_raw[a, b][:].rearrange("p j (m t) -> p m j t", t=PACK)
+            return dst, src
+
+        def quantize_w1(b, a, c0, c1):
+            nc.vector.quantize_mx(
+                out=w1_codes[b][:, a, c0:c1].bitcast(FP8X4),
+                scales=w1_scales[b][:, a, c0:c1],
+                in_=w1_bf[b][:, a, PACK * c0 : PACK * c1],
+            )
+
+        for a in range(PASSES):
+            w1_raw[a, 1] = load_w1(a, 1)
+        permute_w2(1)
+        nc.scalar.copy(*cast_views(0, 0))
+        nc.vector.tensor_copy(*cast_views(1, 0))
+        for c0, c1 in ((0, P), (P, 2 * P), (2 * P, KP)):
+            for a in range(PASSES):
+                quantize_w1(0, a, c0, c1)
+        b_first = keep.tile([P, 2, NT], F32, name="b_first", tag="big2", align_bytes=64)
+
+        def cast_piece(k):
+            a, h = divmod(k, 4)
+            dst, src = cast_views(a, 1)
+            ms = slice(h * 32, (h + 1) * 32)
+            if CAST_ENGINE == "g":
+                nc.gpsimd.tensor_scalar(dst[:, ms], src[:, ms], 1.0, 0.0, MULT, ADD)
+            else:
+                nc.scalar.copy(dst[:, ms], src[:, ms])
+
+        w3c = keep.tile([P, PASSES, N], I32, name="w3c", tag="big3", align_bytes=64)
+        nc.sync.dma_start(w3c[:], w3_words.rearrange("a p c i -> p a (c i)").bitcast(I32))
+        w3s_box = []
+
+        def load_w3s():
+            w3s = keep.tile([P, PASSES, N], U8, name="w3s", tag="big0", align_bytes=64)
+            nc.gpsimd.memset(w3s[:].rearrange("p a c -> p (a c)").bitcast(I32), 0)
+            for d in range(4):
+                nc.sync.dma_start(
+                    w3s[32 * d : 32 * d + 4, :, :].bitcast(I32),
+                    w3_scales[:, 4 * d : 4 * d + 4, :].rearrange("a r c -> r a c").bitcast(I32),
+                )
+            w3s_box.append(w3s)
+
+        groups = [(b, s) for b in range(BLOCKS) for s in range(HALVES)]
+        last = len(groups) - 1
+        units = [(g, t) for g in range(len(groups)) for t in range(PACK)]
+        chunks = [(g, 0, NT) for g in range(last)] + [(last, c0, c1) for c0, c1 in LAST_CHUNKS]
+        steps = [(ch, t) for ch in range(len(chunks)) for t in range(PACK)]
+        b_sb, x_ps, t_pair, h_planes, h_il, h_q = {}, {}, {}, {}, {}, {}
+
+        def matmul_b(u):
+            g, t = units[u]
+            b, s = groups[g]
+            acc = psum.tile([P, NT], F32, name="b_ps", tag=f"b{u % 2}")
+            for a in range(PASSES):
+                nc.tensor.matmul_mx(
+                    out=acc[:],
+                    lhsT=w2p[b][:, a, t, :].bitcast(FP4X4),
+                    lhsT_scale=w2sp[b][:, a, t, :],
+                    rhs=v_words[a, s][:].bitcast(FP8X4),
+                    rhs_scale=v_plane[a][:, s * NT : (s + 1) * NT],
+                    start=(a == 0),
+                    stop=(a == PASSES - 1),
+                )
+            if u < 2:
+                b_sb[g, t] = b_first[:, u, :]
+            else:
+                b_sb[g, t] = ring.tile([P, NT], F32, name="b_sb", bufs=4)
+            nc.scalar.copy(b_sb[g, t][:], acc[:])
+
+        def matmul_x(u):
+            g, t = units[u]
+            b, s = groups[g]
+            acc = psum.tile([P, NT], F32, name="x_ps", tag=f"x{u % 4}")
+            for a in range(PASSES):
+                nc.tensor.matmul_mx(
+                    out=acc[:],
+                    lhsT=w1_codes[b][:, a, t * P : (t + 1) * P].bitcast(FP8X4),
+                    lhsT_scale=w1_scales[b][:, a, t * P : (t + 1) * P],
+                    rhs=v_words[a, s][:].bitcast(FP8X4),
+                    rhs_scale=v_plane[a][:, s * NT : (s + 1) * NT],
+                    start=(a == 0),
+                    stop=(a == PASSES - 1),
+                )
+            x_ps[g, t] = acc
+
+        def horner_inner(i):
+            ch, t = steps[i]
+            g, c0, c1 = chunks[ch]
+            if g not in t_pair:
+                t_pair[g] = keep.tile([P, 2, NT], F32, name="t_pair", tag=f"scratch{g % 2}", align_bytes=64)
+            nc.vector.scalar_tensor_tensor(
+                t_pair[g][:, i % 2, c0:c1],
+                x_ps[g, t][:, c0:c1],
+                q_col[:, groups[g][0], t : t + 1],
+                b_sb[g, t][:, c0:c1],
+                MULT,
+                ADD,
+            )
+
+        def horner_outer(i):
+            ch, t = steps[i]
+            g, c0, c1 = chunks[ch]
+            y = ring.tile([P, c1 - c0], F32, name="y_sb", bufs=3)
+            nc.vector.tensor_tensor(y[:], t_pair[g][:, i % 2, c0:c1], x_ps[g, t][:, c0:c1], MULT)
+            if t == 0:
+                h_planes[ch] = ring.tile([P, PACK, c1 - c0], BF16, name="h_planes", bufs=3, align_bytes=64)
+            nc.scalar.activation(h_planes[ch][:, t, :], y[:], IDENT, bias=c_col[:, groups[g][0], t : t + 1])
+
+        def interleave(ch):
+            g, c0, c1 = chunks[ch]
+            tag = f"scratch{g % 2}" if g < last else f"tail{c0}"
+            h_il[ch] = keep.tile([P, c1 - c0, PACK], BF16, name="h_il", tag=tag, align_bytes=64)
+            for n0 in range(0, c1 - c0, 256):
+                ns = slice(n0, min(n0 + 256, c1 - c0))
+                src = h_planes[ch][:, :, ns]
+                dst = h_il[ch][:, ns, :]
+                if E_ENGINE[ch] == "g":
+                    nc.gpsimd.tensor_scalar(dst, src.rearrange("p t n -> p n t"), 1.0, 0.0, MULT, ADD)
+                else:
+                    copy = nc.vector.tensor_copy if E_ENGINE[ch] == "v" else nc.scalar.copy
+                    copy(dst.rearrange("p (c i) t -> p c t i", i=4), src.rearrange("p t (c i) -> p c t i", i=4))
+
+        def quantize_h(ch):
+            g, c0, c1 = chunks[ch]
+            codes = keep.tile([P, c1 - c0], U32, name=f"hq{ch}", align_bytes=64)
+            scales = keep.tile([P, c1 - c0], U8, name=f"hs{ch}", align_bytes=64)
+            nc.vector.quantize_mx(
+                out=codes[:].bitcast(FP8X4), scales=scales[:], in_=h_il[ch][:].rearrange("p n t -> p (n t)")
+            )
+            h_q[ch] = (codes, scales)
+
+        def stage2(ch):
+            g, c0, c1 = chunks[ch]
+            s = groups[g][1]
+            first = groups.index((0, s))
+            operands = [(h_q[first][0][:, c0:c1], h_q[first][1][:, c0:c1]), (h_q[ch][0][:], h_q[ch][1][:])]
+            accs = [psum.tile([P, c1 - c0], F32, name="o_ps", tag=f"o{n}") for n in range(N // P)]
+            for b, (codes, scales) in enumerate(operands):
+                for n in range(N // P):
+                    nc.tensor.matmul_mx(
+                        out=accs[n][:],
+                        lhsT=w3c[:, b, n * P : (n + 1) * P].bitcast(FP8X4),
+                        lhsT_scale=w3s_box[0][:, b, n * P : (n + 1) * P],
+                        rhs=codes.bitcast(FP8X4),
+                        rhs_scale=scales,
+                        start=(b == 0),
+                        stop=(b == BLOCKS - 1),
+                    )
+            for n in range(N // P):
+                res = ring.tile([P, c1 - c0], F32, name="res", bufs=6)
+                dst = out[n * P : (n + 1) * P, s * NT + c0 : s * NT + c1]
+                if ch == len(chunks) - 1 and n == 1:
+                    nc.vector.tensor_copy(res[:], accs[n][:])
+                    nc.sync.dma_start(dst, res[:])
+                elif ch == len(chunks) - 1:
+                    nc.scalar.copy(res[:], accs[n][:])
+                    nc.scalar.dma_start(dst, res[:])
+                else:
+                    nc.scalar.copy(res[:], accs[n][:])
+                    nc.sync.dma_start(dst, res[:])
+
+        def finish(ch):
+            quantize_h(ch)
+            if groups[chunks[ch][0]][0] == BLOCKS - 1:
+                stage2(ch)
+
+        for u in range(2):
+            matmul_b(u)
+            matmul_x(u)
+        horner_inner(0)
+        for i, (ch, t) in enumerate(steps):
+            if i < 6:
+                for k in CAST_AT[i]:
+                    cast_piece(k)
+            if i == 3:
+                load_w3s()
+            if i == 5:
+                nc.vector.quantize_mx(
+                    out=w1_codes[1][:].rearrange("p a c -> p (a c)").bitcast(FP8X4),
+                    scales=w1_scales[1][:].rearrange("p a c -> p (a c)"),
+                    in_=w1_bf[1][:].rearrange("p a c -> p (a c)"),
+                )
+            if i + 2 < len(units):
+                matmul_b(i + 2)
+                matmul_x(i + 2)
+            if t == 2 and ch > 0:
+                finish(ch - 1)
+            if i + 1 < len(steps):
+                horner_inner(i + 1)
+            horner_outer(i)
+            if t == PACK - 1:
+                interleave(ch)
+        finish(len(chunks) - 1)

@@ -24,9 +24,9 @@ NT = 512
 PASSES = K // KP
 BLOCKS = H // KP
 HALVES = S // NT
-E_ENGINE = ("v", "v", "s", "v", "v")
-CAST_ENGINE = "s"
-CAST_AT = ((0,), (1,), (2, 3), (4,), (5, 6), (7,))
+E_ENGINE = ("s", "s", "s", "v", "v")
+CAST_ENGINE = "v"
+CAST_AT = ((), (0,), (1,), (2,), (3,), ())
 LAST_CHUNKS = ((0, 256), (256, 512))
 
 
@@ -37,18 +37,19 @@ def tile_list_seawater_horner_surrogate_kernel(
     with ExitStack() as ctx:
         keep = ctx.enter_context(tc.tile_pool(name="keep", bufs=1))
         ring = ctx.enter_context(tc.tile_pool(name="ring", bufs=2))
+        early = ctx.enter_context(tc.tile_pool(name="early", bufs=1))
         psum = ctx.enter_context(tc.psum_pool(name="psum", bufs=1))
 
         offsets = keep.tile([P, S // 16], U16, name="offsets")
         nc.sync.dma_start(offsets[:], offs)
 
-        ts_win = keep.tile([P, T], U8, name="ts_win", align_bytes=64)
+        ts_win = early.tile([P, T], U8, name="ts_win", align_bytes=64, offset=3584)
         nc.gpsimd.memset(ts_win[:].bitcast(I32), 0)
         for a in range(PASSES):
-            nc.sync.dma_start(ts_win[4 * a : P : 8, :].bitcast(I32), tab_scales[a].bitcast(I32))
+            nc.scalar.dma_start(ts_win[4 * a : P : 8, :].bitcast(I32), tab_scales[a].bitcast(I32))
 
         w2s_raw = keep.tile([P, PASSES, H], U8, name="w2s_raw", align_bytes=64)
-        nc.vector.memset(w2s_raw[:].rearrange("p a c -> p (a c)").bitcast(I32), 0)
+        nc.gpsimd.memset(w2s_raw[:].rearrange("p a c -> p (a c)").bitcast(I32), 0)
         for d in range(4):
             nc.gpsimd.dma_start(
                 w2s_raw[32 * d : 32 * d + 4, :, :].bitcast(I32),
@@ -56,6 +57,8 @@ def tile_list_seawater_horner_surrogate_kernel(
             )
         q_col = keep.tile([P, BLOCKS, PACK], F32, name="q_col")
         c_col = keep.tile([P, BLOCKS, PACK], F32, name="c_col")
+        nc.gpsimd.dma_start(q_col[:], quad.rearrange("(b p t) -> p b t", p=P, t=PACK))
+        nc.gpsimd.dma_start(c_col[:], cons.rearrange("(b p t) -> p b t", p=P, t=PACK))
 
         v_plane = []
         for a in range(PASSES):
@@ -65,11 +68,6 @@ def tile_list_seawater_horner_surrogate_kernel(
 
         w2_raw = keep.tile([P, PASSES, H // 2], I32, name="w2_raw", align_bytes=64)
         nc.sync.dma_start(w2_raw[:], w2_words.rearrange("a p c -> p a c").bitcast(I32))
-        tab_win = []
-        for a in range(PASSES):
-            win = keep.tile([P, T], I32, name="tab_win", tag=f"big{a}", align_bytes=64)
-            nc.sync.dma_start(win[:], tab_words[a].rearrange("p t i -> p (t i)").bitcast(I32))
-            tab_win.append(win)
 
         def load_w1(a, b):
             raw = keep.tile([P, PACK, KP], F32, name="w1_raw", tag=f"big{2 * (1 - b) + a}", align_bytes=64)
@@ -80,42 +78,50 @@ def tile_list_seawater_horner_surrogate_kernel(
             return raw
 
         w1_raw = {(a, 0): load_w1(a, 0) for a in range(PASSES)}
-        nc.scalar.dma_start(q_col[:], quad.rearrange("(b p t) -> p b t", p=P, t=PACK))
-        nc.scalar.dma_start(c_col[:], cons.rearrange("(b p t) -> p b t", p=P, t=PACK))
+        tab_win = []
+        for a in range(PASSES):
+            win = keep.tile([P, T], I32, name="tab_win", tag=f"big{a}", align_bytes=64)
+            nc.sync.dma_start(win[:], tab_words[a].rearrange("p t i -> p (t i)").bitcast(I32))
+            tab_win.append(win)
 
         ts_got = keep.tile([P, S], U8, name="ts_got", align_bytes=64)
         nc.vector.tensor_copy(ts_got[:], ts_win[:].indirect(offsets[:]))
         for a in range(PASSES):
             for r in range(4):
-                eng = nc.scalar if r % 2 == 0 else nc.gpsimd
+                eng = nc.gpsimd if a == 1 and r >= 1 else nc.sync
                 eng.dma_start(
                     v_plane[a][r:P:32, :].bitcast(I32), ts_got[8 * r + 4 * a : P : 32, :].bitcast(I32)
                 )
 
-        w2p, w2sp = [], []
+        w2p_all = early.tile([P, BLOCKS * PASSES * 2 * KP], U8, name="w2p_all", align_bytes=64, offset=0)
+        w2p = [
+            w2p_all[:, b * PASSES * 2 * KP : (b + 1) * PASSES * 2 * KP].rearrange("p (a t c) -> p a t c", a=PASSES, t=PACK)
+            for b in range(BLOCKS)
+        ]
+        w2sp = []
 
         def permute_w2(b):
-            words = keep.tile([P, PASSES, PACK, 2 * P], U8, name=f"w2p{b}", align_bytes=64)
             src = w2_raw[:].bitcast(U16)[:, :, b * KP : (b + 1) * KP]
-            nc.vector.tensor_copy(words[:].bitcast(U16), src.rearrange("p a (m t) -> p a t m", t=PACK))
+            nc.vector.tensor_copy(w2p[b].bitcast(U16), src.rearrange("p a (m t) -> p a t m", t=PACK))
             scales = keep.tile([P, PASSES, PACK, P], U8, name=f"w2sp{b}", align_bytes=64)
             ssrc = w2s_raw[:, :, b * KP : (b + 1) * KP]
             nc.vector.tensor_copy(scales[:], ssrc.rearrange("p a (m t) -> p a t m", t=PACK))
-            w2p.append(words)
             w2sp.append(scales)
 
-        permute_w2(0)
-
+        v_all = early.tile([P, PASSES * S], I32, name="v_all", align_bytes=64, offset=5120)
         v_words = {}
-        for a in range(PASSES):
-            for s in range(HALVES):
-                got = keep.tile([P, NT], I32, name=f"v_words{a}{s}", align_bytes=64)
-                lists = offsets[:, s * (NT // 16) : (s + 1) * (NT // 16)]
-                nc.vector.tensor_copy(got[:].bitcast(U32), tab_win[a][:].bitcast(U32).indirect(lists))
-                v_words[a, s] = got
+
+        def gather(a, s):
+            got = v_all[:, a * S + s * NT : a * S + (s + 1) * NT]
+            lists = offsets[:, s * (NT // 16) : (s + 1) * (NT // 16)]
+            nc.vector.tensor_copy(got.bitcast(U32), tab_win[a][:].bitcast(U32).indirect(lists))
+            v_words[a, s] = got
 
         w1_codes = [keep.tile([P, PASSES, KP], U32, name=f"w1c{b}", align_bytes=64) for b in range(BLOCKS)]
-        w1_scales = [keep.tile([P, PASSES, KP], U8, name=f"w1s{b}", align_bytes=64) for b in range(BLOCKS)]
+        w1_scales = [
+            early.tile([P, PASSES, KP], U8, name="w1s0", align_bytes=64, offset=4096),
+            keep.tile([P, PASSES, KP], U8, name="w1s1", align_bytes=64),
+        ]
         w1_bf = [keep.tile([P, PASSES, PACK * KP], BF16, name=f"w1b{b}", align_bytes=64) for b in range(BLOCKS)]
 
         def cast_views(a, b):
@@ -131,29 +137,34 @@ def tile_list_seawater_horner_surrogate_kernel(
             )
 
         for a in range(PASSES):
-            w1_raw[a, 1] = load_w1(a, 1)
+            nc.scalar.copy(*cast_views(a, 0))
+        permute_w2(0)
         permute_w2(1)
-        nc.scalar.copy(*cast_views(0, 0))
-        nc.vector.tensor_copy(*cast_views(1, 0))
-        for c0, c1 in ((0, P), (P, 2 * P), (2 * P, KP)):
-            for a in range(PASSES):
-                quantize_w1(0, a, c0, c1)
-        b_first = keep.tile([P, 2, NT], F32, name="b_first", tag="big2", align_bytes=64)
+        quantize_w1(0, 0, 0, KP)
+        gather(0, 0)
+        quantize_w1(0, 1, 0, KP)
+        gather(1, 0)
+        gather(0, 1)
+        gather(1, 1)
+        for a in range(PASSES):
+            w1_raw[a, 1] = load_w1(a, 1)
 
         def cast_piece(k):
-            a, h = divmod(k, 4)
+            a, h = divmod(k, 2)
             dst, src = cast_views(a, 1)
-            ms = slice(h * 32, (h + 1) * 32)
+            ms = slice(h * 64, (h + 1) * 64)
             if CAST_ENGINE == "g":
                 nc.gpsimd.tensor_scalar(dst[:, ms], src[:, ms], 1.0, 0.0, MULT, ADD)
+            elif CAST_ENGINE == "v":
+                nc.vector.tensor_copy(dst[:, ms], src[:, ms])
             else:
                 nc.scalar.copy(dst[:, ms], src[:, ms])
 
-        w3c = keep.tile([P, PASSES, N], I32, name="w3c", tag="big3", align_bytes=64)
-        nc.sync.dma_start(w3c[:], w3_words.rearrange("a p c i -> p a (c i)").bitcast(I32))
         w3s_box = []
 
         def load_w3s():
+            w3c = keep.tile([P, PASSES, N], I32, name="w3c", tag="big1", align_bytes=64)
+            nc.sync.dma_start(w3c[:], w3_words.rearrange("a p c i -> p a (c i)").bitcast(I32))
             w3s = keep.tile([P, PASSES, N], U8, name="w3s", tag="big0", align_bytes=64)
             nc.gpsimd.memset(w3s[:].rearrange("p a c -> p (a c)").bitcast(I32), 0)
             for d in range(4):
@@ -161,7 +172,7 @@ def tile_list_seawater_horner_surrogate_kernel(
                     w3s[32 * d : 32 * d + 4, :, :].bitcast(I32),
                     w3_scales[:, 4 * d : 4 * d + 4, :].rearrange("a r c -> r a c").bitcast(I32),
                 )
-            w3s_box.append(w3s)
+            w3s_box.extend([w3s, w3c])
 
         groups = [(b, s) for b in range(BLOCKS) for s in range(HALVES)]
         last = len(groups) - 1
@@ -179,15 +190,12 @@ def tile_list_seawater_horner_surrogate_kernel(
                     out=acc[:],
                     lhsT=w2p[b][:, a, t, :].bitcast(FP4X4),
                     lhsT_scale=w2sp[b][:, a, t, :],
-                    rhs=v_words[a, s][:].bitcast(FP8X4),
+                    rhs=v_words[a, s].bitcast(FP8X4),
                     rhs_scale=v_plane[a][:, s * NT : (s + 1) * NT],
                     start=(a == 0),
                     stop=(a == PASSES - 1),
                 )
-            if u < 2:
-                b_sb[g, t] = b_first[:, u, :]
-            else:
-                b_sb[g, t] = ring.tile([P, NT], F32, name="b_sb", bufs=4)
+            b_sb[g, t] = ring.tile([P, NT], F32, name="b_sb", bufs=5)
             nc.scalar.copy(b_sb[g, t][:], acc[:])
 
         def matmul_x(u):
@@ -199,7 +207,7 @@ def tile_list_seawater_horner_surrogate_kernel(
                     out=acc[:],
                     lhsT=w1_codes[b][:, a, t * P : (t + 1) * P].bitcast(FP8X4),
                     lhsT_scale=w1_scales[b][:, a, t * P : (t + 1) * P],
-                    rhs=v_words[a, s][:].bitcast(FP8X4),
+                    rhs=v_words[a, s].bitcast(FP8X4),
                     rhs_scale=v_plane[a][:, s * NT : (s + 1) * NT],
                     start=(a == 0),
                     stop=(a == PASSES - 1),
@@ -223,7 +231,7 @@ def tile_list_seawater_horner_surrogate_kernel(
         def horner_outer(i):
             ch, t = steps[i]
             g, c0, c1 = chunks[ch]
-            y = ring.tile([P, c1 - c0], F32, name="y_sb", bufs=3)
+            y = ring.tile([P, c1 - c0], F32, name="y_sb", bufs=4)
             nc.vector.tensor_tensor(y[:], t_pair[g][:, i % 2, c0:c1], x_ps[g, t][:, c0:c1], MULT)
             if t == 0:
                 h_planes[ch] = ring.tile([P, PACK, c1 - c0], BF16, name="h_planes", bufs=3, align_bytes=64)
@@ -233,8 +241,9 @@ def tile_list_seawater_horner_surrogate_kernel(
             g, c0, c1 = chunks[ch]
             tag = f"scratch{g % 2}" if g < last else f"tail{c0}"
             h_il[ch] = keep.tile([P, c1 - c0, PACK], BF16, name="h_il", tag=tag, align_bytes=64)
-            for n0 in range(0, c1 - c0, 256):
-                ns = slice(n0, min(n0 + 256, c1 - c0))
+            width = 256 if E_ENGINE[ch] == "g" else c1 - c0
+            for n0 in range(0, c1 - c0, width):
+                ns = slice(n0, n0 + width)
                 src = h_planes[ch][:, :, ns]
                 dst = h_il[ch][:, ns, :]
                 if E_ENGINE[ch] == "g":
@@ -262,7 +271,7 @@ def tile_list_seawater_horner_surrogate_kernel(
                 for n in range(N // P):
                     nc.tensor.matmul_mx(
                         out=accs[n][:],
-                        lhsT=w3c[:, b, n * P : (n + 1) * P].bitcast(FP8X4),
+                        lhsT=w3s_box[1][:, b, n * P : (n + 1) * P].bitcast(FP8X4),
                         lhsT_scale=w3s_box[0][:, b, n * P : (n + 1) * P],
                         rhs=codes.bitcast(FP8X4),
                         rhs_scale=scales,
@@ -295,7 +304,7 @@ def tile_list_seawater_horner_surrogate_kernel(
             if i < 6:
                 for k in CAST_AT[i]:
                     cast_piece(k)
-            if i == 3:
+            if i == 5:
                 load_w3s()
             if i == 5:
                 nc.vector.quantize_mx(

@@ -24,10 +24,18 @@ NT = 512
 PASSES = K // KP
 BLOCKS = H // KP
 HALVES = S // NT
-E_ENGINE = ("s", "s", "s", "v", "v")
-CAST_ENGINE = "v"
-CAST_AT = ((), (0,), (1,), (2,), (3,), ())
 LAST_CHUNKS = ((0, 256), (256, 512))
+BIAS_ENGINE = ("g", "g", "g", "s", "s")
+WEAVE_ENGINE = ("g", "g", "s", "s", "v")
+WEAVE_AT = {4: ((0, 0, 4),), 5: ((0, 1, 4),), 7: ((0, 2, 4),), 9: ((0, 3, 4),), 11: ((1, 0, 4), (2, 0, 2)), 12: ((1, 1, 4), (2, 1, 2)), 13: ((1, 2, 4),), 14: ((1, 3, 4),), 15: ((3, 0, 1),), 19: ((4, 0, 1),)}
+QUANT_AT = {11: (0,), 14: (2,), 16: (1,), 18: (3,), 20: (4,)}
+CAST_ENGINE = ("s", "s", "s", "s")
+CAST_AT = {0: (0,), 1: (1,), 2: (2,), 3: (3,)}
+W1Q_AT = {2: (0,), 4: (1,)}
+FIRST = 32
+PINS = [0, 2]
+B_LEAD = 4
+X_LEAD = 3
 
 
 def tile_list_seawater_horner_surrogate_kernel(
@@ -43,185 +51,167 @@ def tile_list_seawater_horner_surrogate_kernel(
         offsets = keep.tile([P, S // 16], U16, name="offsets")
         nc.sync.dma_start(offsets[:], offs)
 
-        ts_win = early.tile([P, T], U8, name="ts_win", align_bytes=64, offset=3584)
-        nc.gpsimd.memset(ts_win[:].bitcast(I32), 0)
-        for a in range(PASSES):
-            nc.scalar.dma_start(ts_win[4 * a : P : 8, :].bitcast(I32), tab_scales[a].bitcast(I32))
+        w1_raw = {}
 
-        w2s_raw = keep.tile([P, PASSES, H], U8, name="w2s_raw", align_bytes=64)
-        nc.gpsimd.memset(w2s_raw[:].rearrange("p a c -> p (a c)").bitcast(I32), 0)
-        for d in range(4):
-            nc.gpsimd.dma_start(
-                w2s_raw[32 * d : 32 * d + 4, :, :].bitcast(I32),
-                w2_scales[:, 4 * d : 4 * d + 4, :].rearrange("a r c -> r a c").bitcast(I32),
-            )
+        def load_w1(a, b, m0, m1, room):
+            raw = keep.tile([P, PACK, PACK * (m1 - m0)], F32, name="w1_raw", tag=room, align_bytes=64)
+            cols = slice(b * KP + PACK * m0, b * KP + PACK * m1)
+            nc.sync.dma_start(raw[:], w1[a * KP : (a + 1) * KP, cols].rearrange("(p j) c -> p j c", j=PACK))
+            w1_raw[a, b, m0] = raw
+
+        load_w1(0, 0, 0, FIRST, "room3")
+
+        ts_win = keep.tile([P, T], U8, name="ts_win", align_bytes=64)
+        nc.vector.memset(ts_win[:].bitcast(I32), 0)
+        for e in range(2):
+            nc.scalar.dma_start(ts_win[e:P:16, :].bitcast(I32), tab_scales[0, e:16:2, :].bitcast(I32))
+        nc.scalar.dma_start(ts_win[4:P:8, :].bitcast(I32), tab_scales[1].bitcast(I32))
+
+        def load_scale_rows(name, src, width):
+            rows = keep.tile([P, PASSES, width], U8, name=name, align_bytes=64)
+            nc.gpsimd.memset(rows[:].rearrange("p a c -> p (a c)").bitcast(I32), 0)
+            for d in range(4):
+                nc.gpsimd.dma_start(
+                    rows[32 * d : 32 * d + 4, :, :].bitcast(I32),
+                    src[:, 4 * d : 4 * d + 4, :].rearrange("a r c -> r a c").bitcast(I32),
+                )
+            return rows
+
+        w2s_raw = load_scale_rows("w2s_raw", w2_scales, H)
         q_col = keep.tile([P, BLOCKS, PACK], F32, name="q_col")
         c_col = keep.tile([P, BLOCKS, PACK], F32, name="c_col")
         nc.gpsimd.dma_start(q_col[:], quad.rearrange("(b p t) -> p b t", p=P, t=PACK))
         nc.gpsimd.dma_start(c_col[:], cons.rearrange("(b p t) -> p b t", p=P, t=PACK))
-
-        v_plane = []
-        for a in range(PASSES):
-            plane = keep.tile([P, S], U8, name=f"v_plane{a}", align_bytes=64)
-            nc.vector.memset(plane[:].bitcast(I32), 0)
-            v_plane.append(plane)
+        w3s = load_scale_rows("w3s", w3_scales, N)
 
         w2_raw = keep.tile([P, PASSES, H // 2], I32, name="w2_raw", align_bytes=64)
         nc.sync.dma_start(w2_raw[:], w2_words.rearrange("a p c -> p a c").bitcast(I32))
 
-        def load_w1(a, b):
-            raw = keep.tile([P, PACK, KP], F32, name="w1_raw", tag=f"big{2 * (1 - b) + a}", align_bytes=64)
-            nc.sync.dma_start(
-                raw[:],
-                w1[a * KP : (a + 1) * KP, b * KP : (b + 1) * KP].rearrange("(p j) c -> p j c", j=PACK),
-            )
-            return raw
-
-        w1_raw = {(a, 0): load_w1(a, 0) for a in range(PASSES)}
-        tab_win = []
-        for a in range(PASSES):
-            win = keep.tile([P, T], I32, name="tab_win", tag=f"big{a}", align_bytes=64)
+        def load_table(a):
+            win = keep.tile([P, T], I32, name="tab_win", tag=f"room{a}", align_bytes=64)
             nc.sync.dma_start(win[:], tab_words[a].rearrange("p t i -> p (t i)").bitcast(I32))
-            tab_win.append(win)
+            return win
 
+        tab_win = [load_table(0)]
+        load_w1(0, 0, FIRST, P, "room4")
+        load_w1(1, 0, 0, P, "room2")
+        tab_win.append(load_table(1))
+
+        w1_codes = [keep.tile([P, PASSES, KP], U32, name=f"w1c{b}", align_bytes=64) for b in range(BLOCKS)]
+        w1_scales = [keep.tile([P, PASSES, KP], U8, name=f"w1s{b}", align_bytes=64) for b in range(BLOCKS)]
+        w1_bf = {}
+        for a in range(PASSES):
+            w1_bf[a, 0] = keep.tile([P, PACK * KP], BF16, name=f"w1b{a}0", align_bytes=64)
+            w1_bf[a, 1] = early.tile([P, PACK * KP], BF16, name=f"w1b{a}1", align_bytes=64, offset=a * 4096)
+
+        def cast(a, b, m0, m1, engine, base=0):
+            dst = w1_bf[a, b][:].rearrange("p (t m j) -> p m j t", t=PACK, j=PACK)[:, m0:m1]
+            src = w1_raw[a, b, base][:].rearrange("p j (m t) -> p m j t", t=PACK)[:, m0 - base : m1 - base]
+            if engine == "v":
+                nc.vector.tensor_copy(dst, src)
+            else:
+                nc.scalar.copy(dst, src)
+
+        def quantize_w1(b, a):
+            nc.vector.quantize_mx(
+                out=w1_codes[b][:, a, :].bitcast(FP8X4), scales=w1_scales[b][:, a, :], in_=w1_bf[a, b][:]
+            )
+
+        cast(0, 0, 0, FIRST, "s")
         ts_got = keep.tile([P, S], U8, name="ts_got", align_bytes=64)
         nc.vector.tensor_copy(ts_got[:], ts_win[:].indirect(offsets[:]))
-        for a in range(PASSES):
-            for r in range(4):
-                eng = nc.gpsimd if a == 1 and r >= 1 else nc.sync
-                eng.dma_start(
-                    v_plane[a][r:P:32, :].bitcast(I32), ts_got[8 * r + 4 * a : P : 32, :].bitcast(I32)
-                )
 
-        w2p_all = early.tile([P, BLOCKS * PASSES * 2 * KP], U8, name="w2p_all", align_bytes=64, offset=0)
-        w2p = [
-            w2p_all[:, b * PASSES * 2 * KP : (b + 1) * PASSES * 2 * KP].rearrange("p (a t c) -> p a t c", a=PASSES, t=PACK)
-            for b in range(BLOCKS)
-        ]
-        w2sp = []
+        v_plane = [keep.tile([P, S], U8, name=f"v_plane{a}", align_bytes=64) for a in range(PASSES)]
+        nc.vector.tensor_copy(v_plane[0][:].bitcast(I32), ts_got[:].bitcast(I32))
+        nc.vector.memset(v_plane[1][:].bitcast(I32), 0)
+        for r in range(2, 4):
+            nc.scalar.dma_start(v_plane[0][r:P:32, :].bitcast(I32), ts_got[14 + r : P : 32, :].bitcast(I32))
+        for r in range(4):
+            nc.scalar.dma_start(v_plane[1][r:P:32, :].bitcast(I32), ts_got[8 * r + 4 : P : 32, :].bitcast(I32))
+
+        w2p, w2sp = [], []
 
         def permute_w2(b):
+            words = keep.tile([P, PASSES, PACK, 2 * P], U8, name=f"w2p{b}", align_bytes=64)
             src = w2_raw[:].bitcast(U16)[:, :, b * KP : (b + 1) * KP]
-            nc.vector.tensor_copy(w2p[b].bitcast(U16), src.rearrange("p a (m t) -> p a t m", t=PACK))
+            nc.vector.tensor_copy(words[:].bitcast(U16), src.rearrange("p a (m t) -> p a t m", t=PACK))
             scales = keep.tile([P, PASSES, PACK, P], U8, name=f"w2sp{b}", align_bytes=64)
             ssrc = w2s_raw[:, :, b * KP : (b + 1) * KP]
             nc.vector.tensor_copy(scales[:], ssrc.rearrange("p a (m t) -> p a t m", t=PACK))
+            w2p.append(words)
             w2sp.append(scales)
 
-        v_all = early.tile([P, PASSES * S], I32, name="v_all", align_bytes=64, offset=5120)
         v_words = {}
 
         def gather(a, s):
-            got = v_all[:, a * S + s * NT : a * S + (s + 1) * NT]
+            got = keep.tile([P, NT], I32, name=f"v{a}{s}", align_bytes=64)
             lists = offsets[:, s * (NT // 16) : (s + 1) * (NT // 16)]
-            nc.vector.tensor_copy(got.bitcast(U32), tab_win[a][:].bitcast(U32).indirect(lists))
+            nc.vector.tensor_copy(got[:].bitcast(U32), tab_win[a][:].bitcast(U32).indirect(lists))
             v_words[a, s] = got
 
-        w1_codes = [keep.tile([P, PASSES, KP], U32, name=f"w1c{b}", align_bytes=64) for b in range(BLOCKS)]
-        w1_scales = [
-            early.tile([P, PASSES, KP], U8, name="w1s0", align_bytes=64, offset=4096),
-            keep.tile([P, PASSES, KP], U8, name="w1s1", align_bytes=64),
-        ]
-        w1_bf = [keep.tile([P, PASSES, PACK * KP], BF16, name=f"w1b{b}", align_bytes=64) for b in range(BLOCKS)]
-
-        def cast_views(a, b):
-            dst = w1_bf[b][:, a, :].rearrange("p (t m j) -> p m j t", t=PACK, j=PACK)
-            src = w1_raw[a, b][:].rearrange("p j (m t) -> p m j t", t=PACK)
-            return dst, src
-
-        def quantize_w1(b, a, c0, c1):
-            nc.vector.quantize_mx(
-                out=w1_codes[b][:, a, c0:c1].bitcast(FP8X4),
-                scales=w1_scales[b][:, a, c0:c1],
-                in_=w1_bf[b][:, a, PACK * c0 : PACK * c1],
-            )
-
-        for a in range(PASSES):
-            nc.scalar.copy(*cast_views(a, 0))
         permute_w2(0)
-        permute_w2(1)
-        quantize_w1(0, 0, 0, KP)
         gather(0, 0)
-        quantize_w1(0, 1, 0, KP)
-        gather(1, 0)
         gather(0, 1)
+        load_w1(0, 1, 0, P, "room0")
+        permute_w2(1)
+        cast(0, 0, FIRST, P, "s", FIRST)
+        quantize_w1(0, 0)
+        cast(1, 0, 0, P, "s")
+        load_w1(1, 1, 0, P, "room2")
+        gather(1, 0)
+        quantize_w1(0, 1)
         gather(1, 1)
-        for a in range(PASSES):
-            w1_raw[a, 1] = load_w1(a, 1)
-
-        def cast_piece(k):
-            a, h = divmod(k, 2)
-            dst, src = cast_views(a, 1)
-            ms = slice(h * 64, (h + 1) * 64)
-            if CAST_ENGINE == "g":
-                nc.gpsimd.tensor_scalar(dst[:, ms], src[:, ms], 1.0, 0.0, MULT, ADD)
-            elif CAST_ENGINE == "v":
-                nc.vector.tensor_copy(dst[:, ms], src[:, ms])
-            else:
-                nc.scalar.copy(dst[:, ms], src[:, ms])
-
-        w3s_box = []
-
-        def load_w3s():
-            w3c = keep.tile([P, PASSES, N], I32, name="w3c", tag="big1", align_bytes=64)
-            nc.sync.dma_start(w3c[:], w3_words.rearrange("a p c i -> p a (c i)").bitcast(I32))
-            w3s = keep.tile([P, PASSES, N], U8, name="w3s", tag="big0", align_bytes=64)
-            nc.gpsimd.memset(w3s[:].rearrange("p a c -> p (a c)").bitcast(I32), 0)
-            for d in range(4):
-                nc.sync.dma_start(
-                    w3s[32 * d : 32 * d + 4, :, :].bitcast(I32),
-                    w3_scales[:, 4 * d : 4 * d + 4, :].rearrange("a r c -> r a c").bitcast(I32),
-                )
-            w3s_box.extend([w3s, w3c])
+        w3c = keep.tile([P, PASSES, N], I32, name="w3c", tag="room1", align_bytes=64)
+        nc.sync.dma_start(w3c[:], w3_words.rearrange("a p c i -> p a (c i)").bitcast(I32))
 
         groups = [(b, s) for b in range(BLOCKS) for s in range(HALVES)]
         last = len(groups) - 1
         units = [(g, t) for g in range(len(groups)) for t in range(PACK)]
         chunks = [(g, 0, NT) for g in range(last)] + [(last, c0, c1) for c0, c1 in LAST_CHUNKS]
         steps = [(ch, t) for ch in range(len(chunks)) for t in range(PACK)]
-        b_sb, x_ps, t_pair, h_planes, h_il, h_q = {}, {}, {}, {}, {}, {}
+        b_ps = {}
+        b_sb, x_ps, inner, y_sb, h_planes, h_il, h_q = {}, {}, {}, {}, {}, {}, {}
 
-        def matmul_b(u):
+        def first_stage(acc, codes, scales, a, s, c0, c1):
+            nc.tensor.matmul_mx(
+                out=acc[:],
+                lhsT=codes,
+                lhsT_scale=scales,
+                rhs=v_words[a, s][:, c0:c1].bitcast(FP8X4),
+                rhs_scale=v_plane[a][:, s * NT + c0 : s * NT + c1],
+                start=(a == 0),
+                stop=(a == PASSES - 1),
+            )
+
+        def matmul_b(u, a):
             g, t = units[u]
             b, s = groups[g]
-            acc = psum.tile([P, NT], F32, name="b_ps", tag=f"b{u % 2}")
-            for a in range(PASSES):
-                nc.tensor.matmul_mx(
-                    out=acc[:],
-                    lhsT=w2p[b][:, a, t, :].bitcast(FP4X4),
-                    lhsT_scale=w2sp[b][:, a, t, :],
-                    rhs=v_words[a, s].bitcast(FP8X4),
-                    rhs_scale=v_plane[a][:, s * NT : (s + 1) * NT],
-                    start=(a == 0),
-                    stop=(a == PASSES - 1),
-                )
-            b_sb[g, t] = ring.tile([P, NT], F32, name="b_sb", bufs=5)
-            nc.scalar.copy(b_sb[g, t][:], acc[:])
+            if a == 0:
+                b_ps[u] = psum.tile([P, NT], F32, name="b_ps", tag=f"b{u % 4}")
+            first_stage(b_ps[u], w2p[b][:, a, t, :].bitcast(FP4X4), w2sp[b][:, a, t, :], a, s, 0, NT)
+            if a == PASSES - 1:
+                if u in PINS:
+                    b_sb[g, t] = early.tile([P, NT], F32, name=f"b_pin{u}", align_bytes=64, offset=PINS.index(u) * 4096)
+                else:
+                    b_sb[g, t] = ring.tile([P, NT], F32, name="b_sb", bufs=8)
+                nc.scalar.copy(b_sb[g, t][:], b_ps[u][:])
 
-        def matmul_x(u):
-            g, t = units[u]
+        def matmul_x(i, a):
+            ch, t = steps[i]
+            g, c0, c1 = chunks[ch]
             b, s = groups[g]
-            acc = psum.tile([P, NT], F32, name="x_ps", tag=f"x{u % 4}")
-            for a in range(PASSES):
-                nc.tensor.matmul_mx(
-                    out=acc[:],
-                    lhsT=w1_codes[b][:, a, t * P : (t + 1) * P].bitcast(FP8X4),
-                    lhsT_scale=w1_scales[b][:, a, t * P : (t + 1) * P],
-                    rhs=v_words[a, s].bitcast(FP8X4),
-                    rhs_scale=v_plane[a][:, s * NT : (s + 1) * NT],
-                    start=(a == 0),
-                    stop=(a == PASSES - 1),
-                )
-            x_ps[g, t] = acc
+            if a == 0:
+                x_ps[i] = psum.tile([P, c1 - c0], F32, name="x_ps", tag=f"x{i % 4}")
+            cols = slice(t * P, (t + 1) * P)
+            first_stage(x_ps[i], w1_codes[b][:, a, cols].bitcast(FP8X4), w1_scales[b][:, a, cols], a, s, c0, c1)
 
         def horner_inner(i):
             ch, t = steps[i]
             g, c0, c1 = chunks[ch]
-            if g not in t_pair:
-                t_pair[g] = keep.tile([P, 2, NT], F32, name="t_pair", tag=f"scratch{g % 2}", align_bytes=64)
+            inner[i] = ring.tile([P, c1 - c0], F32, name="inner", bufs=3)
             nc.vector.scalar_tensor_tensor(
-                t_pair[g][:, i % 2, c0:c1],
-                x_ps[g, t][:, c0:c1],
+                inner[i][:],
+                x_ps[i][:],
                 q_col[:, groups[g][0], t : t + 1],
                 b_sb[g, t][:, c0:c1],
                 MULT,
@@ -231,26 +221,42 @@ def tile_list_seawater_horner_surrogate_kernel(
         def horner_outer(i):
             ch, t = steps[i]
             g, c0, c1 = chunks[ch]
-            y = ring.tile([P, c1 - c0], F32, name="y_sb", bufs=4)
-            nc.vector.tensor_tensor(y[:], t_pair[g][:, i % 2, c0:c1], x_ps[g, t][:, c0:c1], MULT)
+            fused = BIAS_ENGINE[ch] == "f"
             if t == 0:
-                h_planes[ch] = ring.tile([P, PACK, c1 - c0], BF16, name="h_planes", bufs=3, align_bytes=64)
-            nc.scalar.activation(h_planes[ch][:, t, :], y[:], IDENT, bias=c_col[:, groups[g][0], t : t + 1])
-
-        def interleave(ch):
-            g, c0, c1 = chunks[ch]
-            tag = f"scratch{g % 2}" if g < last else f"tail{c0}"
-            h_il[ch] = keep.tile([P, c1 - c0, PACK], BF16, name="h_il", tag=tag, align_bytes=64)
-            width = 256 if E_ENGINE[ch] == "g" else c1 - c0
-            for n0 in range(0, c1 - c0, width):
-                ns = slice(n0, n0 + width)
-                src = h_planes[ch][:, :, ns]
-                dst = h_il[ch][:, ns, :]
-                if E_ENGINE[ch] == "g":
-                    nc.gpsimd.tensor_scalar(dst, src.rearrange("p t n -> p n t"), 1.0, 0.0, MULT, ADD)
+                h_il[ch] = keep.tile([P, c1 - c0, PACK], BF16, name=f"h_il{ch}", align_bytes=64)
+                if fused:
+                    y_sb[ch] = keep.tile([P, PACK, c1 - c0], F32, name=f"y_all{ch}")
                 else:
-                    copy = nc.vector.tensor_copy if E_ENGINE[ch] == "v" else nc.scalar.copy
-                    copy(dst.rearrange("p (c i) t -> p c t i", i=4), src.rearrange("p t (c i) -> p c t i", i=4))
+                    h_planes[ch] = keep.tile([P, PACK, c1 - c0], BF16, name=f"h_planes{ch}", align_bytes=64)
+            if fused:
+                y = y_sb[ch][:, t, :]
+            else:
+                y_one = ring.tile([P, c1 - c0], F32, name="y_one", bufs=6)
+                y = y_one[:]
+            nc.vector.tensor_tensor(y, inner[i][:], x_ps[i][:], MULT)
+            bias = c_col[:, groups[g][0], t : t + 1]
+            if BIAS_ENGINE[ch] == "s":
+                nc.scalar.activation(h_planes[ch][:, t, :], y, IDENT, bias=bias)
+            elif BIAS_ENGINE[ch] == "g":
+                nc.gpsimd.tensor_scalar(h_planes[ch][:, t, :], y, 1.0, bias, MULT, ADD)
+
+        def weave(ch, piece, pieces):
+            g, c0, c1 = chunks[ch]
+            width = (c1 - c0) // pieces
+            ns = slice(piece * width, (piece + 1) * width)
+            dst = h_il[ch][:, ns, :]
+            walk_dst = dst.rearrange("p (c i) t -> p c t i", i=4)
+            if BIAS_ENGINE[ch] == "f":
+                src = y_sb[ch][:, :, ns].rearrange("p t (c i) -> p c t i", i=4)
+                bias = c_col[:, groups[g][0], :].unsqueeze(1).unsqueeze(3).to_broadcast([P, width // 4, PACK, 4])
+                nc.vector.tensor_tensor(walk_dst, src, bias, ADD)
+                return
+            src = h_planes[ch][:, :, ns]
+            if WEAVE_ENGINE[ch] == "g":
+                nc.gpsimd.tensor_scalar(dst, src.rearrange("p t n -> p n t"), 1.0, 0.0, MULT, ADD)
+            else:
+                copy = nc.vector.tensor_copy if WEAVE_ENGINE[ch] == "v" else nc.scalar.copy
+                copy(walk_dst, src.rearrange("p t (c i) -> p c t i", i=4))
 
         def quantize_h(ch):
             g, c0, c1 = chunks[ch]
@@ -261,25 +267,25 @@ def tile_list_seawater_horner_surrogate_kernel(
             )
             h_q[ch] = (codes, scales)
 
-        def stage2(ch):
+        def second_stage(ch):
             g, c0, c1 = chunks[ch]
             s = groups[g][1]
             first = groups.index((0, s))
             operands = [(h_q[first][0][:, c0:c1], h_q[first][1][:, c0:c1]), (h_q[ch][0][:], h_q[ch][1][:])]
-            accs = [psum.tile([P, c1 - c0], F32, name="o_ps", tag=f"o{n}") for n in range(N // P)]
+            accs = [psum.tile([P, c1 - c0], F32, name="o_ps", tag=f"b{2 * (ch % 2) + n}") for n in range(N // P)]
             for b, (codes, scales) in enumerate(operands):
                 for n in range(N // P):
                     nc.tensor.matmul_mx(
                         out=accs[n][:],
-                        lhsT=w3s_box[1][:, b, n * P : (n + 1) * P].bitcast(FP8X4),
-                        lhsT_scale=w3s_box[0][:, b, n * P : (n + 1) * P],
+                        lhsT=w3c[:, b, n * P : (n + 1) * P].bitcast(FP8X4),
+                        lhsT_scale=w3s[:, b, n * P : (n + 1) * P],
                         rhs=codes.bitcast(FP8X4),
                         rhs_scale=scales,
                         start=(b == 0),
                         stop=(b == BLOCKS - 1),
                     )
             for n in range(N // P):
-                res = ring.tile([P, c1 - c0], F32, name="res", bufs=6)
+                res = keep.tile([P, c1 - c0], F32, name=f"res{ch}{n}")
                 dst = out[n * P : (n + 1) * P, s * NT + c0 : s * NT + c1]
                 if ch == len(chunks) - 1 and n == 1:
                     nc.vector.tensor_copy(res[:], accs[n][:])
@@ -294,32 +300,33 @@ def tile_list_seawater_horner_surrogate_kernel(
         def finish(ch):
             quantize_h(ch)
             if groups[chunks[ch][0]][0] == BLOCKS - 1:
-                stage2(ch)
+                second_stage(ch)
 
-        for u in range(2):
-            matmul_b(u)
-            matmul_x(u)
+        for u in range(B_LEAD):
+            matmul_b(u, 0)
+        for u in range(X_LEAD):
+            matmul_x(u, 0)
+        for u in range(B_LEAD):
+            matmul_b(u, 1)
+            if u < X_LEAD:
+                matmul_x(u, 1)
         horner_inner(0)
-        for i, (ch, t) in enumerate(steps):
-            if i < 6:
-                for k in CAST_AT[i]:
-                    cast_piece(k)
-            if i == 5:
-                load_w3s()
-            if i == 5:
-                nc.vector.quantize_mx(
-                    out=w1_codes[1][:].rearrange("p a c -> p (a c)").bitcast(FP8X4),
-                    scales=w1_scales[1][:].rearrange("p a c -> p (a c)"),
-                    in_=w1_bf[1][:].rearrange("p a c -> p (a c)"),
-                )
-            if i + 2 < len(units):
-                matmul_b(i + 2)
-                matmul_x(i + 2)
-            if t == 2 and ch > 0:
-                finish(ch - 1)
+        for i in range(len(steps) + 2):
+            for a in range(PASSES):
+                if i + X_LEAD < len(steps):
+                    matmul_x(i + X_LEAD, a)
+            for a in range(PASSES):
+                if i + B_LEAD < len(units):
+                    matmul_b(i + B_LEAD, a)
+            for k in CAST_AT.get(i, ()):
+                cast(k // 2, 1, (k % 2) * 64, (k % 2) * 64 + 64, CAST_ENGINE[k])
+            for a in W1Q_AT.get(i, ()):
+                quantize_w1(1, a)
             if i + 1 < len(steps):
                 horner_inner(i + 1)
-            horner_outer(i)
-            if t == PACK - 1:
-                interleave(ch)
-        finish(len(chunks) - 1)
+            for ch in QUANT_AT.get(i, ()):
+                finish(ch)
+            if i < len(steps):
+                horner_outer(i)
+            for ch, piece, pieces in WEAVE_AT.get(i, ()):
+                weave(ch, piece, pieces)

@@ -25,15 +25,16 @@ PASSES = K // KP
 BLOCKS = H // KP
 HALVES = S // NT
 LAST_CHUNKS = ((0, 256), (256, 512))
-BIAS_ENGINE = ("g", "g", "g", "s", "s")
-WEAVE_ENGINE = ("g", "g", "s", "s", "v")
-WEAVE_AT = {4: ((0, 0, 4),), 5: ((0, 1, 4),), 7: ((0, 2, 4),), 9: ((0, 3, 4),), 11: ((1, 0, 4), (2, 0, 2)), 12: ((1, 1, 4), (2, 1, 2)), 13: ((1, 2, 4),), 14: ((1, 3, 4),), 15: ((3, 0, 1),), 19: ((4, 0, 1),)}
-QUANT_AT = {11: (0,), 14: (2,), 16: (1,), 18: (3,), 20: (4,)}
+BIAS_ENGINE = ("g", "g", "g", "g", "s")
+WEAVE_ENGINE = ("g", "s", "s", "s", "v")
+WEAVE_AT = {4: ((0, 0, 4),), 5: ((0, 1, 4),), 6: ((0, 2, 4),), 7: ((0, 3, 4),), 8: ((1, 0, 2),), 9: ((1, 1, 2),), 11: ((2, 0, 2),), 12: ((2, 1, 2),), 15: ((3, 0, 1),), 19: ((4, 0, 1),)}
+QUANT_AT = {10: (0,), 11: (1,), 15: (2,), 18: (3,), 20: (4,)}
 CAST_ENGINE = ("s", "s", "s", "s")
 CAST_AT = {0: (0,), 1: (1,), 2: (2,), 3: (3,)}
 W1Q_AT = {2: (0,), 4: (1,)}
 FIRST = 32
 PINS = [0, 2]
+ROOM = 8192
 B_LEAD = 4
 X_LEAD = 3
 
@@ -46,6 +47,8 @@ def tile_list_seawater_horner_surrogate_kernel(
         keep = ctx.enter_context(tc.tile_pool(name="keep", bufs=1))
         ring = ctx.enter_context(tc.tile_pool(name="ring", bufs=2))
         early = ctx.enter_context(tc.tile_pool(name="early", bufs=1))
+        head = ctx.enter_context(tc.tile_pool(name="head", bufs=1))
+        pin = ctx.enter_context(tc.tile_pool(name="pin", bufs=1))
         psum = ctx.enter_context(tc.psum_pool(name="psum", bufs=1))
 
         offsets = keep.tile([P, S // 16], U16, name="offsets")
@@ -54,14 +57,14 @@ def tile_list_seawater_horner_surrogate_kernel(
         w1_raw = {}
 
         def load_w1(a, b, m0, m1, room):
-            raw = keep.tile([P, PACK, PACK * (m1 - m0)], F32, name="w1_raw", tag=room, align_bytes=64)
+            raw = head.tile([P, PACK, PACK * (m1 - m0)], F32, name=f"w1_raw{a}{b}{m0}", align_bytes=64, offset=room)
             cols = slice(b * KP + PACK * m0, b * KP + PACK * m1)
             nc.sync.dma_start(raw[:], w1[a * KP : (a + 1) * KP, cols].rearrange("(p j) c -> p j c", j=PACK))
             w1_raw[a, b, m0] = raw
 
-        load_w1(0, 0, 0, FIRST, "room3")
+        load_w1(0, 0, 0, FIRST, 2 * ROOM - 1024)
 
-        ts_win = keep.tile([P, T], U8, name="ts_win", align_bytes=64)
+        ts_win = pin.tile([P, T], U8, name="ts_win", align_bytes=64, offset=1984)
         nc.vector.memset(ts_win[:].bitcast(I32), 0)
         for e in range(2):
             nc.scalar.dma_start(ts_win[e:P:16, :].bitcast(I32), tab_scales[0, e:16:2, :].bitcast(I32))
@@ -69,7 +72,7 @@ def tile_list_seawater_horner_surrogate_kernel(
 
         def load_scale_rows(name, src, width):
             rows = keep.tile([P, PASSES, width], U8, name=name, align_bytes=64)
-            nc.gpsimd.memset(rows[:].rearrange("p a c -> p (a c)").bitcast(I32), 0)
+            nc.vector.memset(rows[:].rearrange("p a c -> p (a c)").bitcast(I32), 0)
             for d in range(4):
                 nc.gpsimd.dma_start(
                     rows[32 * d : 32 * d + 4, :, :].bitcast(I32),
@@ -88,20 +91,22 @@ def tile_list_seawater_horner_surrogate_kernel(
         nc.sync.dma_start(w2_raw[:], w2_words.rearrange("a p c -> p a c").bitcast(I32))
 
         def load_table(a):
-            win = keep.tile([P, T], I32, name="tab_win", tag=f"room{a}", align_bytes=64)
+            win = head.tile([P, T], I32, name=f"tab_win{a}", align_bytes=64, offset=2 * a * ROOM)
             nc.sync.dma_start(win[:], tab_words[a].rearrange("p t i -> p (t i)").bitcast(I32))
             return win
 
         tab_win = [load_table(0)]
-        load_w1(0, 0, FIRST, P, "room4")
-        load_w1(1, 0, 0, P, "room2")
+        load_w1(0, 0, FIRST, P, 3 * ROOM)
+        load_w1(1, 0, 0, P, ROOM)
         tab_win.append(load_table(1))
 
         w1_codes = [keep.tile([P, PASSES, KP], U32, name=f"w1c{b}", align_bytes=64) for b in range(BLOCKS)]
-        w1_scales = [keep.tile([P, PASSES, KP], U8, name=f"w1s{b}", align_bytes=64) for b in range(BLOCKS)]
+        w1_scales = {(0, 0): pin.tile([P, KP], U8, name="w1s00", align_bytes=64, offset=3072)}
+        for a, b in ((1, 0), (0, 1), (1, 1)):
+            w1_scales[a, b] = keep.tile([P, KP], U8, name=f"w1s{a}{b}", align_bytes=64)
         w1_bf = {}
         for a in range(PASSES):
-            w1_bf[a, 0] = keep.tile([P, PACK * KP], BF16, name=f"w1b{a}0", align_bytes=64)
+            w1_bf[a, 0] = pin.tile([P, PACK * KP], BF16, name=f"w1b{a}0", align_bytes=64, offset=8192 + a * 4096)
             w1_bf[a, 1] = early.tile([P, PACK * KP], BF16, name=f"w1b{a}1", align_bytes=64, offset=a * 4096)
 
         def cast(a, b, m0, m1, engine, base=0):
@@ -114,7 +119,7 @@ def tile_list_seawater_horner_surrogate_kernel(
 
         def quantize_w1(b, a):
             nc.vector.quantize_mx(
-                out=w1_codes[b][:, a, :].bitcast(FP8X4), scales=w1_scales[b][:, a, :], in_=w1_bf[a, b][:]
+                out=w1_codes[b][:, a, :].bitcast(FP8X4), scales=w1_scales[a, b][:], in_=w1_bf[a, b][:]
             )
 
         cast(0, 0, 0, FIRST, "s")
@@ -132,36 +137,40 @@ def tile_list_seawater_horner_surrogate_kernel(
         w2p, w2sp = [], []
 
         def permute_w2(b):
-            words = keep.tile([P, PASSES, PACK, 2 * P], U8, name=f"w2p{b}", align_bytes=64)
+            words = pin.tile([P, PASSES, PACK, 2 * P], U8, name=f"w2p{b}", align_bytes=64, offset=b * 8192)
             src = w2_raw[:].bitcast(U16)[:, :, b * KP : (b + 1) * KP]
             nc.vector.tensor_copy(words[:].bitcast(U16), src.rearrange("p a (m t) -> p a t m", t=PACK))
-            scales = keep.tile([P, PASSES, PACK, P], U8, name=f"w2sp{b}", align_bytes=64)
+            scales = pin.tile([P, PASSES, PACK, P], U8, name=f"w2sp{b}", align_bytes=64, offset=b * 8192 + 2048)
             ssrc = w2s_raw[:, :, b * KP : (b + 1) * KP]
             nc.vector.tensor_copy(scales[:], ssrc.rearrange("p a (m t) -> p a t m", t=PACK))
             w2p.append(words)
             w2sp.append(scales)
 
         v_words = {}
+        v_pass = [
+            pin.tile([P, S], I32, name="v_pass0", align_bytes=64, offset=3968),
+            keep.tile([P, S], I32, name="v_pass1", align_bytes=64),
+        ]
 
         def gather(a, s):
-            got = keep.tile([P, NT], I32, name=f"v{a}{s}", align_bytes=64)
+            got = v_pass[a][:, s * NT : (s + 1) * NT]
             lists = offsets[:, s * (NT // 16) : (s + 1) * (NT // 16)]
-            nc.vector.tensor_copy(got[:].bitcast(U32), tab_win[a][:].bitcast(U32).indirect(lists))
+            nc.vector.tensor_copy(got.bitcast(U32), tab_win[a][:].bitcast(U32).indirect(lists))
             v_words[a, s] = got
 
         permute_w2(0)
         gather(0, 0)
         gather(0, 1)
-        load_w1(0, 1, 0, P, "room0")
-        permute_w2(1)
+        load_w1(0, 1, 0, P, 0)
         cast(0, 0, FIRST, P, "s", FIRST)
         quantize_w1(0, 0)
+        permute_w2(1)
         cast(1, 0, 0, P, "s")
-        load_w1(1, 1, 0, P, "room2")
+        load_w1(1, 1, 0, P, ROOM)
         gather(1, 0)
         quantize_w1(0, 1)
         gather(1, 1)
-        w3c = keep.tile([P, PASSES, N], I32, name="w3c", tag="room1", align_bytes=64)
+        w3c = head.tile([P, PASSES, N], I32, name="w3c", align_bytes=64, offset=2 * ROOM)
         nc.sync.dma_start(w3c[:], w3_words.rearrange("a p c i -> p a (c i)").bitcast(I32))
 
         groups = [(b, s) for b in range(BLOCKS) for s in range(HALVES)]
@@ -203,7 +212,7 @@ def tile_list_seawater_horner_surrogate_kernel(
             if a == 0:
                 x_ps[i] = psum.tile([P, c1 - c0], F32, name="x_ps", tag=f"x{i % 4}")
             cols = slice(t * P, (t + 1) * P)
-            first_stage(x_ps[i], w1_codes[b][:, a, cols].bitcast(FP8X4), w1_scales[b][:, a, cols], a, s, c0, c1)
+            first_stage(x_ps[i], w1_codes[b][:, a, cols].bitcast(FP8X4), w1_scales[a, b][:, cols], a, s, c0, c1)
 
         def horner_inner(i):
             ch, t = steps[i]

@@ -24,11 +24,11 @@ NT = 512
 PASSES = K // KP
 BLOCKS = H // KP
 HALVES = S // NT
-LAST_CHUNKS = ((0, 256), (256, 512))
-BIAS_ENGINE = ("g", "g", "g", "g", "s")
-WEAVE_ENGINE = ("g", "s", "s", "s", "v")
-WEAVE_AT = {4: ((0, 0, 4),), 5: ((0, 1, 4),), 6: ((0, 2, 4),), 7: ((0, 3, 4),), 8: ((1, 0, 2),), 9: ((1, 1, 2),), 11: ((2, 0, 2),), 12: ((2, 1, 2),), 15: ((3, 0, 1),), 19: ((4, 0, 1),)}
-QUANT_AT = {10: (0,), 11: (1,), 15: (2,), 18: (3,), 20: (4,)}
+LAST_CHUNKS = ((0, 256), (256, 384), (384, 512))
+BIAS_ENGINE = ("g", "g", "g", "g", "s", "s")
+WEAVE_ENGINE = ("g", "s", "s", "s", "v", "v")
+WEAVE_AT = {4: ((0, 0, 4),), 5: ((0, 1, 4),), 6: ((0, 2, 4),), 7: ((0, 3, 4),), 8: ((1, 0, 2),), 9: ((1, 1, 2),), 11: ((2, 0, 2),), 12: ((2, 1, 2),), 15: ((3, 0, 1),), 20: ((4, 0, 1),), 23: ((5, 0, 1),)}
+QUANT_AT = {10: (0,), 11: (1,), 15: (2,), 19: (3,), 22: (4,), 24: (5,)}
 CAST_ENGINE = ("s", "s", "s", "s")
 CAST_AT = {0: (0,), 1: (1,), 2: (2,), 3: (3,)}
 W1Q_AT = {2: (0,), 4: (1,)}
@@ -64,11 +64,18 @@ def tile_list_seawater_horner_surrogate_kernel(
 
         load_w1(0, 0, 0, FIRST, 2 * ROOM - 1024)
 
+        q_col = keep.tile([P, BLOCKS, PACK], F32, name="q_col")
+        c_col = keep.tile([P, BLOCKS, PACK], F32, name="c_col")
+        nc.sync.dma_start(q_col[:], quad.rearrange("(b p t) -> p b t", p=P, t=PACK))
+        nc.sync.dma_start(c_col[:], cons.rearrange("(b p t) -> p b t", p=P, t=PACK))
+        w2_raw = keep.tile([P, PASSES, H // 2], I32, name="w2_raw", align_bytes=64)
+        nc.sync.dma_start(w2_raw[:], w2_words.rearrange("a p c -> p a c").bitcast(I32))
+
         ts_win = pin.tile([P, T], U8, name="ts_win", align_bytes=64, offset=1984)
         nc.vector.memset(ts_win[:].bitcast(I32), 0)
         for e in range(2):
-            nc.scalar.dma_start(ts_win[e:P:16, :].bitcast(I32), tab_scales[0, e:16:2, :].bitcast(I32))
-        nc.scalar.dma_start(ts_win[4:P:8, :].bitcast(I32), tab_scales[1].bitcast(I32))
+            nc.sync.dma_start(ts_win[e:P:16, :].bitcast(I32), tab_scales[0, e:16:2, :].bitcast(I32))
+        nc.sync.dma_start(ts_win[4:P:8, :].bitcast(I32), tab_scales[1].bitcast(I32))
 
         def load_scale_rows(name, src, width):
             rows = keep.tile([P, PASSES, width], U8, name=name, align_bytes=64)
@@ -81,24 +88,20 @@ def tile_list_seawater_horner_surrogate_kernel(
             return rows
 
         w2s_raw = load_scale_rows("w2s_raw", w2_scales, H)
-        q_col = keep.tile([P, BLOCKS, PACK], F32, name="q_col")
-        c_col = keep.tile([P, BLOCKS, PACK], F32, name="c_col")
-        nc.gpsimd.dma_start(q_col[:], quad.rearrange("(b p t) -> p b t", p=P, t=PACK))
-        nc.gpsimd.dma_start(c_col[:], cons.rearrange("(b p t) -> p b t", p=P, t=PACK))
         w3s = load_scale_rows("w3s", w3_scales, N)
 
-        w2_raw = keep.tile([P, PASSES, H // 2], I32, name="w2_raw", align_bytes=64)
-        nc.sync.dma_start(w2_raw[:], w2_words.rearrange("a p c -> p a c").bitcast(I32))
 
         def load_table(a):
-            win = head.tile([P, T], I32, name=f"tab_win{a}", align_bytes=64, offset=2 * a * ROOM)
+            if a == 0:
+                win = head.tile([P, T], I32, name="tab_win0", align_bytes=64, offset=0)
+            else:
+                win = pin.tile([P, T], I32, name="tab_win1", align_bytes=64, offset=3968)
             nc.sync.dma_start(win[:], tab_words[a].rearrange("p t i -> p (t i)").bitcast(I32))
             return win
 
         tab_win = [load_table(0)]
         load_w1(0, 0, FIRST, P, 3 * ROOM)
         load_w1(1, 0, 0, P, ROOM)
-        tab_win.append(load_table(1))
 
         w1_codes = [keep.tile([P, PASSES, KP], U32, name=f"w1c{b}", align_bytes=64) for b in range(BLOCKS)]
         w1_scales = {(0, 0): pin.tile([P, KP], U8, name="w1s00", align_bytes=64, offset=3072)}
@@ -106,7 +109,7 @@ def tile_list_seawater_horner_surrogate_kernel(
             w1_scales[a, b] = keep.tile([P, KP], U8, name=f"w1s{a}{b}", align_bytes=64)
         w1_bf = {}
         for a in range(PASSES):
-            w1_bf[a, 0] = pin.tile([P, PACK * KP], BF16, name=f"w1b{a}0", align_bytes=64, offset=8192 + a * 4096)
+            w1_bf[a, 0] = pin.tile([P, PACK * KP], BF16, name=f"w1b{a}0", align_bytes=64, offset=12288 + a * 4096)
             w1_bf[a, 1] = early.tile([P, PACK * KP], BF16, name=f"w1b{a}1", align_bytes=64, offset=a * 4096)
 
         def cast(a, b, m0, m1, engine, base=0):
@@ -129,18 +132,19 @@ def tile_list_seawater_horner_surrogate_kernel(
         v_plane = [keep.tile([P, S], U8, name=f"v_plane{a}", align_bytes=64) for a in range(PASSES)]
         nc.vector.tensor_copy(v_plane[0][:].bitcast(I32), ts_got[:].bitcast(I32))
         nc.vector.memset(v_plane[1][:].bitcast(I32), 0)
-        for r in range(2, 4):
-            nc.scalar.dma_start(v_plane[0][r:P:32, :].bitcast(I32), ts_got[14 + r : P : 32, :].bitcast(I32))
         for r in range(4):
-            nc.scalar.dma_start(v_plane[1][r:P:32, :].bitcast(I32), ts_got[8 * r + 4 : P : 32, :].bitcast(I32))
+            nc.sync.dma_start(v_plane[1][r:P:32, :].bitcast(I32), ts_got[8 * r + 4 : P : 32, :].bitcast(I32))
+        for r in range(2, 4):
+            nc.sync.dma_start(v_plane[0][r:P:32, :].bitcast(I32), ts_got[14 + r : P : 32, :].bitcast(I32))
+        tab_win.append(load_table(1))
 
         w2p, w2sp = [], []
 
         def permute_w2(b):
-            words = pin.tile([P, PASSES, PACK, 2 * P], U8, name=f"w2p{b}", align_bytes=64, offset=b * 8192)
+            words = pin.tile([P, PASSES, PACK, 2 * P], U8, name=f"w2p{b}", align_bytes=64, offset=b * 12288)
             src = w2_raw[:].bitcast(U16)[:, :, b * KP : (b + 1) * KP]
             nc.vector.tensor_copy(words[:].bitcast(U16), src.rearrange("p a (m t) -> p a t m", t=PACK))
-            scales = pin.tile([P, PASSES, PACK, P], U8, name=f"w2sp{b}", align_bytes=64, offset=b * 8192 + 2048)
+            scales = pin.tile([P, PASSES, PACK, P], U8, name=f"w2sp{b}", align_bytes=64, offset=b * 12288 + 2048)
             ssrc = w2s_raw[:, :, b * KP : (b + 1) * KP]
             nc.vector.tensor_copy(scales[:], ssrc.rearrange("p a (m t) -> p a t m", t=PACK))
             w2p.append(words)
@@ -148,7 +152,7 @@ def tile_list_seawater_horner_surrogate_kernel(
 
         v_words = {}
         v_pass = [
-            pin.tile([P, S], I32, name="v_pass0", align_bytes=64, offset=3968),
+            keep.tile([P, S], I32, name="v_pass0", align_bytes=64),
             keep.tile([P, S], I32, name="v_pass1", align_bytes=64),
         ]
 
@@ -170,7 +174,7 @@ def tile_list_seawater_horner_surrogate_kernel(
         gather(1, 0)
         quantize_w1(0, 1)
         gather(1, 1)
-        w3c = head.tile([P, PASSES, N], I32, name="w3c", align_bytes=64, offset=2 * ROOM)
+        w3c = pin.tile([P, PASSES, N], I32, name="w3c", align_bytes=64, offset=8192)
         nc.sync.dma_start(w3c[:], w3_words.rearrange("a p c i -> p a (c i)").bitcast(I32))
 
         groups = [(b, s) for b in range(BLOCKS) for s in range(HALVES)]

@@ -35,6 +35,9 @@ W1Q_AT = {2: (0,), 4: (1,)}
 FIRST = 32
 PINS = [0, 2]
 ROOM = 8192
+B_EARLY = 3
+X_EARLY = 2
+MOVES_FIRST = 6
 B_LEAD = 4
 X_LEAD = 3
 
@@ -73,9 +76,8 @@ def tile_list_seawater_horner_surrogate_kernel(
 
         ts_win = pin.tile([P, T], U8, name="ts_win", align_bytes=64, offset=1984)
         nc.vector.memset(ts_win[:].bitcast(I32), 0)
-        for e in range(2):
-            nc.sync.dma_start(ts_win[e:P:16, :].bitcast(I32), tab_scales[0, e:16:2, :].bitcast(I32))
-        nc.sync.dma_start(ts_win[4:P:8, :].bitcast(I32), tab_scales[1].bitcast(I32))
+        for a in range(PASSES):
+            nc.sync.dma_start(ts_win[4 * a : P : 8, :].bitcast(I32), tab_scales[a].bitcast(I32))
 
         def load_scale_rows(name, src, width):
             rows = keep.tile([P, PASSES, width], U8, name=name, align_bytes=64)
@@ -130,24 +132,29 @@ def tile_list_seawater_horner_surrogate_kernel(
         nc.vector.tensor_copy(ts_got[:], ts_win[:].indirect(offsets[:]))
 
         v_plane = [keep.tile([P, S], U8, name=f"v_plane{a}", align_bytes=64) for a in range(PASSES)]
-        nc.vector.tensor_copy(v_plane[0][:].bitcast(I32), ts_got[:].bitcast(I32))
-        nc.vector.memset(v_plane[1][:].bitcast(I32), 0)
-        for r in range(4):
-            nc.sync.dma_start(v_plane[1][r:P:32, :].bitcast(I32), ts_got[8 * r + 4 : P : 32, :].bitcast(I32))
-        for r in range(2, 4):
-            nc.sync.dma_start(v_plane[0][r:P:32, :].bitcast(I32), ts_got[14 + r : P : 32, :].bitcast(I32))
-        tab_win.append(load_table(1))
+        for a in range(PASSES):
+            nc.vector.memset(v_plane[a][:].bitcast(I32), 0)
+        for k in range(PASSES * 4):
+            a, d = divmod(k, 4)
+            if k == MOVES_FIRST:
+                tab_win.append(load_table(1))
+            nc.sync.dma_start(
+                v_plane[a][32 * d : 32 * d + 4, :].bitcast(I32),
+                ts_got[32 * d + 4 * a : 32 * d + 32 : 8, :].bitcast(I32),
+            )
 
         w2p, w2sp = [], []
 
-        def permute_w2(b):
+        def permute_words(b):
             words = pin.tile([P, PASSES, PACK, 2 * P], U8, name=f"w2p{b}", align_bytes=64, offset=b * 12288)
             src = w2_raw[:].bitcast(U16)[:, :, b * KP : (b + 1) * KP]
             nc.vector.tensor_copy(words[:].bitcast(U16), src.rearrange("p a (m t) -> p a t m", t=PACK))
-            scales = pin.tile([P, PASSES, PACK, P], U8, name=f"w2sp{b}", align_bytes=64, offset=b * 12288 + 2048)
+            w2p.append(words)
+
+        def permute_scales(b):
+            scales = pin.tile([P, PASSES, PACK, P], U8, name=f"w2sp{b}", align_bytes=64, offset=12288 + 2048 + b * 1024)
             ssrc = w2s_raw[:, :, b * KP : (b + 1) * KP]
             nc.vector.tensor_copy(scales[:], ssrc.rearrange("p a (m t) -> p a t m", t=PACK))
-            w2p.append(words)
             w2sp.append(scales)
 
         v_words = {}
@@ -162,13 +169,15 @@ def tile_list_seawater_horner_surrogate_kernel(
             nc.vector.tensor_copy(got.bitcast(U32), tab_win[a][:].bitcast(U32).indirect(lists))
             v_words[a, s] = got
 
-        permute_w2(0)
+        permute_words(0)
         gather(0, 0)
         gather(0, 1)
         load_w1(0, 1, 0, P, 0)
         cast(0, 0, FIRST, P, "s", FIRST)
         quantize_w1(0, 0)
-        permute_w2(1)
+        permute_scales(0)
+        permute_words(1)
+        permute_scales(1)
         cast(1, 0, 0, P, "s")
         load_w1(1, 1, 0, P, ROOM)
         gather(1, 0)
@@ -185,38 +194,40 @@ def tile_list_seawater_horner_surrogate_kernel(
         b_ps = {}
         b_sb, x_ps, inner, y_sb, h_planes, h_il, h_q = {}, {}, {}, {}, {}, {}, {}
 
-        def first_stage(acc, codes, scales, a, s, c0, c1):
+        def first_stage(acc, codes, scales, a, k, s, c0, c1):
             nc.tensor.matmul_mx(
                 out=acc[:],
                 lhsT=codes,
                 lhsT_scale=scales,
                 rhs=v_words[a, s][:, c0:c1].bitcast(FP8X4),
                 rhs_scale=v_plane[a][:, s * NT + c0 : s * NT + c1],
-                start=(a == 0),
-                stop=(a == PASSES - 1),
+                start=(k == 0),
+                stop=(k == PASSES - 1),
             )
 
-        def matmul_b(u, a):
+        def matmul_b(u, k):
             g, t = units[u]
             b, s = groups[g]
-            if a == 0:
+            a = k if u < B_EARLY else 1 - k
+            if k == 0:
                 b_ps[u] = psum.tile([P, NT], F32, name="b_ps", tag=f"b{u % 4}")
-            first_stage(b_ps[u], w2p[b][:, a, t, :].bitcast(FP4X4), w2sp[b][:, a, t, :], a, s, 0, NT)
-            if a == PASSES - 1:
+            first_stage(b_ps[u], w2p[b][:, a, t, :].bitcast(FP4X4), w2sp[b][:, a, t, :], a, k, s, 0, NT)
+            if k == PASSES - 1:
                 if u in PINS:
                     b_sb[g, t] = early.tile([P, NT], F32, name=f"b_pin{u}", align_bytes=64, offset=PINS.index(u) * 4096)
                 else:
                     b_sb[g, t] = ring.tile([P, NT], F32, name="b_sb", bufs=8)
                 nc.scalar.copy(b_sb[g, t][:], b_ps[u][:])
 
-        def matmul_x(i, a):
+        def matmul_x(i, k):
             ch, t = steps[i]
             g, c0, c1 = chunks[ch]
             b, s = groups[g]
-            if a == 0:
+            a = k if i < X_EARLY else 1 - k
+            if k == 0:
                 x_ps[i] = psum.tile([P, c1 - c0], F32, name="x_ps", tag=f"x{i % 4}")
             cols = slice(t * P, (t + 1) * P)
-            first_stage(x_ps[i], w1_codes[b][:, a, cols].bitcast(FP8X4), w1_scales[a, b][:, cols], a, s, c0, c1)
+            first_stage(x_ps[i], w1_codes[b][:, a, cols].bitcast(FP8X4), w1_scales[a, b][:, cols], a, k, s, c0, c1)
 
         def horner_inner(i):
             ch, t = steps[i]
@@ -315,14 +326,16 @@ def tile_list_seawater_horner_surrogate_kernel(
             if groups[chunks[ch][0]][0] == BLOCKS - 1:
                 second_stage(ch)
 
-        for u in range(B_LEAD):
-            matmul_b(u, 0)
-        for u in range(X_LEAD):
+        for u in range(X_EARLY):
             matmul_x(u, 0)
+        for u in range(B_EARLY):
+            matmul_b(u, 0)
         for u in range(B_LEAD):
-            matmul_b(u, 1)
+            for k in range(1 if u < B_EARLY else 0, PASSES):
+                matmul_b(u, k)
             if u < X_LEAD:
-                matmul_x(u, 1)
+                for k in range(1 if u < X_EARLY else 0, PASSES):
+                    matmul_x(u, k)
         horner_inner(0)
         for i in range(len(steps) + 2):
             for a in range(PASSES):

@@ -15,7 +15,7 @@ FP8X4 = mybir.dt.float8_e4m3fn_x4
 FP4X4 = mybir.dt.float4_e2m1fn_x4
 MULT = mybir.AluOpType.mult
 ADD = mybir.AluOpType.add
-IDENT = mybir.ActivationFunctionType.Identity
+IDENTITY = mybir.ActivationFunctionType.Identity
 
 P = 128
 PACK = 4
@@ -24,22 +24,29 @@ NT = 512
 PASSES = K // KP
 BLOCKS = H // KP
 HALVES = S // NT
+QUADRANTS = P // 32
+RING = 4
+
 LAST_CHUNKS = ((0, 256), (256, 384), (384, 512))
-BIAS_ENGINE = ("g", "g", "g", "g", "s", "s")
-WEAVE_ENGINE = ("g", "s", "s", "s", "v", "v")
-WEAVE_AT = {4: ((0, 0, 4),), 5: ((0, 1, 4),), 6: ((0, 2, 4),), 7: ((0, 3, 4),), 8: ((1, 0, 2),), 9: ((1, 1, 2),), 11: ((2, 0, 2),), 12: ((2, 1, 2),), 15: ((3, 0, 1),), 20: ((4, 0, 1),), 23: ((5, 0, 1),)}
-QUANT_AT = {10: (0,), 11: (1,), 15: (2,), 19: (3,), 22: (4,), 24: (5,)}
-CAST_ENGINE = ("s", "s", "s", "s")
-CAST_AT = {0: (0,), 1: (1,), 2: (2,), 3: (3,)}
-W1Q_AT = {2: (0,), 4: (1,)}
-FIRST = 32
-PINS = [0, 2]
-ROOM = 8192
+WEAVE = (("gpsimd", 4), ("scalar", 2), ("scalar", 2), ("scalar", 1), ("vector", 1), ("vector", 1))
+QUANT_AFTER_OTHERS = 7
+QUANT_AFTER_VECTOR = 3
+B_LEAD = 4
+X_LEAD = 3
 B_EARLY = 3
 X_EARLY = 2
 MOVES_FIRST = 6
-B_LEAD = 4
-X_LEAD = 3
+
+ROOM = 8192
+W2_WORDS_AT = (0, 12288)
+SCALE_WINDOW_AT = 1984
+W1_SCALES_AT = 3072
+TABLE1_AT = 3968
+W3_AT = 8192
+W1_BF16_AT = (12288, 16384)
+W2_SCALES_AT = (14336, 15360)
+LATE_AT = (0, 4096)
+LATE_STEPS = (0, 2)
 
 
 def tile_list_seawater_horner_surrogate_kernel(
@@ -49,310 +56,293 @@ def tile_list_seawater_horner_surrogate_kernel(
     with ExitStack() as ctx:
         keep = ctx.enter_context(tc.tile_pool(name="keep", bufs=1))
         ring = ctx.enter_context(tc.tile_pool(name="ring", bufs=2))
-        early = ctx.enter_context(tc.tile_pool(name="early", bufs=1))
-        head = ctx.enter_context(tc.tile_pool(name="head", bufs=1))
-        pin = ctx.enter_context(tc.tile_pool(name="pin", bufs=1))
+        late = ctx.enter_context(tc.tile_pool(name="late", bufs=1))
+        rooms = ctx.enter_context(tc.tile_pool(name="rooms", bufs=1))
+        shared = ctx.enter_context(tc.tile_pool(name="shared", bufs=1))
         psum = ctx.enter_context(tc.psum_pool(name="psum", bufs=1))
 
         offsets = keep.tile([P, S // 16], U16, name="offsets")
         nc.sync.dma_start(offsets[:], offs)
 
-        w1_raw = {}
-
-        def load_w1(a, b, m0, m1, room):
-            raw = head.tile([P, PACK, PACK * (m1 - m0)], F32, name=f"w1_raw{a}{b}{m0}", align_bytes=64, offset=room)
-            cols = slice(b * KP + PACK * m0, b * KP + PACK * m1)
-            nc.sync.dma_start(raw[:], w1[a * KP : (a + 1) * KP, cols].rearrange("(p j) c -> p j c", j=PACK))
-            w1_raw[a, b, m0] = raw
-
-        load_w1(0, 0, 0, FIRST, 2 * ROOM - 1024)
-
         q_col = keep.tile([P, BLOCKS, PACK], F32, name="q_col")
         c_col = keep.tile([P, BLOCKS, PACK], F32, name="c_col")
         nc.sync.dma_start(q_col[:], quad.rearrange("(b p t) -> p b t", p=P, t=PACK))
-        nc.sync.dma_start(c_col[:], cons.rearrange("(b p t) -> p b t", p=P, t=PACK))
         w2_raw = keep.tile([P, PASSES, H // 2], I32, name="w2_raw", align_bytes=64)
-        nc.sync.dma_start(w2_raw[:], w2_words.rearrange("a p c -> p a c").bitcast(I32))
-
-        ts_win = pin.tile([P, T], U8, name="ts_win", align_bytes=64, offset=1984)
-        nc.vector.memset(ts_win[:].bitcast(I32), 0)
         for a in range(PASSES):
-            nc.sync.dma_start(ts_win[4 * a : P : 8, :].bitcast(I32), tab_scales[a].bitcast(I32))
+            nc.sync.dma_start(w2_raw[:, a, :], w2_words[a].bitcast(I32))
 
-        def load_scale_rows(name, src, width):
-            rows = keep.tile([P, PASSES, width], U8, name=name, align_bytes=64)
-            nc.vector.memset(rows[:].rearrange("p a c -> p (a c)").bitcast(I32), 0)
-            for d in range(4):
+        scale_window = shared.tile([P, T], U8, name="scale_window", align_bytes=64, offset=SCALE_WINDOW_AT)
+        nc.vector.memset(scale_window[:].bitcast(I32), 0)
+        for a in range(PASSES):
+            nc.sync.dma_start(scale_window[4 * a : P : 8, :].bitcast(I32), tab_scales[a].bitcast(I32))
+
+        def load_planes(name, src, width):
+            planes = keep.tile([P, PASSES, width], U8, name=name, align_bytes=64)
+            nc.vector.memset(planes[:].rearrange("p a c -> p (a c)").bitcast(I32), 0)
+            for d in range(QUADRANTS):
                 nc.gpsimd.dma_start(
-                    rows[32 * d : 32 * d + 4, :, :].bitcast(I32),
+                    planes[32 * d : 32 * d + 4, :, :].bitcast(I32),
                     src[:, 4 * d : 4 * d + 4, :].rearrange("a r c -> r a c").bitcast(I32),
                 )
-            return rows
+            return planes
 
-        w2s_raw = load_scale_rows("w2s_raw", w2_scales, H)
-        w3s = load_scale_rows("w3s", w3_scales, N)
+        w2_planes_raw = load_planes("w2_planes_raw", w2_scales, H)
+        nc.gpsimd.dma_start(c_col[:], cons.rearrange("(b p t) -> p b t", p=P, t=PACK))
+        w3_planes = load_planes("w3_planes", w3_scales, N)
 
+        def load_table(a, pool, at):
+            window = pool.tile([P, T], I32, name=f"table{a}", align_bytes=64, offset=at)
+            nc.sync.dma_start(window[:], tab_words[a].rearrange("p t i -> p (t i)").bitcast(I32))
+            return window
 
-        def load_table(a):
-            if a == 0:
-                win = head.tile([P, T], I32, name="tab_win0", align_bytes=64, offset=0)
-            else:
-                win = pin.tile([P, T], I32, name="tab_win1", align_bytes=64, offset=3968)
-            nc.sync.dma_start(win[:], tab_words[a].rearrange("p t i -> p (t i)").bitcast(I32))
-            return win
+        w1_raw = {}
 
-        tab_win = [load_table(0)]
-        load_w1(0, 0, FIRST, P, 3 * ROOM)
-        load_w1(1, 0, 0, P, ROOM)
+        def load_w1(a, b, room):
+            raw = rooms.tile([P, PACK, KP], F32, name=f"w1_raw{a}{b}", align_bytes=64, offset=room * ROOM)
+            rows = w1[a * KP : (a + 1) * KP, b * KP : (b + 1) * KP]
+            nc.sync.dma_start(raw[:], rows.rearrange("(p j) c -> p j c", j=PACK))
+            w1_raw[a, b] = raw
 
-        w1_codes = [keep.tile([P, PASSES, KP], U32, name=f"w1c{b}", align_bytes=64) for b in range(BLOCKS)]
-        w1_scales = {(0, 0): pin.tile([P, KP], U8, name="w1s00", align_bytes=64, offset=3072)}
+        table = [load_table(0, rooms, 0)]
+        load_w1(0, 0, 2)
+        load_w1(1, 0, 1)
+
+        w1_codes = [keep.tile([P, PASSES, KP], U32, name=f"w1_codes{b}", align_bytes=64) for b in range(BLOCKS)]
+        w1_planes = {(0, 0): shared.tile([P, KP], U8, name="w1_plane00", align_bytes=64, offset=W1_SCALES_AT)}
         for a, b in ((1, 0), (0, 1), (1, 1)):
-            w1_scales[a, b] = keep.tile([P, KP], U8, name=f"w1s{a}{b}", align_bytes=64)
-        w1_bf = {}
+            w1_planes[a, b] = keep.tile([P, KP], U8, name=f"w1_plane{a}{b}", align_bytes=64)
+        w1_bf16 = {}
         for a in range(PASSES):
-            w1_bf[a, 0] = pin.tile([P, PACK * KP], BF16, name=f"w1b{a}0", align_bytes=64, offset=12288 + a * 4096)
-            w1_bf[a, 1] = early.tile([P, PACK * KP], BF16, name=f"w1b{a}1", align_bytes=64, offset=a * 4096)
+            w1_bf16[a, 0] = shared.tile([P, PACK * KP], BF16, name=f"w1_bf{a}0", align_bytes=64, offset=W1_BF16_AT[a])
+            w1_bf16[a, 1] = late.tile([P, PACK * KP], BF16, name=f"w1_bf{a}1", align_bytes=64, offset=LATE_AT[a])
 
-        def cast(a, b, m0, m1, engine, base=0):
-            dst = w1_bf[a, b][:].rearrange("p (t m j) -> p m j t", t=PACK, j=PACK)[:, m0:m1]
-            src = w1_raw[a, b, base][:].rearrange("p j (m t) -> p m j t", t=PACK)[:, m0 - base : m1 - base]
-            if engine == "v":
-                nc.vector.tensor_copy(dst, src)
-            else:
-                nc.scalar.copy(dst, src)
+        def cast_w1(a, b, m0, m1):
+            dst = w1_bf16[a, b][:].rearrange("p (t m j) -> p m j t", t=PACK, j=PACK)[:, m0:m1]
+            src = w1_raw[a, b][:].rearrange("p j (m t) -> p m j t", t=PACK)[:, m0:m1]
+            nc.scalar.copy(dst, src)
 
-        def quantize_w1(b, a):
+        def quantize_w1(a, b):
             nc.vector.quantize_mx(
-                out=w1_codes[b][:, a, :].bitcast(FP8X4), scales=w1_scales[a, b][:], in_=w1_bf[a, b][:]
+                out=w1_codes[b][:, a, :].bitcast(FP8X4), scales=w1_planes[a, b][:], in_=w1_bf16[a, b][:]
             )
 
-        cast(0, 0, 0, FIRST, "s")
-        ts_got = keep.tile([P, S], U8, name="ts_got", align_bytes=64)
-        nc.vector.tensor_copy(ts_got[:], ts_win[:].indirect(offsets[:]))
-
-        v_plane = [keep.tile([P, S], U8, name=f"v_plane{a}", align_bytes=64) for a in range(PASSES)]
+        scales_got = keep.tile([P, S], U8, name="scales_got", align_bytes=64)
+        nc.vector.tensor_copy(scales_got[:], scale_window[:].indirect(offsets[:]))
+        v_planes = [keep.tile([P, S], U8, name=f"v_plane{a}", align_bytes=64) for a in range(PASSES)]
         for a in range(PASSES):
-            nc.vector.memset(v_plane[a][:].bitcast(I32), 0)
-        for k in range(PASSES * 4):
-            a, d = divmod(k, 4)
-            if k == MOVES_FIRST:
-                tab_win.append(load_table(1))
+            nc.vector.memset(v_planes[a][:].bitcast(I32), 0)
+        for move in range(PASSES * QUADRANTS):
+            a, d = divmod(move, QUADRANTS)
+            if move == MOVES_FIRST:
+                table.append(load_table(1, shared, TABLE1_AT))
             nc.sync.dma_start(
-                v_plane[a][32 * d : 32 * d + 4, :].bitcast(I32),
-                ts_got[32 * d + 4 * a : 32 * d + 32 : 8, :].bitcast(I32),
+                v_planes[a][32 * d : 32 * d + 4, :].bitcast(I32),
+                scales_got[32 * d + 4 * a : 32 * d + 32 : 8, :].bitcast(I32),
             )
 
-        w2p, w2sp = [], []
+        w2_codes, w2_planes = [], []
 
-        def permute_words(b):
-            words = pin.tile([P, PASSES, PACK, 2 * P], U8, name=f"w2p{b}", align_bytes=64, offset=b * 12288)
+        def order_w2_words(b):
+            words = shared.tile([P, PASSES, PACK, 2 * P], U8, name=f"w2_codes{b}", align_bytes=64, offset=W2_WORDS_AT[b])
             src = w2_raw[:].bitcast(U16)[:, :, b * KP : (b + 1) * KP]
             nc.vector.tensor_copy(words[:].bitcast(U16), src.rearrange("p a (m t) -> p a t m", t=PACK))
-            w2p.append(words)
+            w2_codes.append(words)
 
-        def permute_scales(b):
-            scales = pin.tile([P, PASSES, PACK, P], U8, name=f"w2sp{b}", align_bytes=64, offset=12288 + 2048 + b * 1024)
-            ssrc = w2s_raw[:, :, b * KP : (b + 1) * KP]
-            nc.vector.tensor_copy(scales[:], ssrc.rearrange("p a (m t) -> p a t m", t=PACK))
-            w2sp.append(scales)
+        def order_w2_scales(b):
+            planes = shared.tile([P, PASSES, PACK, P], U8, name=f"w2_planes{b}", align_bytes=64, offset=W2_SCALES_AT[b])
+            src = w2_planes_raw[:, :, b * KP : (b + 1) * KP]
+            nc.vector.tensor_copy(planes[:], src.rearrange("p a (m t) -> p a t m", t=PACK))
+            w2_planes.append(planes)
 
-        v_words = {}
-        v_pass = [
-            keep.tile([P, S], I32, name="v_pass0", align_bytes=64),
-            keep.tile([P, S], I32, name="v_pass1", align_bytes=64),
-        ]
+        v_codes = [keep.tile([P, S], I32, name=f"v_codes{a}", align_bytes=64) for a in range(PASSES)]
 
-        def gather(a, s):
-            got = v_pass[a][:, s * NT : (s + 1) * NT]
-            lists = offsets[:, s * (NT // 16) : (s + 1) * (NT // 16)]
-            nc.vector.tensor_copy(got.bitcast(U32), tab_win[a][:].bitcast(U32).indirect(lists))
-            v_words[a, s] = got
+        def gather_words(a, half):
+            lists = offsets[:, half * (NT // 16) : (half + 1) * (NT // 16)]
+            got = v_codes[a][:, half * NT : (half + 1) * NT]
+            nc.vector.tensor_copy(got.bitcast(U32), table[a][:].bitcast(U32).indirect(lists))
 
-        permute_words(0)
-        gather(0, 0)
-        gather(0, 1)
-        load_w1(0, 1, 0, P, 0)
-        cast(0, 0, FIRST, P, "s", FIRST)
+        order_w2_words(0)
+        gather_words(0, 0)
+        gather_words(0, 1)
+        load_w1(0, 1, 0)
+        cast_w1(0, 0, 0, P)
         quantize_w1(0, 0)
-        permute_scales(0)
-        permute_words(1)
-        permute_scales(1)
-        cast(1, 0, 0, P, "s")
-        load_w1(1, 1, 0, P, ROOM)
-        gather(1, 0)
-        quantize_w1(0, 1)
-        gather(1, 1)
-        w3c = pin.tile([P, PASSES, N], I32, name="w3c", align_bytes=64, offset=8192)
-        nc.sync.dma_start(w3c[:], w3_words.rearrange("a p c i -> p a (c i)").bitcast(I32))
+        order_w2_scales(0)
+        order_w2_words(1)
+        order_w2_scales(1)
+        cast_w1(1, 0, 0, P)
+        load_w1(1, 1, 1)
+        gather_words(1, 0)
+        quantize_w1(1, 0)
+        gather_words(1, 1)
+        w3_codes = shared.tile([P, PASSES, N], I32, name="w3_codes", align_bytes=64, offset=W3_AT)
+        nc.sync.dma_start(w3_codes[:], w3_words.rearrange("a p c i -> p a (c i)").bitcast(I32))
 
-        groups = [(b, s) for b in range(BLOCKS) for s in range(HALVES)]
-        last = len(groups) - 1
-        units = [(g, t) for g in range(len(groups)) for t in range(PACK)]
-        chunks = [(g, 0, NT) for g in range(last)] + [(last, c0, c1) for c0, c1 in LAST_CHUNKS]
+        groups = [(b, half) for b in range(BLOCKS) for half in range(HALVES)]
+        last_group = len(groups) - 1
+        chunks = [(g, 0, NT) for g in range(last_group)] + [(last_group, c0, c1) for c0, c1 in LAST_CHUNKS]
+        last_chunk = len(chunks) - 1
         steps = [(ch, t) for ch in range(len(chunks)) for t in range(PACK)]
-        b_ps = {}
-        b_sb, x_ps, inner, y_sb, h_planes, h_il, h_q = {}, {}, {}, {}, {}, {}, {}
+        banks = []
+        for i, (ch, t) in enumerate(steps):
+            if t % (NT // (chunks[ch][2] - chunks[ch][1])) == 0:
+                banks.append([])
+            banks[-1].append(i)
+        b_ps, b_sb, x_ps, inner, y_chunk, h_slots, h_woven, h_mx = {}, {}, {}, {}, {}, {}, {}, {}
 
-        def first_stage(acc, codes, scales, a, k, s, c0, c1):
+        def first_stage(acc, codes, plane, a, nth, c0, c1):
             nc.tensor.matmul_mx(
-                out=acc[:],
+                out=acc,
                 lhsT=codes,
-                lhsT_scale=scales,
-                rhs=v_words[a, s][:, c0:c1].bitcast(FP8X4),
-                rhs_scale=v_plane[a][:, s * NT + c0 : s * NT + c1],
-                start=(k == 0),
-                stop=(k == PASSES - 1),
+                lhsT_scale=plane,
+                rhs=v_codes[a][:, c0:c1].bitcast(FP8X4),
+                rhs_scale=v_planes[a][:, c0:c1],
+                start=(nth == 0),
+                stop=(nth == PASSES - 1),
             )
 
-        def matmul_b(u, k):
-            g, t = units[u]
-            b, s = groups[g]
-            a = k if u < B_EARLY else 1 - k
-            if k == 0:
-                b_ps[u] = psum.tile([P, NT], F32, name="b_ps", tag=f"b{u % 4}")
-            first_stage(b_ps[u], w2p[b][:, a, t, :].bitcast(FP4X4), w2sp[b][:, a, t, :], a, k, s, 0, NT)
-            if k == PASSES - 1:
-                if u in PINS:
-                    b_sb[g, t] = early.tile([P, NT], F32, name=f"b_pin{u}", align_bytes=64, offset=PINS.index(u) * 4096)
+        def matmul_b(u, nth):
+            g, t = divmod(u, PACK)
+            b, half = groups[g]
+            a = nth if u < B_EARLY else 1 - nth
+            if nth == 0:
+                b_ps[u] = psum.tile([P, NT], F32, name="b_ps", tag=f"b{u % RING}")
+            codes = w2_codes[b][:, a, t, :].bitcast(FP4X4)
+            first_stage(b_ps[u][:], codes, w2_planes[b][:, a, t, :], a, nth, half * NT, (half + 1) * NT)
+            if nth == PASSES - 1:
+                if u in LATE_STEPS:
+                    at = LATE_AT[LATE_STEPS.index(u)]
+                    b_sb[g, t] = late.tile([P, NT], F32, name=f"b_sb{u}", align_bytes=64, offset=at)
                 else:
-                    b_sb[g, t] = ring.tile([P, NT], F32, name="b_sb", bufs=8)
+                    b_sb[g, t] = ring.tile([P, NT], F32, name="b_sb", bufs=2 * RING)
                 nc.scalar.copy(b_sb[g, t][:], b_ps[u][:])
 
-        def matmul_x(i, k):
-            ch, t = steps[i]
-            g, c0, c1 = chunks[ch]
-            b, s = groups[g]
-            a = k if i < X_EARLY else 1 - k
-            if k == 0:
-                x_ps[i] = psum.tile([P, c1 - c0], F32, name="x_ps", tag=f"x{i % 4}")
-            cols = slice(t * P, (t + 1) * P)
-            first_stage(x_ps[i], w1_codes[b][:, a, cols].bitcast(FP8X4), w1_scales[a, b][:, cols], a, k, s, c0, c1)
+        def matmul_x(bank, nths):
+            if nths[0] == 0:
+                whole = psum.tile([P, NT], F32, name="x_ps", tag=f"x{bank % RING}")
+            for place, i in enumerate(banks[bank]):
+                ch, t = steps[i]
+                g, c0, c1 = chunks[ch]
+                b, half = groups[g]
+                if nths[0] == 0:
+                    x_ps[i] = whole[:, place * (c1 - c0) : (place + 1) * (c1 - c0)]
+                cols = slice(t * P, (t + 1) * P)
+                for nth in nths:
+                    a = nth if bank < X_EARLY else 1 - nth
+                    codes = w1_codes[b][:, a, cols].bitcast(FP8X4)
+                    first_stage(x_ps[i], codes, w1_planes[a, b][:, cols], a, nth, half * NT + c0, half * NT + c1)
 
         def horner_inner(i):
             ch, t = steps[i]
             g, c0, c1 = chunks[ch]
             inner[i] = ring.tile([P, c1 - c0], F32, name="inner", bufs=3)
-            nc.vector.scalar_tensor_tensor(
-                inner[i][:],
-                x_ps[i][:],
-                q_col[:, groups[g][0], t : t + 1],
-                b_sb[g, t][:, c0:c1],
-                MULT,
-                ADD,
-            )
+            q_t = q_col[:, groups[g][0], t : t + 1]
+            nc.vector.scalar_tensor_tensor(inner[i][:], x_ps[i], q_t, b_sb[g, t][:, c0:c1], MULT, ADD)
 
         def horner_outer(i):
             ch, t = steps[i]
             g, c0, c1 = chunks[ch]
-            fused = BIAS_ENGINE[ch] == "f"
             if t == 0:
-                h_il[ch] = keep.tile([P, c1 - c0, PACK], BF16, name=f"h_il{ch}", align_bytes=64)
-                if fused:
-                    y_sb[ch] = keep.tile([P, PACK, c1 - c0], F32, name=f"y_all{ch}")
-                else:
-                    h_planes[ch] = keep.tile([P, PACK, c1 - c0], BF16, name=f"h_planes{ch}", align_bytes=64)
-            if fused:
-                y = y_sb[ch][:, t, :]
-            else:
-                y_one = ring.tile([P, c1 - c0], F32, name="y_one", bufs=6)
-                y = y_one[:]
-            nc.vector.tensor_tensor(y, inner[i][:], x_ps[i][:], MULT)
-            bias = c_col[:, groups[g][0], t : t + 1]
-            if BIAS_ENGINE[ch] == "s":
-                nc.scalar.activation(h_planes[ch][:, t, :], y, IDENT, bias=bias)
-            elif BIAS_ENGINE[ch] == "g":
-                nc.gpsimd.tensor_scalar(h_planes[ch][:, t, :], y, 1.0, bias, MULT, ADD)
-
-        def weave(ch, piece, pieces):
-            g, c0, c1 = chunks[ch]
-            width = (c1 - c0) // pieces
-            ns = slice(piece * width, (piece + 1) * width)
-            dst = h_il[ch][:, ns, :]
-            walk_dst = dst.rearrange("p (c i) t -> p c t i", i=4)
-            if BIAS_ENGINE[ch] == "f":
-                src = y_sb[ch][:, :, ns].rearrange("p t (c i) -> p c t i", i=4)
-                bias = c_col[:, groups[g][0], :].unsqueeze(1).unsqueeze(3).to_broadcast([P, width // 4, PACK, 4])
-                nc.vector.tensor_tensor(walk_dst, src, bias, ADD)
+                h_woven[ch] = keep.tile([P, c1 - c0, PACK], BF16, name=f"h_woven{ch}", align_bytes=64)
+            if WEAVE[ch][0] == "vector":
+                if t == 0:
+                    y_chunk[ch] = keep.tile([P, PACK, c1 - c0], F32, name=f"y_chunk{ch}")
+                nc.vector.tensor_tensor(y_chunk[ch][:, t, :], inner[i][:], x_ps[i], MULT)
                 return
-            src = h_planes[ch][:, :, ns]
-            if WEAVE_ENGINE[ch] == "g":
-                nc.gpsimd.tensor_scalar(dst, src.rearrange("p t n -> p n t"), 1.0, 0.0, MULT, ADD)
+            if t == 0:
+                h_slots[ch] = keep.tile([P, PACK, c1 - c0], BF16, name=f"h_slots{ch}", align_bytes=64)
+            y = ring.tile([P, c1 - c0], F32, name="y", bufs=6)
+            nc.vector.tensor_tensor(y[:], inner[i][:], x_ps[i], MULT)
+            nc.gpsimd.tensor_scalar(h_slots[ch][:, t, :], y[:], 1.0, c_col[:, groups[g][0], t : t + 1], MULT, ADD)
+
+        def weave(ch, piece):
+            g, c0, c1 = chunks[ch]
+            engine, pieces = WEAVE[ch]
+            width = (c1 - c0) // pieces
+            cols = slice(piece * width, (piece + 1) * width)
+            dst = h_woven[ch][:, cols, :]
+            if engine == "gpsimd":
+                nc.gpsimd.tensor_scalar(dst, h_slots[ch][:, :, cols].rearrange("p t n -> p n t"), 1.0, 0.0, MULT, ADD)
+                return
+            dst_by_four = dst.rearrange("p (c i) t -> p c t i", i=4)
+            if engine == "scalar":
+                nc.scalar.copy(dst_by_four, h_slots[ch][:, :, cols].rearrange("p t (c i) -> p c t i", i=4))
             else:
-                copy = nc.vector.tensor_copy if WEAVE_ENGINE[ch] == "v" else nc.scalar.copy
-                copy(walk_dst, src.rearrange("p t (c i) -> p c t i", i=4))
+                src = y_chunk[ch][:, :, cols].rearrange("p t (c i) -> p c t i", i=4)
+                c_t = c_col[:, groups[g][0], :].unsqueeze(1).unsqueeze(3).to_broadcast([P, width // 4, PACK, 4])
+                nc.vector.tensor_tensor(dst_by_four, src, c_t, ADD)
 
         def quantize_h(ch):
             g, c0, c1 = chunks[ch]
-            codes = keep.tile([P, c1 - c0], U32, name=f"hq{ch}", align_bytes=64)
-            scales = keep.tile([P, c1 - c0], U8, name=f"hs{ch}", align_bytes=64)
+            codes = keep.tile([P, c1 - c0], U32, name=f"h_codes{ch}", align_bytes=64)
+            plane = keep.tile([P, c1 - c0], U8, name=f"h_plane{ch}", align_bytes=64)
             nc.vector.quantize_mx(
-                out=codes[:].bitcast(FP8X4), scales=scales[:], in_=h_il[ch][:].rearrange("p n t -> p (n t)")
+                out=codes[:].bitcast(FP8X4), scales=plane[:], in_=h_woven[ch][:].rearrange("p n t -> p (n t)")
             )
-            h_q[ch] = (codes, scales)
+            h_mx[ch] = (codes, plane)
 
         def second_stage(ch):
             g, c0, c1 = chunks[ch]
-            s = groups[g][1]
-            first = groups.index((0, s))
-            operands = [(h_q[first][0][:, c0:c1], h_q[first][1][:, c0:c1]), (h_q[ch][0][:], h_q[ch][1][:])]
+            half = groups[g][1]
+            first_codes, first_plane = h_mx[groups.index((0, half))]
+            operands = [(first_codes[:, c0:c1], first_plane[:, c0:c1]), (h_mx[ch][0][:], h_mx[ch][1][:])]
             accs = [psum.tile([P, c1 - c0], F32, name="o_ps", tag=f"b{2 * (ch % 2) + n}") for n in range(N // P)]
-            for b, (codes, scales) in enumerate(operands):
+            for b, (codes, plane) in enumerate(operands):
                 for n in range(N // P):
                     nc.tensor.matmul_mx(
                         out=accs[n][:],
-                        lhsT=w3c[:, b, n * P : (n + 1) * P].bitcast(FP8X4),
-                        lhsT_scale=w3s[:, b, n * P : (n + 1) * P],
+                        lhsT=w3_codes[:, b, n * P : (n + 1) * P].bitcast(FP8X4),
+                        lhsT_scale=w3_planes[:, b, n * P : (n + 1) * P],
                         rhs=codes.bitcast(FP8X4),
-                        rhs_scale=scales,
+                        rhs_scale=plane,
                         start=(b == 0),
                         stop=(b == BLOCKS - 1),
                     )
             for n in range(N // P):
                 res = keep.tile([P, c1 - c0], F32, name=f"res{ch}{n}")
-                dst = out[n * P : (n + 1) * P, s * NT + c0 : s * NT + c1]
-                if ch == len(chunks) - 1 and n == 1:
-                    nc.vector.tensor_copy(res[:], accs[n][:])
-                    nc.sync.dma_start(dst, res[:])
-                elif ch == len(chunks) - 1:
-                    nc.scalar.copy(res[:], accs[n][:])
-                    nc.scalar.dma_start(dst, res[:])
-                else:
-                    nc.scalar.copy(res[:], accs[n][:])
-                    nc.sync.dma_start(dst, res[:])
+                dst = out[n * P : (n + 1) * P, half * NT + c0 : half * NT + c1]
+                copy = nc.vector.tensor_copy if ch == last_chunk and n == 1 else nc.scalar.copy
+                queue = nc.scalar if ch == last_chunk and n == 0 else nc.sync
+                copy(res[:], accs[n][:])
+                queue.dma_start(dst, res[:])
 
-        def finish(ch):
-            quantize_h(ch)
-            if groups[chunks[ch][0]][0] == BLOCKS - 1:
-                second_stage(ch)
+        weave_at, quantize_at = {}, {}
+        for ch in reversed(range(len(chunks))):
+            engine, pieces = WEAVE[ch]
+            end = PACK * ch + PACK - 1
+            first = min(end + 1, len(steps) - 1) if engine == "vector" else end
+            for piece in range(pieces):
+                weave_at.setdefault(first + piece, []).append((ch, piece))
+            after = QUANT_AFTER_VECTOR if engine == "vector" else QUANT_AFTER_OTHERS
+            quantize_at.setdefault(min(end + after, len(steps)), []).append(ch)
 
-        for u in range(X_EARLY):
-            matmul_x(u, 0)
+        for bank in range(X_EARLY):
+            matmul_x(bank, (0,))
         for u in range(B_EARLY):
             matmul_b(u, 0)
         for u in range(B_LEAD):
-            for k in range(1 if u < B_EARLY else 0, PASSES):
-                matmul_b(u, k)
+            for nth in range(1 if u < B_EARLY else 0, PASSES):
+                matmul_b(u, nth)
             if u < X_LEAD:
-                for k in range(1 if u < X_EARLY else 0, PASSES):
-                    matmul_x(u, k)
+                matmul_x(u, (1,) if u < X_EARLY else (0, 1))
         horner_inner(0)
-        for i in range(len(steps) + 2):
-            for a in range(PASSES):
-                if i + X_LEAD < len(steps):
-                    matmul_x(i + X_LEAD, a)
-            for a in range(PASSES):
-                if i + B_LEAD < len(units):
-                    matmul_b(i + B_LEAD, a)
-            for k in CAST_AT.get(i, ()):
-                cast(k // 2, 1, (k % 2) * 64, (k % 2) * 64 + 64, CAST_ENGINE[k])
-            for a in W1Q_AT.get(i, ()):
-                quantize_w1(1, a)
+        for i in range(len(steps) + 1):
+            if i + X_LEAD < len(banks):
+                matmul_x(i + X_LEAD, (0, 1))
+            if i + B_LEAD < len(groups) * PACK:
+                for nth in range(PASSES):
+                    matmul_b(i + B_LEAD, nth)
+            if i < 2 * PASSES:
+                cast_w1(i // 2, 1, (i % 2) * (P // 2), (i % 2 + 1) * (P // 2))
+            if i in (2, 4):
+                quantize_w1(i // 2 - 1, 1)
             if i + 1 < len(steps):
                 horner_inner(i + 1)
-            for ch in QUANT_AT.get(i, ()):
-                finish(ch)
+            for ch in quantize_at.get(i, ()):
+                quantize_h(ch)
+                if groups[chunks[ch][0]][0] == BLOCKS - 1:
+                    second_stage(ch)
             if i < len(steps):
                 horner_outer(i)
-            for ch, piece, pieces in WEAVE_AT.get(i, ()):
-                weave(ch, piece, pieces)
+            for ch, piece in weave_at.get(i, ()):
+                weave(ch, piece)

@@ -38,7 +38,8 @@ X_EARLY = 2
 MOVES_FIRST = 6
 
 ROOM = 8192
-W2_WORDS_AT = (0, 12288)
+W2_WORDS_AT = (0, 4096)
+W2_RAW_AT = 20480
 SCALE_WINDOW_AT = 1984
 W1_SCALES_AT = 3072
 TABLE1_AT = 3968
@@ -67,9 +68,10 @@ def tile_list_seawater_horner_surrogate_kernel(
         q_col = keep.tile([P, BLOCKS, PACK], F32, name="q_col")
         c_col = keep.tile([P, BLOCKS, PACK], F32, name="c_col")
         nc.sync.dma_start(q_col[:], quad.rearrange("(b p t) -> p b t", p=P, t=PACK))
-        w2_raw = keep.tile([P, PASSES, H // 2], I32, name="w2_raw", align_bytes=64)
+        w2_by_block = w2_words.bitcast(I32).rearrange("a p (b c) -> b p a c", b=BLOCKS)
+        w2_raw = [shared.tile([P, PASSES, KP // 2], I32, name="w2_raw0", align_bytes=64, offset=W2_RAW_AT)]
         for a in range(PASSES):
-            nc.sync.dma_start(w2_raw[:, a, :], w2_words[a].bitcast(I32))
+            nc.sync.dma_start(w2_raw[0][:, a, :], w2_by_block[0, :, a])
 
         scale_window = shared.tile([P, T], U8, name="scale_window", align_bytes=64, offset=SCALE_WINDOW_AT)
         nc.vector.memset(scale_window[:].bitcast(I32), 0)
@@ -144,7 +146,7 @@ def tile_list_seawater_horner_surrogate_kernel(
 
         def order_w2_words(b):
             words = shared.tile([P, PASSES, PACK, 2 * P], U8, name=f"w2_codes{b}", align_bytes=64, offset=W2_WORDS_AT[b])
-            src = w2_raw[:].bitcast(U16)[:, :, b * KP : (b + 1) * KP]
+            src = w2_raw[b][:].bitcast(U16)
             nc.vector.tensor_copy(words[:].bitcast(U16), src.rearrange("p a (m t) -> p a t m", t=PACK))
             w2_codes.append(words)
 
@@ -162,19 +164,21 @@ def tile_list_seawater_horner_surrogate_kernel(
             nc.vector.tensor_copy(got.bitcast(U32), table[a][:].bitcast(U32).indirect(lists))
 
         order_w2_words(0)
+        w2_raw.append(shared.tile([P, PASSES, KP // 2], I32, name="w2_raw1", align_bytes=64, offset=W2_RAW_AT))
+        nc.sync.dma_start(w2_raw[1][:], w2_by_block[1])
         gather_words(0, 0)
         gather_words(0, 1)
         load_w1(0, 1, 0)
         cast_w1(0, 0, 0, P)
         quantize_w1(0, 0)
         order_w2_scales(0)
-        order_w2_words(1)
         order_w2_scales(1)
         cast_w1(1, 0, 0, P)
         load_w1(1, 1, 1)
         gather_words(1, 0)
         quantize_w1(1, 0)
         gather_words(1, 1)
+        order_w2_words(1)
         w3_codes = shared.tile([P, PASSES, N], I32, name="w3_codes", align_bytes=64, offset=W3_AT)
         nc.sync.dma_start(w3_codes[:], w3_words.rearrange("a p c i -> p a (c i)").bitcast(I32))
 
@@ -188,6 +192,7 @@ def tile_list_seawater_horner_surrogate_kernel(
             if t % (NT // (chunks[ch][2] - chunks[ch][1])) == 0:
                 banks.append([])
             banks[-1].append(i)
+        x_bank = {}
         b_ps, b_sb, x_ps, inner, y_chunk, h_slots, h_woven, h_mx = {}, {}, {}, {}, {}, {}, {}, {}
 
         def first_stage(acc, codes, plane, a, nth, c0, c1):
@@ -226,6 +231,7 @@ def tile_list_seawater_horner_surrogate_kernel(
                 b, half = groups[g]
                 if nths[0] == 0:
                     x_ps[i] = whole[:, place * (c1 - c0) : (place + 1) * (c1 - c0)]
+                    x_bank[i] = whole[:]
                 cols = slice(t * P, (t + 1) * P)
                 for nth in nths:
                     a = nth if bank < X_EARLY else 1 - nth
@@ -235,7 +241,12 @@ def tile_list_seawater_horner_surrogate_kernel(
         def horner_inner(i):
             ch, t = steps[i]
             g, c0, c1 = chunks[ch]
-            inner[i] = ring.tile([P, c1 - c0], F32, name="inner", bufs=3)
+            if WEAVE[ch][0] == "vector":
+                if t == 0:
+                    inner[ch, "all"] = keep.tile([P, NT], F32, name=f"inner{ch}")
+                inner[i] = inner[ch, "all"][:, t * (c1 - c0) : (t + 1) * (c1 - c0)]
+            else:
+                inner[i] = ring.tile([P, c1 - c0], F32, name="inner", bufs=3)
             q_t = q_col[:, groups[g][0], t : t + 1]
             nc.vector.scalar_tensor_tensor(inner[i][:], x_ps[i], q_t, b_sb[g, t][:, c0:c1], MULT, ADD)
 
@@ -245,9 +256,9 @@ def tile_list_seawater_horner_surrogate_kernel(
             if t == 0:
                 h_woven[ch] = keep.tile([P, c1 - c0, PACK], BF16, name=f"h_woven{ch}", align_bytes=64)
             if WEAVE[ch][0] == "vector":
-                if t == 0:
+                if t == PACK - 1:
                     y_chunk[ch] = keep.tile([P, PACK, c1 - c0], F32, name=f"y_chunk{ch}")
-                nc.vector.tensor_tensor(y_chunk[ch][:, t, :], inner[i][:], x_ps[i], MULT)
+                    nc.vector.tensor_tensor(y_chunk[ch][:].rearrange("p t n -> p (t n)"), inner[ch, "all"][:], x_bank[i], MULT)
                 return
             if t == 0:
                 h_slots[ch] = keep.tile([P, PACK, c1 - c0], BF16, name=f"h_slots{ch}", align_bytes=64)
@@ -336,12 +347,12 @@ def tile_list_seawater_horner_surrogate_kernel(
                 cast_w1(i // 2, 1, (i % 2) * (P // 2), (i % 2 + 1) * (P // 2))
             if i in (2, 4):
                 quantize_w1(i // 2 - 1, 1)
-            if i + 1 < len(steps):
-                horner_inner(i + 1)
             for ch in quantize_at.get(i, ()):
                 quantize_h(ch)
                 if groups[chunks[ch][0]][0] == BLOCKS - 1:
                     second_stage(ch)
+            if i + 1 < len(steps):
+                horner_inner(i + 1)
             if i < len(steps):
                 horner_outer(i)
             for ch, piece in weave_at.get(i, ()):

@@ -33,21 +33,21 @@ QUANT_AFTER_OTHERS = 7
 QUANT_AFTER_VECTOR = 3
 B_LEAD = 4
 X_LEAD = 3
-B_EARLY = 3
 X_EARLY = 2
-MOVES_FIRST = 6
+B_FIRST = 3
+W1_CAST_STEPS = (1, 2, 3, 4)
+W1_QUANT_STEPS = (4, 6)
 
 ROOM = 8192
-W2_WORDS_AT = (0, 4096)
-W2_RAW_AT = 20480
 SCALE_WINDOW_AT = 1984
 W1_SCALES_AT = 3072
-TABLE1_AT = 3968
-W3_AT = 8192
-W1_BF16_AT = (12288, 16384)
-W2_SCALES_AT = (14336, 15360)
-LATE_AT = (0, 4096)
-LATE_STEPS = (0, 2)
+TABLE1_AT = 4096
+W1_BF16_AT = 12288
+W1_PAIRS_AT = (16384, 18432)
+W2_RAW_AT = (20480, 6144)
+W2_WORDS_AT = (0, W1_PAIRS_AT[1])
+W2_SCALES_AT = (4096, W1_PAIRS_AT[0], 5120)
+W3_AT = W1_BF16_AT
 
 
 def tile_list_seawater_horner_surrogate_kernel(
@@ -57,7 +57,6 @@ def tile_list_seawater_horner_surrogate_kernel(
     with ExitStack() as ctx:
         keep = ctx.enter_context(tc.tile_pool(name="keep", bufs=1))
         ring = ctx.enter_context(tc.tile_pool(name="ring", bufs=2))
-        late = ctx.enter_context(tc.tile_pool(name="late", bufs=1))
         rooms = ctx.enter_context(tc.tile_pool(name="rooms", bufs=1))
         shared = ctx.enter_context(tc.tile_pool(name="shared", bufs=1))
         psum = ctx.enter_context(tc.psum_pool(name="psum", bufs=1))
@@ -65,18 +64,24 @@ def tile_list_seawater_horner_surrogate_kernel(
         offsets = keep.tile([P, S // 16], U16, name="offsets")
         nc.sync.dma_start(offsets[:], offs)
 
+        warm = keep.tile([P, 2], F32, name="warm")
+        nc.gpsimd.memset(warm[:, 0:1], 0.0)
+        nc.scalar.copy(warm[:, 1:2], warm[:, 0:1])
+
         q_col = keep.tile([P, BLOCKS, PACK], F32, name="q_col")
         c_col = keep.tile([P, BLOCKS, PACK], F32, name="c_col")
         nc.sync.dma_start(q_col[:], quad.rearrange("(b p t) -> p b t", p=P, t=PACK))
         w2_by_block = w2_words.bitcast(I32).rearrange("a p (b c) -> b p a c", b=BLOCKS)
-        w2_raw = [shared.tile([P, PASSES, KP // 2], I32, name="w2_raw0", align_bytes=64, offset=W2_RAW_AT)]
-        for a in range(PASSES):
-            nc.sync.dma_start(w2_raw[0][:, a, :], w2_by_block[0, :, a])
+        w2_raw = [shared.tile([P, PASSES, KP // 2], I32, name="w2_raw0", align_bytes=64, offset=W2_RAW_AT[0])]
+        nc.sync.dma_start(c_col[:], cons.rearrange("(b p t) -> p b t", p=P, t=PACK))
+        nc.sync.dma_start(w2_raw[0][:], w2_by_block[0])
 
         scale_window = shared.tile([P, T], U8, name="scale_window", align_bytes=64, offset=SCALE_WINDOW_AT)
         nc.vector.memset(scale_window[:].bitcast(I32), 0)
-        for a in range(PASSES):
-            nc.sync.dma_start(scale_window[4 * a : P : 8, :].bitcast(I32), tab_scales[a].bitcast(I32))
+        scale_rows = tab_scales.bitcast(I32)
+        for e in range(2):
+            nc.sync.dma_start(scale_window[e:P:16, :].bitcast(I32), scale_rows[0, e::2])
+        nc.sync.dma_start(scale_window[4:P:8, :].bitcast(I32), scale_rows[1])
 
         def load_planes(name, src, width):
             planes = keep.tile([P, PASSES, width], U8, name=name, align_bytes=64)
@@ -89,7 +94,6 @@ def tile_list_seawater_horner_surrogate_kernel(
             return planes
 
         w2_planes_raw = load_planes("w2_planes_raw", w2_scales, H)
-        nc.gpsimd.dma_start(c_col[:], cons.rearrange("(b p t) -> p b t", p=P, t=PACK))
         w3_planes = load_planes("w3_planes", w3_scales, N)
 
         def load_table(a, pool, at):
@@ -105,7 +109,7 @@ def tile_list_seawater_horner_surrogate_kernel(
             nc.sync.dma_start(raw[:], rows.rearrange("(p j) c -> p j c", j=PACK))
             w1_raw[a, b] = raw
 
-        table = [load_table(0, rooms, 0)]
+        table = [load_table(0, rooms, 0), load_table(1, shared, TABLE1_AT)]
         load_w1(0, 0, 2)
         load_w1(1, 0, 1)
 
@@ -113,10 +117,7 @@ def tile_list_seawater_horner_surrogate_kernel(
         w1_planes = {(0, 0): shared.tile([P, KP], U8, name="w1_plane00", align_bytes=64, offset=W1_SCALES_AT)}
         for a, b in ((1, 0), (0, 1), (1, 1)):
             w1_planes[a, b] = keep.tile([P, KP], U8, name=f"w1_plane{a}{b}", align_bytes=64)
-        w1_bf16 = {}
-        for a in range(PASSES):
-            w1_bf16[a, 0] = shared.tile([P, PACK * KP], BF16, name=f"w1_bf{a}0", align_bytes=64, offset=W1_BF16_AT[a])
-            w1_bf16[a, 1] = late.tile([P, PACK * KP], BF16, name=f"w1_bf{a}1", align_bytes=64, offset=LATE_AT[a])
+        w1_bf16 = {(0, 0): shared.tile([P, PACK * KP], BF16, name="w1_bf00", align_bytes=64, offset=W1_BF16_AT)}
 
         def cast_w1(a, b, m0, m1):
             dst = w1_bf16[a, b][:].rearrange("p (t m j) -> p m j t", t=PACK, j=PACK)[:, m0:m1]
@@ -129,20 +130,17 @@ def tile_list_seawater_horner_surrogate_kernel(
             )
 
         scales_got = keep.tile([P, S], U8, name="scales_got", align_bytes=64)
-        nc.vector.tensor_copy(scales_got[:], scale_window[:].indirect(offsets[:]))
         v_planes = [keep.tile([P, S], U8, name=f"v_plane{a}", align_bytes=64) for a in range(PASSES)]
-        for a in range(PASSES):
-            nc.vector.memset(v_planes[a][:].bitcast(I32), 0)
-        for move in range(PASSES * QUADRANTS):
-            a, d = divmod(move, QUADRANTS)
-            if move == MOVES_FIRST:
-                table.append(load_table(1, shared, TABLE1_AT))
-            nc.sync.dma_start(
-                v_planes[a][32 * d : 32 * d + 4, :].bitcast(I32),
-                scales_got[32 * d + 4 * a : 32 * d + 32 : 8, :].bitcast(I32),
-            )
+        nc.vector.memset(v_planes[1][:].bitcast(I32), 0)
+        nc.vector.tensor_copy(scales_got[:], scale_window[:].indirect(offsets[:]))
+        nc.vector.tensor_copy(v_planes[0][:].bitcast(I32), scales_got[:].bitcast(I32))
+        got, planes = scales_got[:].bitcast(I32), [plane[:].bitcast(I32) for plane in v_planes]
+        for e in range(2):
+            nc.scalar.dma_start(planes[0][2 + e : P : 32], got[16 + e : P : 32])
+        for d in range(QUADRANTS):
+            nc.scalar.dma_start(planes[1][32 * d : 32 * d + 4], got[32 * d + 4 : 32 * d + 32 : 8])
 
-        w2_codes, w2_planes = [], []
+        w2_codes, w2_planes = [], {}
 
         def order_w2_words(b):
             words = shared.tile([P, PASSES, PACK, 2 * P], U8, name=f"w2_codes{b}", align_bytes=64, offset=W2_WORDS_AT[b])
@@ -150,34 +148,44 @@ def tile_list_seawater_horner_surrogate_kernel(
             nc.vector.tensor_copy(words[:].bitcast(U16), src.rearrange("p a (m t) -> p a t m", t=PACK))
             w2_codes.append(words)
 
-        def order_w2_scales(b):
-            planes = shared.tile([P, PASSES, PACK, P], U8, name=f"w2_planes{b}", align_bytes=64, offset=W2_SCALES_AT[b])
-            src = w2_planes_raw[:, :, b * KP : (b + 1) * KP]
-            nc.vector.tensor_copy(planes[:], src.rearrange("p a (m t) -> p a t m", t=PACK))
-            w2_planes.append(planes)
+        def order_w2_scales(b, t0, t1, at):
+            planes = shared.tile([P, PASSES, t1 - t0, P], U8, name=f"w2_planes{b}{t0}", align_bytes=64, offset=at)
+            src = w2_planes_raw[:, :, b * KP : (b + 1) * KP].rearrange("p a (m t) -> p a t m", t=PACK)
+            nc.vector.tensor_copy(planes[:], src[:, :, t0:t1])
+            for t in range(t0, t1):
+                w2_planes[b, t] = planes[:, :, t - t0, :]
 
-        v_codes = [keep.tile([P, S], I32, name=f"v_codes{a}", align_bytes=64) for a in range(PASSES)]
+        v_codes = {}
 
         def gather_words(a, half):
             lists = offsets[:, half * (NT // 16) : (half + 1) * (NT // 16)]
-            got = v_codes[a][:, half * NT : (half + 1) * NT]
-            nc.vector.tensor_copy(got.bitcast(U32), table[a][:].bitcast(U32).indirect(lists))
+            v_codes[a, half] = keep.tile([P, NT], I32, name=f"v_codes{a}{half}", align_bytes=64)
+            nc.vector.tensor_copy(v_codes[a, half][:].bitcast(U32), table[a][:].bitcast(U32).indirect(lists))
 
         order_w2_words(0)
-        w2_raw.append(shared.tile([P, PASSES, KP // 2], I32, name="w2_raw1", align_bytes=64, offset=W2_RAW_AT))
-        nc.sync.dma_start(w2_raw[1][:], w2_by_block[1])
         gather_words(0, 0)
         gather_words(0, 1)
         load_w1(0, 1, 0)
-        cast_w1(0, 0, 0, P)
-        quantize_w1(0, 0)
-        order_w2_scales(0)
-        order_w2_scales(1)
-        cast_w1(1, 0, 0, P)
-        load_w1(1, 1, 1)
         gather_words(1, 0)
-        quantize_w1(1, 0)
         gather_words(1, 1)
+        order_w2_scales(0, 0, B_FIRST, W2_SCALES_AT[0])
+        order_w2_scales(1, 0, PACK, W2_SCALES_AT[2])
+        w2_raw.append(shared.tile([P, PASSES, KP // 2], I32, name="w2_raw1", align_bytes=64, offset=W2_RAW_AT[1]))
+        nc.sync.dma_start(w2_raw[1][:], w2_by_block[1])
+        cast_w1(0, 0, 0, P)
+        load_w1(1, 1, 2)
+        quantize_w1(0, 0)
+        pairs = []
+        for pair, copy in enumerate((nc.vector.tensor_copy, nc.scalar.copy)):
+            pairs.append(shared.tile([P, 2 * KP], BF16, name=f"w1_pair{pair}", align_bytes=64, offset=W1_PAIRS_AT[pair]))
+            dst = pairs[pair][:].rearrange("p (t m j) -> p m j t", t=2, j=PACK)
+            copy(dst, w1_raw[1, 0][:].rearrange("p j (m t) -> p m j t", t=PACK)[:, :, :, 2 * pair : 2 * pair + 2])
+        for pair in range(2):
+            cols = slice(pair * 2 * P, (pair + 1) * 2 * P)
+            nc.vector.quantize_mx(
+                out=w1_codes[0][:, 1, cols].bitcast(FP8X4), scales=w1_planes[1, 0][:, cols], in_=pairs[pair][:]
+            )
+        order_w2_scales(0, B_FIRST, PACK, W2_SCALES_AT[1])
         order_w2_words(1)
         w3_codes = shared.tile([P, PASSES, N], I32, name="w3_codes", align_bytes=64, offset=W3_AT)
         nc.sync.dma_start(w3_codes[:], w3_words.rearrange("a p c i -> p a (c i)").bitcast(I32))
@@ -200,7 +208,7 @@ def tile_list_seawater_horner_surrogate_kernel(
                 out=acc,
                 lhsT=codes,
                 lhsT_scale=plane,
-                rhs=v_codes[a][:, c0:c1].bitcast(FP8X4),
+                rhs=v_codes[a, c0 // NT][:, c0 % NT : c0 % NT + c1 - c0].bitcast(FP8X4),
                 rhs_scale=v_planes[a][:, c0:c1],
                 start=(nth == 0),
                 stop=(nth == PASSES - 1),
@@ -209,15 +217,14 @@ def tile_list_seawater_horner_surrogate_kernel(
         def matmul_b(u, nth):
             g, t = divmod(u, PACK)
             b, half = groups[g]
-            a = nth if u < B_EARLY else 1 - nth
+            a = nth
             if nth == 0:
                 b_ps[u] = psum.tile([P, NT], F32, name="b_ps", tag=f"b{u % RING}")
             codes = w2_codes[b][:, a, t, :].bitcast(FP4X4)
-            first_stage(b_ps[u][:], codes, w2_planes[b][:, a, t, :], a, nth, half * NT, (half + 1) * NT)
+            first_stage(b_ps[u][:], codes, w2_planes[b, t][:, a, :], a, nth, half * NT, (half + 1) * NT)
             if nth == PASSES - 1:
-                if u in LATE_STEPS:
-                    at = LATE_AT[LATE_STEPS.index(u)]
-                    b_sb[g, t] = late.tile([P, NT], F32, name=f"b_sb{u}", align_bytes=64, offset=at)
+                if u < PACK:
+                    b_sb[g, t] = rooms.tile([P, NT], F32, name=f"b_sb{u}", align_bytes=64, offset=ROOM + u * ROOM // PACK)
                 else:
                     b_sb[g, t] = ring.tile([P, NT], F32, name="b_sb", bufs=2 * RING)
                 nc.scalar.copy(b_sb[g, t][:], b_ps[u][:])
@@ -327,26 +334,35 @@ def tile_list_seawater_horner_surrogate_kernel(
             after = QUANT_AFTER_VECTOR if engine == "vector" else QUANT_AFTER_OTHERS
             quantize_at.setdefault(min(end + after, len(steps)), []).append(ch)
 
-        for bank in range(X_EARLY):
-            matmul_x(bank, (0,))
-        for u in range(B_EARLY):
-            matmul_b(u, 0)
-        for u in range(B_LEAD):
-            for nth in range(1 if u < B_EARLY else 0, PASSES):
+        for u in range(B_FIRST):
+            for nth in range(PASSES):
                 matmul_b(u, nth)
-            if u < X_LEAD:
-                matmul_x(u, (1,) if u < X_EARLY else (0, 1))
+        for nth in range(PASSES):
+            for bank in range(X_EARLY):
+                matmul_x(bank, (nth,))
+        for bank in range(X_EARLY, X_LEAD):
+            matmul_x(bank, (0, 1))
+        for u in range(B_FIRST, B_LEAD):
+            for nth in range(PASSES):
+                matmul_b(u, nth)
+        filled = X_LEAD
         horner_inner(0)
         for i in range(len(steps) + 1):
-            if i + X_LEAD < len(banks):
-                matmul_x(i + X_LEAD, (0, 1))
+            if i in W1_CAST_STEPS:
+                a, half = divmod(W1_CAST_STEPS.index(i), 2)
+                if half == 0:
+                    at = ROOM + a * ROOM // 2
+                    w1_bf16[a, 1] = rooms.tile([P, PACK * KP], BF16, name=f"w1_bf{a}1", align_bytes=64, offset=at)
+                cast_w1(a, 1, half * (P // 2), (half + 1) * (P // 2))
+            if i in W1_QUANT_STEPS:
+                quantize_w1(W1_QUANT_STEPS.index(i), 1)
+            ahead = i + X_LEAD + 1 if i >= W1_QUANT_STEPS[-1] else min(i + X_LEAD + 1, HALVES * PACK)
+            while filled < min(ahead, len(banks)):
+                matmul_x(filled, (0, 1))
+                filled = filled + 1
             if i + B_LEAD < len(groups) * PACK:
                 for nth in range(PASSES):
                     matmul_b(i + B_LEAD, nth)
-            if i < 2 * PASSES:
-                cast_w1(i // 2, 1, (i % 2) * (P // 2), (i % 2 + 1) * (P // 2))
-            if i in (2, 4):
-                quantize_w1(i // 2 - 1, 1)
             for ch in quantize_at.get(i, ()):
                 quantize_h(ch)
                 if groups[chunks[ch][0]][0] == BLOCKS - 1:

@@ -28,13 +28,13 @@ QUADRANTS = P // 32
 RING = 4
 
 LAST_CHUNKS = ((0, 256), (256, 384), (384, 512))
-WEAVE = (("gpsimd", 4), ("scalar", 2), ("scalar", 2), ("scalar", 1), ("vector", 1), ("vector", 1))
+WEAVE = (("scalar", 2), ("scalar", 2), ("scalar", 2), ("scalar", 1), ("vector", 1), ("vector", 1))
 QUANT_AFTER_OTHERS = 7
 QUANT_AFTER_VECTOR = 3
 B_LEAD = 4
 X_LEAD = 3
-X_EARLY = 2
-B_FIRST = 3
+X_EARLY = 1
+B_FIRST = 2
 W1_CAST_STEPS = (1, 2, 3, 4)
 W1_QUANT_STEPS = (4, 6)
 
@@ -45,7 +45,7 @@ TABLE1_AT = 4096
 W1_BF16_AT = 12288
 W1_PAIRS_AT = (16384, 18432)
 W2_RAW_AT = (20480, 6144)
-W2_WORDS_AT = (0, W1_PAIRS_AT[1])
+W2_WORDS_AT = (0, 22528)
 W2_SCALES_AT = (4096, W1_PAIRS_AT[0], 5120)
 W3_AT = W1_BF16_AT
 
@@ -186,7 +186,6 @@ def tile_list_seawater_horner_surrogate_kernel(
                 out=w1_codes[0][:, 1, cols].bitcast(FP8X4), scales=w1_planes[1, 0][:, cols], in_=pairs[pair][:]
             )
         order_w2_scales(0, B_FIRST, PACK, W2_SCALES_AT[1])
-        order_w2_words(1)
         w3_codes = shared.tile([P, PASSES, N], I32, name="w3_codes", align_bytes=64, offset=W3_AT)
         nc.sync.dma_start(w3_codes[:], w3_words.rearrange("a p c i -> p a (c i)").bitcast(I32))
 
@@ -252,6 +251,8 @@ def tile_list_seawater_horner_surrogate_kernel(
                 if t == 0:
                     inner[ch, "all"] = keep.tile([P, NT], F32, name=f"inner{ch}")
                 inner[i] = inner[ch, "all"][:, t * (c1 - c0) : (t + 1) * (c1 - c0)]
+            elif i == 0:
+                inner[i] = shared.tile([P, c1 - c0], F32, name="inner_first", align_bytes=64, offset=W2_WORDS_AT[1])
             else:
                 inner[i] = ring.tile([P, c1 - c0], F32, name="inner", bufs=3)
             q_t = q_col[:, groups[g][0], t : t + 1]
@@ -279,9 +280,6 @@ def tile_list_seawater_horner_surrogate_kernel(
             width = (c1 - c0) // pieces
             cols = slice(piece * width, (piece + 1) * width)
             dst = h_woven[ch][:, cols, :]
-            if engine == "gpsimd":
-                nc.gpsimd.tensor_scalar(dst, h_slots[ch][:, :, cols].rearrange("p t n -> p n t"), 1.0, 0.0, MULT, ADD)
-                return
             dst_by_four = dst.rearrange("p (c i) t -> p c t i", i=4)
             if engine == "scalar":
                 nc.scalar.copy(dst_by_four, h_slots[ch][:, :, cols].rearrange("p t (c i) -> p c t i", i=4))
@@ -328,7 +326,7 @@ def tile_list_seawater_horner_surrogate_kernel(
         for ch in reversed(range(len(chunks))):
             engine, pieces = WEAVE[ch]
             end = PACK * ch + PACK - 1
-            first = min(end + 1, len(steps) - 1) if engine == "vector" else end
+            first = min(end + 1, len(steps) - 1) if engine == "vector" else max(end, W1_CAST_STEPS[-1] + 1)
             for piece in range(pieces):
                 weave_at.setdefault(first + piece, []).append((ch, piece))
             after = QUANT_AFTER_VECTOR if engine == "vector" else QUANT_AFTER_OTHERS
@@ -340,14 +338,17 @@ def tile_list_seawater_horner_surrogate_kernel(
         for nth in range(PASSES):
             for bank in range(X_EARLY):
                 matmul_x(bank, (nth,))
-        for bank in range(X_EARLY, X_LEAD):
-            matmul_x(bank, (0, 1))
-        for u in range(B_FIRST, B_LEAD):
-            for nth in range(PASSES):
-                matmul_b(u, nth)
+        for u in range(X_EARLY, B_LEAD):
+            if u >= B_FIRST:
+                for nth in range(PASSES):
+                    matmul_b(u, nth)
+            if u < X_LEAD:
+                matmul_x(u, (0, 1))
         filled = X_LEAD
         horner_inner(0)
         for i in range(len(steps) + 1):
+            if i == 1:
+                order_w2_words(1)
             if i in W1_CAST_STEPS:
                 a, half = divmod(W1_CAST_STEPS.index(i), 2)
                 if half == 0:

@@ -15,7 +15,6 @@ FP8X4 = mybir.dt.float8_e4m3fn_x4
 FP4X4 = mybir.dt.float4_e2m1fn_x4
 MULT = mybir.AluOpType.mult
 ADD = mybir.AluOpType.add
-IDENTITY = mybir.ActivationFunctionType.Identity
 
 P = 128
 PACK = 4
@@ -27,27 +26,25 @@ HALVES = S // NT
 QUADRANTS = P // 32
 RING = 4
 
+PAIRS = PACK // 2
+
 LAST_CHUNKS = ((0, 256), (256, 384), (384, 512))
-WEAVE = (("scalar", 2), ("scalar", 2), ("scalar", 2), ("scalar", 1), ("vector", 1), ("vector", 1))
-QUANT_AFTER_OTHERS = 7
-QUANT_AFTER_VECTOR = 3
-B_LEAD = 4
-X_LEAD = 3
-X_EARLY = 1
-B_FIRST = 2
-W1_CAST_STEPS = (1, 2, 3, 4)
+NARROW = 128
+LEAD = 4
+GPSIMD_CAST_PIECES = 4
+W1_CAST_STEPS = (2, 3)
+W2_ORDER_STEP = 2
 W1_QUANT_STEPS = (4, 6)
+WEAVE_STEPS = ((6, 7), (8, 9), (11, 12), (15,), (20,), (23,))
+H_QUANT_STEPS = (11, 14, 18, 22, 22, 24)
 
 ROOM = 8192
-SCALE_WINDOW_AT = 1984
-W1_SCALES_AT = 3072
-TABLE1_AT = 4096
-W1_BF16_AT = 12288
-W1_PAIRS_AT = (16384, 18432)
-W2_RAW_AT = (20480, 6144)
-W2_WORDS_AT = (0, 22528)
-W2_SCALES_AT = (4096, W1_PAIRS_AT[0], 5120)
-W3_AT = W1_BF16_AT
+TABLE0_AT = 6144
+LATE_AT = {"w1_01": 0, "w2_raw1": 8192, "w3": 10240, "w1_11": 12288}
+W1_EARLY_AT = (20480, 28672)
+B_FIRST_AT = (20480, 22528, 28672, 30720)
+TABLE1_AT = 36864
+W2_PLANES1_AT = TABLE1_AT
 
 
 def tile_list_seawater_horner_surrogate_kernel(
@@ -57,103 +54,65 @@ def tile_list_seawater_horner_surrogate_kernel(
     with ExitStack() as ctx:
         keep = ctx.enter_context(tc.tile_pool(name="keep", bufs=1))
         ring = ctx.enter_context(tc.tile_pool(name="ring", bufs=2))
-        rooms = ctx.enter_context(tc.tile_pool(name="rooms", bufs=1))
-        shared = ctx.enter_context(tc.tile_pool(name="shared", bufs=1))
+        placed = ctx.enter_context(tc.tile_pool(name="placed", bufs=1))
         psum = ctx.enter_context(tc.psum_pool(name="psum", bufs=1))
 
         offsets = keep.tile([P, S // 16], U16, name="offsets")
         nc.sync.dma_start(offsets[:], offs)
 
-        warm = keep.tile([P, 2], F32, name="warm")
-        nc.gpsimd.memset(warm[:, 0:1], 0.0)
-        nc.scalar.copy(warm[:, 1:2], warm[:, 0:1])
-
         q_col = keep.tile([P, BLOCKS, PACK], F32, name="q_col")
         c_col = keep.tile([P, BLOCKS, PACK], F32, name="c_col")
-        nc.sync.dma_start(q_col[:], quad.rearrange("(b p t) -> p b t", p=P, t=PACK))
         w2_by_block = w2_words.bitcast(I32).rearrange("a p (b c) -> b p a c", b=BLOCKS)
-        w2_raw = [shared.tile([P, PASSES, KP // 2], I32, name="w2_raw0", align_bytes=64, offset=W2_RAW_AT[0])]
-        nc.sync.dma_start(c_col[:], cons.rearrange("(b p t) -> p b t", p=P, t=PACK))
+        w2_raw = [keep.tile([P, PASSES, KP // 2], I32, name="w2_raw0", align_bytes=64)]
+        nc.sync.dma_start(q_col[:], quad.rearrange("(b p t) -> p b t", p=P, t=PACK))
         nc.sync.dma_start(w2_raw[0][:], w2_by_block[0])
+        nc.sync.dma_start(c_col[:], cons.rearrange("(b p t) -> p b t", p=P, t=PACK))
 
-        scale_window = shared.tile([P, T], U8, name="scale_window", align_bytes=64, offset=SCALE_WINDOW_AT)
+        scale_window = keep.tile([P, T], U8, name="scale_window", align_bytes=64)
+        weight_rows = keep.tile([P, PASSES, H], U8, name="weight_rows", align_bytes=64)
+        v_planes = keep.tile([P, PASSES, S], U8, name="v_planes", align_bytes=64)
         nc.vector.memset(scale_window[:].bitcast(I32), 0)
-        scale_rows = tab_scales.bitcast(I32)
-        for e in range(2):
-            nc.sync.dma_start(scale_window[e:P:16, :].bitcast(I32), scale_rows[0, e::2])
-        nc.sync.dma_start(scale_window[4:P:8, :].bitcast(I32), scale_rows[1])
+        nc.sync.dma_start(scale_window[0:P:4, :].bitcast(I32), tab_scales.bitcast(I32).rearrange("a q t -> q a t"))
+        nc.vector.memset(weight_rows[:].rearrange("p a c -> p (a c)").bitcast(I32), 0)
+        nc.vector.memset(v_planes[:].rearrange("p a c -> p (a c)").bitcast(I32), 0)
 
-        def load_planes(name, src, width):
-            planes = keep.tile([P, PASSES, width], U8, name=name, align_bytes=64)
-            nc.vector.memset(planes[:].rearrange("p a c -> p (a c)").bitcast(I32), 0)
+        def load_rows(src, width):
             for d in range(QUADRANTS):
-                nc.gpsimd.dma_start(
-                    planes[32 * d : 32 * d + 4, :, :].bitcast(I32),
+                nc.sync.dma_start(
+                    weight_rows[32 * d : 32 * d + 4, :, 0:width].bitcast(I32),
                     src[:, 4 * d : 4 * d + 4, :].rearrange("a r c -> r a c").bitcast(I32),
                 )
-            return planes
 
-        w2_planes_raw = load_planes("w2_planes_raw", w2_scales, H)
-        w3_planes = load_planes("w3_planes", w3_scales, N)
-
-        def load_table(a, pool, at):
-            window = pool.tile([P, T], I32, name=f"table{a}", align_bytes=64, offset=at)
+        def load_table(a, at):
+            window = placed.tile([P, T], I32, name=f"table{a}", align_bytes=64, offset=at)
             nc.sync.dma_start(window[:], tab_words[a].rearrange("p t i -> p (t i)").bitcast(I32))
             return window
 
         w1_raw = {}
 
-        def load_w1(a, b, room):
-            raw = rooms.tile([P, PACK, KP], F32, name=f"w1_raw{a}{b}", align_bytes=64, offset=room * ROOM)
+        def load_w1(a, b, at):
+            raw = placed.tile([P, PACK, KP], F32, name=f"w1_raw{a}{b}", align_bytes=64, offset=at)
             rows = w1[a * KP : (a + 1) * KP, b * KP : (b + 1) * KP]
             nc.sync.dma_start(raw[:], rows.rearrange("(p j) c -> p j c", j=PACK))
             w1_raw[a, b] = raw
 
-        table = [load_table(0, rooms, 0), load_table(1, shared, TABLE1_AT)]
-        load_w1(0, 0, 2)
-        load_w1(1, 0, 1)
+        table = [load_table(0, TABLE0_AT)]
+        load_rows(w2_scales, H)
+        table.append(load_table(1, TABLE1_AT))
+        load_w1(0, 0, W1_EARLY_AT[0])
+        load_w1(1, 0, W1_EARLY_AT[1])
 
-        w1_codes = [keep.tile([P, PASSES, KP], U32, name=f"w1_codes{b}", align_bytes=64) for b in range(BLOCKS)]
-        w1_planes = {(0, 0): shared.tile([P, KP], U8, name="w1_plane00", align_bytes=64, offset=W1_SCALES_AT)}
-        for a, b in ((1, 0), (0, 1), (1, 1)):
-            w1_planes[a, b] = keep.tile([P, KP], U8, name=f"w1_plane{a}{b}", align_bytes=64)
-        w1_bf16 = {(0, 0): shared.tile([P, PACK * KP], BF16, name="w1_bf00", align_bytes=64, offset=W1_BF16_AT)}
-
-        def cast_w1(a, b, m0, m1):
-            dst = w1_bf16[a, b][:].rearrange("p (t m j) -> p m j t", t=PACK, j=PACK)[:, m0:m1]
-            src = w1_raw[a, b][:].rearrange("p j (m t) -> p m j t", t=PACK)[:, m0:m1]
-            nc.scalar.copy(dst, src)
-
-        def quantize_w1(a, b):
-            nc.vector.quantize_mx(
-                out=w1_codes[b][:, a, :].bitcast(FP8X4), scales=w1_planes[a, b][:], in_=w1_bf16[a, b][:]
-            )
-
-        scales_got = keep.tile([P, S], U8, name="scales_got", align_bytes=64)
-        v_planes = [keep.tile([P, S], U8, name=f"v_plane{a}", align_bytes=64) for a in range(PASSES)]
-        nc.vector.memset(v_planes[1][:].bitcast(I32), 0)
-        nc.vector.tensor_copy(scales_got[:], scale_window[:].indirect(offsets[:]))
-        nc.vector.tensor_copy(v_planes[0][:].bitcast(I32), scales_got[:].bitcast(I32))
-        got, planes = scales_got[:].bitcast(I32), [plane[:].bitcast(I32) for plane in v_planes]
-        for e in range(2):
-            nc.scalar.dma_start(planes[0][2 + e : P : 32], got[16 + e : P : 32])
-        for d in range(QUADRANTS):
-            nc.scalar.dma_start(planes[1][32 * d : 32 * d + 4], got[32 * d + 4 : 32 * d + 32 : 8])
-
-        w2_codes, w2_planes = [], {}
+        w2_codes, w2_planes = {}, {}
 
         def order_w2_words(b):
-            words = shared.tile([P, PASSES, PACK, 2 * P], U8, name=f"w2_codes{b}", align_bytes=64, offset=W2_WORDS_AT[b])
+            w2_codes[b] = keep.tile([P, PASSES, PACK, 2 * P], U8, name=f"w2_codes{b}", align_bytes=64)
             src = w2_raw[b][:].bitcast(U16)
-            nc.vector.tensor_copy(words[:].bitcast(U16), src.rearrange("p a (m t) -> p a t m", t=PACK))
-            w2_codes.append(words)
+            nc.scalar.copy(w2_codes[b][:].bitcast(U16), src.rearrange("p a (m t) -> p a t m", t=PACK))
 
-        def order_w2_scales(b, t0, t1, at):
-            planes = shared.tile([P, PASSES, t1 - t0, P], U8, name=f"w2_planes{b}{t0}", align_bytes=64, offset=at)
-            src = w2_planes_raw[:, :, b * KP : (b + 1) * KP].rearrange("p a (m t) -> p a t m", t=PACK)
-            nc.vector.tensor_copy(planes[:], src[:, :, t0:t1])
-            for t in range(t0, t1):
-                w2_planes[b, t] = planes[:, :, t - t0, :]
+        def order_w2_scales(b, planes):
+            src = weight_rows[:, :, b * KP : (b + 1) * KP].rearrange("p a (m t) -> p a t m", t=PACK)
+            nc.vector.tensor_copy(planes[:], src)
+            w2_planes[b] = planes
 
         v_codes = {}
 
@@ -163,31 +122,49 @@ def tile_list_seawater_horner_surrogate_kernel(
             nc.vector.tensor_copy(v_codes[a, half][:].bitcast(U32), table[a][:].bitcast(U32).indirect(lists))
 
         order_w2_words(0)
+        scales_got = keep.tile([P, S], U8, name="scales_got", align_bytes=64)
+        nc.vector.tensor_copy(scales_got[:], scale_window[:].indirect(offsets[:]))
+        for d in range(QUADRANTS):
+            nc.scalar.dma_start(
+                v_planes[32 * d : 32 * d + 4].rearrange("p a c -> p (a c)").bitcast(I32),
+                scales_got[32 * d : 32 * d + 32 : 4].bitcast(I32),
+            )
         gather_words(0, 0)
         gather_words(0, 1)
-        load_w1(0, 1, 0)
-        gather_words(1, 0)
-        gather_words(1, 1)
-        order_w2_scales(0, 0, B_FIRST, W2_SCALES_AT[0])
-        order_w2_scales(1, 0, PACK, W2_SCALES_AT[2])
-        w2_raw.append(shared.tile([P, PASSES, KP // 2], I32, name="w2_raw1", align_bytes=64, offset=W2_RAW_AT[1]))
+        load_w1(0, 1, LATE_AT["w1_01"])
+        load_w1(1, 1, LATE_AT["w1_11"])
+        w2_raw.append(placed.tile([P, PASSES, KP // 2], I32, name="w2_raw1", align_bytes=64, offset=LATE_AT["w2_raw1"]))
         nc.sync.dma_start(w2_raw[1][:], w2_by_block[1])
-        cast_w1(0, 0, 0, P)
-        load_w1(1, 1, 2)
-        quantize_w1(0, 0)
-        pairs = []
-        for pair, copy in enumerate((nc.vector.tensor_copy, nc.scalar.copy)):
-            pairs.append(shared.tile([P, 2 * KP], BF16, name=f"w1_pair{pair}", align_bytes=64, offset=W1_PAIRS_AT[pair]))
-            dst = pairs[pair][:].rearrange("p (t m j) -> p m j t", t=2, j=PACK)
-            copy(dst, w1_raw[1, 0][:].rearrange("p j (m t) -> p m j t", t=PACK)[:, :, :, 2 * pair : 2 * pair + 2])
-        for pair in range(2):
-            cols = slice(pair * 2 * P, (pair + 1) * 2 * P)
-            nc.vector.quantize_mx(
-                out=w1_codes[0][:, 1, cols].bitcast(FP8X4), scales=w1_planes[1, 0][:, cols], in_=pairs[pair][:]
-            )
-        order_w2_scales(0, B_FIRST, PACK, W2_SCALES_AT[1])
-        w3_codes = shared.tile([P, PASSES, N], I32, name="w3_codes", align_bytes=64, offset=W3_AT)
+        w3_codes = placed.tile([P, PASSES, N], I32, name="w3_codes", align_bytes=64, offset=LATE_AT["w3"])
         nc.sync.dma_start(w3_codes[:], w3_words.rearrange("a p c i -> p a (c i)").bitcast(I32))
+        gather_words(1, 0)
+        order_w2_scales(0, keep.tile([P, PASSES, PACK, P], U8, name="w2_planes0", align_bytes=64))
+        gather_words(1, 1)
+        order_w2_scales(1, placed.tile([P, PASSES, PACK, P], U8, name="w2_planes1", align_bytes=64, offset=W2_PLANES1_AT))
+        load_rows(w3_scales, N)
+
+        w1_codes = [keep.tile([P, PASSES, KP], U32, name=f"w1_codes{b}", align_bytes=64) for b in range(BLOCKS)]
+        w1_bf16, w1_planes = {}, {}
+
+        def cast_w1(engine, a, b, t0, t1, m0, m1):
+            if m0 == 0:
+                w1_bf16[a, b, t0] = keep.tile([P, (t1 - t0) * KP], BF16, name=f"w1_bf{a}{b}{t0}", align_bytes=64)
+            dst = w1_bf16[a, b, t0][:].rearrange("p (t m j) -> p m j t", t=t1 - t0, j=PACK)[:, m0:m1]
+            src = w1_raw[a, b][:].rearrange("p j (m t) -> p m j t", t=PACK)[:, m0:m1, :, t0:t1]
+            if engine == "gpsimd":
+                order = "p m j t -> p t m j"
+                nc.gpsimd.tensor_scalar(dst.rearrange(order), src.rearrange(order), 1.0, 0.0, MULT, ADD)
+            elif engine == "scalar":
+                nc.scalar.copy(dst, src)
+            else:
+                nc.vector.tensor_copy(dst, src)
+
+        def quantize_w1(a, b, t0, t1):
+            plane = keep.tile([P, (t1 - t0) * P], U8, name=f"w1_plane{a}{b}{t0}", align_bytes=64)
+            codes = w1_codes[b][:, a, t0 * P : t1 * P]
+            nc.vector.quantize_mx(out=codes.bitcast(FP8X4), scales=plane[:], in_=w1_bf16[a, b, t0][:])
+            for t in range(t0, t1):
+                w1_planes[a, b, t] = plane[:, (t - t0) * P : (t - t0 + 1) * P]
 
         groups = [(b, half) for b in range(BLOCKS) for half in range(HALVES)]
         last_group = len(groups) - 1
@@ -200,7 +177,7 @@ def tile_list_seawater_horner_surrogate_kernel(
                 banks.append([])
             banks[-1].append(i)
         x_bank = {}
-        b_ps, b_sb, x_ps, inner, y_chunk, h_slots, h_woven, h_mx = {}, {}, {}, {}, {}, {}, {}, {}
+        b_sb, x_ps, inner, y_chunk, h_slots, h_woven, h_mx = {}, {}, {}, {}, {}, {}, {}
 
         def first_stage(acc, codes, plane, a, nth, c0, c1):
             nc.tensor.matmul_mx(
@@ -208,27 +185,25 @@ def tile_list_seawater_horner_surrogate_kernel(
                 lhsT=codes,
                 lhsT_scale=plane,
                 rhs=v_codes[a, c0 // NT][:, c0 % NT : c0 % NT + c1 - c0].bitcast(FP8X4),
-                rhs_scale=v_planes[a][:, c0:c1],
+                rhs_scale=v_planes[:, a, c0:c1],
                 start=(nth == 0),
                 stop=(nth == PASSES - 1),
             )
 
-        def matmul_b(u, nth):
+        def make_b(u):
             g, t = divmod(u, PACK)
             b, half = groups[g]
-            a = nth
-            if nth == 0:
-                b_ps[u] = psum.tile([P, NT], F32, name="b_ps", tag=f"b{u % RING}")
-            codes = w2_codes[b][:, a, t, :].bitcast(FP4X4)
-            first_stage(b_ps[u][:], codes, w2_planes[b, t][:, a, :], a, nth, half * NT, (half + 1) * NT)
-            if nth == PASSES - 1:
-                if u < PACK:
-                    b_sb[g, t] = rooms.tile([P, NT], F32, name=f"b_sb{u}", align_bytes=64, offset=ROOM + u * ROOM // PACK)
-                else:
-                    b_sb[g, t] = ring.tile([P, NT], F32, name="b_sb", bufs=2 * RING)
-                nc.scalar.copy(b_sb[g, t][:], b_ps[u][:])
+            acc = psum.tile([P, NT], F32, name="b_ps", tag=f"b{u % RING}")
+            for a in range(PASSES):
+                codes = w2_codes[b][:, a, t, :].bitcast(FP4X4)
+                first_stage(acc[:], codes, w2_planes[b][:, a, t, :], a, a, half * NT, (half + 1) * NT)
+            if u < len(B_FIRST_AT):
+                b_sb[g, t] = placed.tile([P, NT], F32, name=f"b_sb{u}", align_bytes=64, offset=B_FIRST_AT[u])
+            else:
+                b_sb[g, t] = ring.tile([P, NT], F32, name="b_sb", bufs=2 * RING)
+            nc.scalar.copy(b_sb[g, t][:], acc[:])
 
-        def matmul_x(bank, nths):
+        def matmul_x(bank, nths, order):
             if nths[0] == 0:
                 whole = psum.tile([P, NT], F32, name="x_ps", tag=f"x{bank % RING}")
             for place, i in enumerate(banks[bank]):
@@ -238,21 +213,21 @@ def tile_list_seawater_horner_surrogate_kernel(
                 if nths[0] == 0:
                     x_ps[i] = whole[:, place * (c1 - c0) : (place + 1) * (c1 - c0)]
                     x_bank[i] = whole[:]
-                cols = slice(t * P, (t + 1) * P)
                 for nth in nths:
-                    a = nth if bank < X_EARLY else 1 - nth
-                    codes = w1_codes[b][:, a, cols].bitcast(FP8X4)
-                    first_stage(x_ps[i], codes, w1_planes[a, b][:, cols], a, nth, half * NT + c0, half * NT + c1)
+                    a = order[nth]
+                    codes = w1_codes[b][:, a, t * P : (t + 1) * P].bitcast(FP8X4)
+                    first_stage(x_ps[i], codes, w1_planes[a, b, t], a, nth, half * NT + c0, half * NT + c1)
+
+        def is_narrow(ch):
+            return chunks[ch][2] - chunks[ch][1] == NARROW
 
         def horner_inner(i):
             ch, t = steps[i]
             g, c0, c1 = chunks[ch]
-            if WEAVE[ch][0] == "vector":
+            if is_narrow(ch):
                 if t == 0:
                     inner[ch, "all"] = keep.tile([P, NT], F32, name=f"inner{ch}")
                 inner[i] = inner[ch, "all"][:, t * (c1 - c0) : (t + 1) * (c1 - c0)]
-            elif i == 0:
-                inner[i] = shared.tile([P, c1 - c0], F32, name="inner_first", align_bytes=64, offset=W2_WORDS_AT[1])
             else:
                 inner[i] = ring.tile([P, c1 - c0], F32, name="inner", bufs=3)
             q_t = q_col[:, groups[g][0], t : t + 1]
@@ -263,30 +238,28 @@ def tile_list_seawater_horner_surrogate_kernel(
             g, c0, c1 = chunks[ch]
             if t == 0:
                 h_woven[ch] = keep.tile([P, c1 - c0, PACK], BF16, name=f"h_woven{ch}", align_bytes=64)
-            if WEAVE[ch][0] == "vector":
+            if is_narrow(ch):
                 if t == PACK - 1:
                     y_chunk[ch] = keep.tile([P, PACK, c1 - c0], F32, name=f"y_chunk{ch}")
                     nc.vector.tensor_tensor(y_chunk[ch][:].rearrange("p t n -> p (t n)"), inner[ch, "all"][:], x_bank[i], MULT)
                 return
             if t == 0:
                 h_slots[ch] = keep.tile([P, PACK, c1 - c0], BF16, name=f"h_slots{ch}", align_bytes=64)
-            y = ring.tile([P, c1 - c0], F32, name="y", bufs=6)
+            y = ring.tile([P, c1 - c0], F32, name="y", bufs=8)
             nc.vector.tensor_tensor(y[:], inner[i][:], x_ps[i], MULT)
             nc.gpsimd.tensor_scalar(h_slots[ch][:, t, :], y[:], 1.0, c_col[:, groups[g][0], t : t + 1], MULT, ADD)
 
         def weave(ch, piece):
             g, c0, c1 = chunks[ch]
-            engine, pieces = WEAVE[ch]
-            width = (c1 - c0) // pieces
+            width = (c1 - c0) // len(WEAVE_STEPS[ch])
             cols = slice(piece * width, (piece + 1) * width)
-            dst = h_woven[ch][:, cols, :]
-            dst_by_four = dst.rearrange("p (c i) t -> p c t i", i=4)
-            if engine == "scalar":
-                nc.scalar.copy(dst_by_four, h_slots[ch][:, :, cols].rearrange("p t (c i) -> p c t i", i=4))
-            else:
+            dst = h_woven[ch][:, cols, :].rearrange("p (c i) t -> p c t i", i=4)
+            if is_narrow(ch):
                 src = y_chunk[ch][:, :, cols].rearrange("p t (c i) -> p c t i", i=4)
                 c_t = c_col[:, groups[g][0], :].unsqueeze(1).unsqueeze(3).to_broadcast([P, width // 4, PACK, 4])
-                nc.vector.tensor_tensor(dst_by_four, src, c_t, ADD)
+                nc.vector.tensor_tensor(dst, src, c_t, ADD)
+            else:
+                nc.scalar.copy(dst, h_slots[ch][:, :, cols].rearrange("p t (c i) -> p c t i", i=4))
 
         def quantize_h(ch):
             g, c0, c1 = chunks[ch]
@@ -308,7 +281,7 @@ def tile_list_seawater_horner_surrogate_kernel(
                     nc.tensor.matmul_mx(
                         out=accs[n][:],
                         lhsT=w3_codes[:, b, n * P : (n + 1) * P].bitcast(FP8X4),
-                        lhsT_scale=w3_planes[:, b, n * P : (n + 1) * P],
+                        lhsT_scale=weight_rows[:, b, n * P : (n + 1) * P],
                         rhs=codes.bitcast(FP8X4),
                         rhs_scale=plane,
                         start=(b == 0),
@@ -322,55 +295,50 @@ def tile_list_seawater_horner_surrogate_kernel(
                 copy(res[:], accs[n][:])
                 queue.dma_start(dst, res[:])
 
-        weave_at, quantize_at = {}, {}
-        for ch in reversed(range(len(chunks))):
-            engine, pieces = WEAVE[ch]
-            end = PACK * ch + PACK - 1
-            first = min(end + 1, len(steps) - 1) if engine == "vector" else max(end, W1_CAST_STEPS[-1] + 1)
-            for piece in range(pieces):
-                weave_at.setdefault(first + piece, []).append((ch, piece))
-            after = QUANT_AFTER_VECTOR if engine == "vector" else QUANT_AFTER_OTHERS
-            quantize_at.setdefault(min(end + after, len(steps)), []).append(ch)
-
-        for u in range(B_FIRST):
-            for nth in range(PASSES):
-                matmul_b(u, nth)
-        for nth in range(PASSES):
-            for bank in range(X_EARLY):
-                matmul_x(bank, (nth,))
-        for u in range(X_EARLY, B_LEAD):
-            if u >= B_FIRST:
-                for nth in range(PASSES):
-                    matmul_b(u, nth)
-            if u < X_LEAD:
-                matmul_x(u, (0, 1))
-        filled = X_LEAD
+        cast_w1("scalar", 0, 0, 0, 2, 0, P)
+        cast_w1("vector", 0, 0, 2, 4, 0, P)
+        quantize_w1(0, 0, 0, 2)
+        for u in range(2):
+            make_b(u)
+        for bank in range(2):
+            matmul_x(bank, (0,), (0, 1))
+        cast_w1("vector", 1, 0, 0, 2, 0, P)
+        quantize_w1(0, 0, 2, 4)
+        quantize_w1(1, 0, 0, 2)
+        for bank in range(2):
+            matmul_x(bank, (1,), (0, 1))
+        cast_w1("scalar", 1, 0, 2, 4, 0, P)
+        for u in range(2, LEAD):
+            make_b(u)
         horner_inner(0)
+        quantize_w1(1, 0, 2, 4)
+        for piece in range(GPSIMD_CAST_PIECES):
+            width = P // GPSIMD_CAST_PIECES
+            cast_w1("gpsimd", 0, 1, 0, PACK, piece * width, (piece + 1) * width)
+        filled = 2
         for i in range(len(steps) + 1):
-            if i == 1:
-                order_w2_words(1)
             if i in W1_CAST_STEPS:
-                a, half = divmod(W1_CAST_STEPS.index(i), 2)
-                if half == 0:
-                    at = ROOM + a * ROOM // 2
-                    w1_bf16[a, 1] = rooms.tile([P, PACK * KP], BF16, name=f"w1_bf{a}1", align_bytes=64, offset=at)
-                cast_w1(a, 1, half * (P // 2), (half + 1) * (P // 2))
+                half = W1_CAST_STEPS.index(i)
+                cast_w1("scalar", 1, 1, 0, PACK, half * (P // 2), (half + 1) * (P // 2))
+            if i == W2_ORDER_STEP:
+                order_w2_words(1)
             if i in W1_QUANT_STEPS:
-                quantize_w1(W1_QUANT_STEPS.index(i), 1)
-            ahead = i + X_LEAD + 1 if i >= W1_QUANT_STEPS[-1] else min(i + X_LEAD + 1, HALVES * PACK)
+                quantize_w1(W1_QUANT_STEPS.index(i), 1, 0, PACK)
+            ahead = i + LEAD if i >= W1_QUANT_STEPS[-1] else min(i + LEAD, HALVES * PACK)
             while filled < min(ahead, len(banks)):
-                matmul_x(filled, (0, 1))
+                matmul_x(filled, (0, 1), (1, 0) if filled < PACK else (0, 1))
                 filled = filled + 1
-            if i + B_LEAD < len(groups) * PACK:
-                for nth in range(PASSES):
-                    matmul_b(i + B_LEAD, nth)
-            for ch in quantize_at.get(i, ()):
-                quantize_h(ch)
-                if groups[chunks[ch][0]][0] == BLOCKS - 1:
-                    second_stage(ch)
+            if i + LEAD < len(groups) * PACK:
+                make_b(i + LEAD)
+            for ch in range(len(chunks)):
+                if H_QUANT_STEPS[ch] == i:
+                    quantize_h(ch)
+                    if groups[chunks[ch][0]][0] == BLOCKS - 1:
+                        second_stage(ch)
             if i + 1 < len(steps):
                 horner_inner(i + 1)
             if i < len(steps):
                 horner_outer(i)
-            for ch, piece in weave_at.get(i, ()):
-                weave(ch, piece)
+            for ch in range(len(chunks)):
+                if i in WEAVE_STEPS[ch]:
+                    weave(ch, WEAVE_STEPS[ch].index(i))

@@ -31,11 +31,10 @@ PAIRS = PACK // 2
 LAST_CHUNKS = ((0, 256), (256, 384), (384, 512))
 NARROW = 128
 LEAD = 4
-GPSIMD_CAST_PIECES = 4
-W1_CAST_STEPS = (2, 3)
-W2_ORDER_STEP = 2
+W1_CAST_STEPS = (0, 1, 2, 3)
+W2_ORDER_STEP = 4
 W1_QUANT_STEPS = (4, 6)
-WEAVE_STEPS = ((6, 7), (8, 9), (11, 12), (15,), (20,), (23,))
+WEAVE_STEPS = ((5, 6), (7, 8), (11, 12), (15,), (20,), (23,))
 H_QUANT_STEPS = (11, 14, 18, 22, 22, 24)
 
 ROOM = 8192
@@ -107,7 +106,8 @@ def tile_list_seawater_horner_surrogate_kernel(
         def order_w2_words(b):
             w2_codes[b] = keep.tile([P, PASSES, PACK, 2 * P], U8, name=f"w2_codes{b}", align_bytes=64)
             src = w2_raw[b][:].bitcast(U16)
-            nc.scalar.copy(w2_codes[b][:].bitcast(U16), src.rearrange("p a (m t) -> p a t m", t=PACK))
+            copy = nc.scalar.copy if b == 0 else nc.vector.tensor_copy
+            copy(w2_codes[b][:].bitcast(U16), src.rearrange("p a (m t) -> p a t m", t=PACK))
 
         def order_w2_scales(b, planes):
             src = weight_rows[:, :, b * KP : (b + 1) * KP].rearrange("p a (m t) -> p a t m", t=PACK)
@@ -151,10 +151,7 @@ def tile_list_seawater_horner_surrogate_kernel(
                 w1_bf16[a, b, t0] = keep.tile([P, (t1 - t0) * KP], BF16, name=f"w1_bf{a}{b}{t0}", align_bytes=64)
             dst = w1_bf16[a, b, t0][:].rearrange("p (t m j) -> p m j t", t=t1 - t0, j=PACK)[:, m0:m1]
             src = w1_raw[a, b][:].rearrange("p j (m t) -> p m j t", t=PACK)[:, m0:m1, :, t0:t1]
-            if engine == "gpsimd":
-                order = "p m j t -> p t m j"
-                nc.gpsimd.tensor_scalar(dst.rearrange(order), src.rearrange(order), 1.0, 0.0, MULT, ADD)
-            elif engine == "scalar":
+            if engine == "scalar":
                 nc.scalar.copy(dst, src)
             else:
                 nc.vector.tensor_copy(dst, src)
@@ -310,16 +307,13 @@ def tile_list_seawater_horner_surrogate_kernel(
         cast_w1("scalar", 1, 0, 2, 4, 0, P)
         for u in range(2, LEAD):
             make_b(u)
-        horner_inner(0)
         quantize_w1(1, 0, 2, 4)
-        for piece in range(GPSIMD_CAST_PIECES):
-            width = P // GPSIMD_CAST_PIECES
-            cast_w1("gpsimd", 0, 1, 0, PACK, piece * width, (piece + 1) * width)
+        horner_inner(0)
         filled = 2
         for i in range(len(steps) + 1):
             if i in W1_CAST_STEPS:
-                half = W1_CAST_STEPS.index(i)
-                cast_w1("scalar", 1, 1, 0, PACK, half * (P // 2), (half + 1) * (P // 2))
+                a, half = divmod(W1_CAST_STEPS.index(i), 2)
+                cast_w1("scalar", a, 1, 0, PACK, half * (P // 2), (half + 1) * (P // 2))
             if i == W2_ORDER_STEP:
                 order_w2_words(1)
             if i in W1_QUANT_STEPS:

@@ -31,11 +31,12 @@ PAIRS = PACK // 2
 LAST_CHUNKS = ((0, 256), (256, 384), (384, 512))
 NARROW = 128
 LEAD = 4
-W1_CAST_STEPS = (0, 1, 2, 3)
-W2_ORDER_STEP = 4
+W1_CAST_STEPS = (2, 3)
+W2_ORDER_STEP = 2
 W1_QUANT_STEPS = (4, 6)
-WEAVE_STEPS = ((5, 6), (7, 8), (11, 12), (15,), (20,), (23,))
-H_QUANT_STEPS = (11, 14, 18, 22, 22, 24)
+WEAVE_STEPS = ((5, 6), (7, 8), (11, 12), (15,), (19,), (23,))
+OUT_BANKS = (("b0", "b1"), ("b2", "b3"), ("x0", "x1"), ("x2", "x3"))
+H_QUANT_STEPS = (11, 14, 18, 21, 23, 24)
 
 ROOM = 8192
 TABLE0_AT = 6144
@@ -106,8 +107,7 @@ def tile_list_seawater_horner_surrogate_kernel(
         def order_w2_words(b):
             w2_codes[b] = keep.tile([P, PASSES, PACK, 2 * P], U8, name=f"w2_codes{b}", align_bytes=64)
             src = w2_raw[b][:].bitcast(U16)
-            copy = nc.scalar.copy if b == 0 else nc.vector.tensor_copy
-            copy(w2_codes[b][:].bitcast(U16), src.rearrange("p a (m t) -> p a t m", t=PACK))
+            nc.scalar.copy(w2_codes[b][:].bitcast(U16), src.rearrange("p a (m t) -> p a t m", t=PACK))
 
         def order_w2_scales(b, planes):
             src = weight_rows[:, :, b * KP : (b + 1) * KP].rearrange("p a (m t) -> p a t m", t=PACK)
@@ -151,13 +151,19 @@ def tile_list_seawater_horner_surrogate_kernel(
                 w1_bf16[a, b, t0] = keep.tile([P, (t1 - t0) * KP], BF16, name=f"w1_bf{a}{b}{t0}", align_bytes=64)
             dst = w1_bf16[a, b, t0][:].rearrange("p (t m j) -> p m j t", t=t1 - t0, j=PACK)[:, m0:m1]
             src = w1_raw[a, b][:].rearrange("p j (m t) -> p m j t", t=PACK)[:, m0:m1, :, t0:t1]
-            if engine == "scalar":
+            if engine == "gpsimd":
+                for t in range(t1 - t0):
+                    nc.gpsimd.tensor_scalar(dst[:, :, :, t], src[:, :, :, t], 1.0, 0.0, MULT, ADD)
+            elif engine == "scalar":
                 nc.scalar.copy(dst, src)
             else:
                 nc.vector.tensor_copy(dst, src)
 
         def quantize_w1(a, b, t0, t1):
-            plane = keep.tile([P, (t1 - t0) * P], U8, name=f"w1_plane{a}{b}{t0}", align_bytes=64)
+            if (a, b, t0) == (0, 1, 0):
+                plane = placed.tile([P, 2 * P], U8, name="w1_plane010", align_bytes=64, offset=B_FIRST_AT[3])
+            else:
+                plane = keep.tile([P, (t1 - t0) * P], U8, name=f"w1_plane{a}{b}{t0}", align_bytes=64)
             codes = w1_codes[b][:, a, t0 * P : t1 * P]
             nc.vector.quantize_mx(out=codes.bitcast(FP8X4), scales=plane[:], in_=w1_bf16[a, b, t0][:])
             for t in range(t0, t1):
@@ -216,7 +222,7 @@ def tile_list_seawater_horner_surrogate_kernel(
                     first_stage(x_ps[i], codes, w1_planes[a, b, t], a, nth, half * NT + c0, half * NT + c1)
 
         def is_narrow(ch):
-            return chunks[ch][2] - chunks[ch][1] == NARROW
+            return ch == last_chunk
 
         def horner_inner(i):
             ch, t = steps[i]
@@ -272,7 +278,7 @@ def tile_list_seawater_horner_surrogate_kernel(
             half = groups[g][1]
             first_codes, first_plane = h_mx[groups.index((0, half))]
             operands = [(first_codes[:, c0:c1], first_plane[:, c0:c1]), (h_mx[ch][0][:], h_mx[ch][1][:])]
-            accs = [psum.tile([P, c1 - c0], F32, name="o_ps", tag=f"b{2 * (ch % 2) + n}") for n in range(N // P)]
+            accs = [psum.tile([P, c1 - c0], F32, name="o_ps", tag=OUT_BANKS[ch - HALVES][n]) for n in range(N // P)]
             for b, (codes, plane) in enumerate(operands):
                 for n in range(N // P):
                     nc.tensor.matmul_mx(
@@ -309,15 +315,21 @@ def tile_list_seawater_horner_surrogate_kernel(
             make_b(u)
         quantize_w1(1, 0, 2, 4)
         horner_inner(0)
+        cast_w1("gpsimd", 0, 1, 0, 2, 0, P)
         filled = 2
         for i in range(len(steps) + 1):
             if i in W1_CAST_STEPS:
-                a, half = divmod(W1_CAST_STEPS.index(i), 2)
-                cast_w1("scalar", a, 1, 0, PACK, half * (P // 2), (half + 1) * (P // 2))
+                half = W1_CAST_STEPS.index(i)
+                cast_w1("scalar", 1, 1, 0, PACK, half * (P // 2), (half + 1) * (P // 2))
+            if i == 0:
+                cast_w1("scalar", 0, 1, 2, PACK, 0, P)
             if i == W2_ORDER_STEP:
                 order_w2_words(1)
-            if i in W1_QUANT_STEPS:
-                quantize_w1(W1_QUANT_STEPS.index(i), 1, 0, PACK)
+            if i == W1_QUANT_STEPS[0]:
+                quantize_w1(0, 1, 0, 2)
+                quantize_w1(0, 1, 2, PACK)
+            if i == W1_QUANT_STEPS[1]:
+                quantize_w1(1, 1, 0, PACK)
             ahead = i + LEAD if i >= W1_QUANT_STEPS[-1] else min(i + LEAD, HALVES * PACK)
             while filled < min(ahead, len(banks)):
                 matmul_x(filled, (0, 1), (1, 0) if filled < PACK else (0, 1))

@@ -32,19 +32,20 @@ LAST_CHUNKS = ((0, 256), (256, 384), (384, 512))
 NARROW = 128
 LEAD = 4
 W1_CAST_STEPS = (2, 3)
-W2_ORDER_STEP = 2
-W1_QUANT_STEPS = (4, 6)
+W2_ORDER_STEP = 4
+W1_QUANT_STEP = 6
 WEAVE_STEPS = ((5, 6), (7, 8), (11, 12), (15,), (19,), (23,))
 OUT_BANKS = (("b0", "b1"), ("b2", "b3"), ("x0", "x1"), ("x2", "x3"))
-H_QUANT_STEPS = (11, 14, 18, 21, 23, 24)
+H_QUANT_STEPS = (11, 14, 18)
 
 ROOM = 8192
 TABLE0_AT = 6144
 LATE_AT = {"w1_01": 0, "w2_raw1": 8192, "w3": 10240, "w1_11": 12288}
 W1_EARLY_AT = (20480, 28672)
-B_FIRST_AT = (20480, 22528, 28672, 30720)
+B_FIRST_AT = (20480, 22528, 28672, 30720, 24576, 26624)
 TABLE1_AT = 36864
 W2_PLANES1_AT = TABLE1_AT
+W1_SHARED_AT = 45056
 
 
 def tile_list_seawater_horner_surrogate_kernel(
@@ -147,7 +148,9 @@ def tile_list_seawater_horner_surrogate_kernel(
         w1_bf16, w1_planes = {}, {}
 
         def cast_w1(engine, a, b, t0, t1, m0, m1):
-            if m0 == 0:
+            if (a, b, t0) in ((1, 0, 2), (0, 1, 0)):
+                w1_bf16[a, b, t0] = placed.tile([P, 2 * KP], BF16, name=f"w1_bf{a}{b}{t0}", align_bytes=64, offset=W1_SHARED_AT)
+            elif m0 == 0:
                 w1_bf16[a, b, t0] = keep.tile([P, (t1 - t0) * KP], BF16, name=f"w1_bf{a}{b}{t0}", align_bytes=64)
             dst = w1_bf16[a, b, t0][:].rearrange("p (t m j) -> p m j t", t=t1 - t0, j=PACK)[:, m0:m1]
             src = w1_raw[a, b][:].rearrange("p j (m t) -> p m j t", t=PACK)[:, m0:m1, :, t0:t1]
@@ -161,7 +164,7 @@ def tile_list_seawater_horner_surrogate_kernel(
 
         def quantize_w1(a, b, t0, t1):
             if (a, b, t0) == (0, 1, 0):
-                plane = placed.tile([P, 2 * P], U8, name="w1_plane010", align_bytes=64, offset=B_FIRST_AT[3])
+                plane = placed.tile([P, 2 * P], U8, name="w1_plane010", align_bytes=64, offset=B_FIRST_AT[5])
             else:
                 plane = keep.tile([P, (t1 - t0) * P], U8, name=f"w1_plane{a}{b}{t0}", align_bytes=64)
             codes = w1_codes[b][:, a, t0 * P : t1 * P]
@@ -179,7 +182,7 @@ def tile_list_seawater_horner_surrogate_kernel(
             if t % (NT // (chunks[ch][2] - chunks[ch][1])) == 0:
                 banks.append([])
             banks[-1].append(i)
-        x_bank = {}
+        x_bank, out_ps = {}, {}
         b_sb, x_ps, inner, y_chunk, h_slots, h_woven, h_mx = {}, {}, {}, {}, {}, {}, {}
 
         def first_stage(acc, codes, plane, a, nth, c0, c1):
@@ -290,13 +293,14 @@ def tile_list_seawater_horner_surrogate_kernel(
                         start=(b == 0),
                         stop=(b == BLOCKS - 1),
                     )
-            for n in range(N // P):
-                res = keep.tile([P, c1 - c0], F32, name=f"res{ch}{n}")
-                dst = out[n * P : (n + 1) * P, half * NT + c0 : half * NT + c1]
-                copy = nc.vector.tensor_copy if ch == last_chunk and n == 1 else nc.scalar.copy
-                queue = nc.scalar if ch == last_chunk and n == 0 else nc.sync
-                copy(res[:], accs[n][:])
-                queue.dma_start(dst, res[:])
+            out_ps[ch] = accs
+
+        def store(ch, n, copy, queue):
+            g, c0, c1 = chunks[ch]
+            half = groups[g][1]
+            res = keep.tile([P, c1 - c0], F32, name=f"res{ch}{n}")
+            copy(res[:], out_ps[ch][n][:])
+            queue.dma_start(out[n * P : (n + 1) * P, half * NT + c0 : half * NT + c1], res[:])
 
         cast_w1("scalar", 0, 0, 0, 2, 0, P)
         cast_w1("vector", 0, 0, 2, 4, 0, P)
@@ -317,7 +321,7 @@ def tile_list_seawater_horner_surrogate_kernel(
         horner_inner(0)
         cast_w1("gpsimd", 0, 1, 0, 2, 0, P)
         filled = 2
-        for i in range(len(steps) + 1):
+        for i in range(len(steps) - 1):
             if i in W1_CAST_STEPS:
                 half = W1_CAST_STEPS.index(i)
                 cast_w1("scalar", 1, 1, 0, PACK, half * (P // 2), (half + 1) * (P // 2))
@@ -325,26 +329,40 @@ def tile_list_seawater_horner_surrogate_kernel(
                 cast_w1("scalar", 0, 1, 2, PACK, 0, P)
             if i == W2_ORDER_STEP:
                 order_w2_words(1)
-            if i == W1_QUANT_STEPS[0]:
+            if i == W1_QUANT_STEP:
                 quantize_w1(0, 1, 0, 2)
                 quantize_w1(0, 1, 2, PACK)
-            if i == W1_QUANT_STEPS[1]:
                 quantize_w1(1, 1, 0, PACK)
-            ahead = i + LEAD if i >= W1_QUANT_STEPS[-1] else min(i + LEAD, HALVES * PACK)
+            ahead = i + LEAD if i >= W1_QUANT_STEP else min(i + LEAD, HALVES * PACK)
             while filled < min(ahead, len(banks)):
                 matmul_x(filled, (0, 1), (1, 0) if filled < PACK else (0, 1))
                 filled = filled + 1
             if i + LEAD < len(groups) * PACK:
                 make_b(i + LEAD)
-            for ch in range(len(chunks)):
-                if H_QUANT_STEPS[ch] == i:
-                    quantize_h(ch)
-                    if groups[chunks[ch][0]][0] == BLOCKS - 1:
-                        second_stage(ch)
-            if i + 1 < len(steps):
-                horner_inner(i + 1)
-            if i < len(steps):
-                horner_outer(i)
-            for ch in range(len(chunks)):
+            if i in H_QUANT_STEPS:
+                ch = H_QUANT_STEPS.index(i)
+                quantize_h(ch)
+                if groups[chunks[ch][0]][0] == BLOCKS - 1:
+                    second_stage(ch)
+                    store(ch, 0, nc.scalar.copy, nc.sync)
+            horner_inner(i + 1)
+            horner_outer(i)
+            for ch in range(last_chunk):
                 if i in WEAVE_STEPS[ch]:
                     weave(ch, WEAVE_STEPS[ch].index(i))
+            if i == H_QUANT_STEPS[-1] + 1:
+                store(HALVES, 1, nc.scalar.copy, nc.sync)
+        quantize_h(last_chunk - 2)
+        second_stage(last_chunk - 2)
+        store(last_chunk - 2, 0, nc.scalar.copy, nc.sync)
+        horner_outer(len(steps) - 1)
+        quantize_h(last_chunk - 1)
+        second_stage(last_chunk - 1)
+        weave(last_chunk, 0)
+        store(last_chunk - 2, 1, nc.vector.tensor_copy, nc.sync)
+        quantize_h(last_chunk)
+        second_stage(last_chunk)
+        for n in range(N // P):
+            store(last_chunk - 1, n, nc.scalar.copy, nc.sync)
+        store(last_chunk, 0, nc.scalar.copy, nc.scalar)
+        store(last_chunk, 1, nc.vector.tensor_copy, nc.sync)

@@ -31,12 +31,11 @@ PAIRS = PACK // 2
 LAST_CHUNKS = ((0, 256), (256, 384), (384, 512))
 NARROW = 128
 LEAD = 4
-W1_CAST_STEPS = (2, 3)
-W2_ORDER_STEP = 4
-W1_QUANT_STEP = 6
+W2_ORDER_STEP = 2
+W1_QUANT_STEPS = (5, 7)
 WEAVE_STEPS = ((5, 6), (7, 8), (11, 12), (15,), (19,), (23,))
-OUT_BANKS = (("b0", "b1"), ("b2", "b3"), ("x0", "x1"), ("x2", "x3"))
-H_QUANT_STEPS = (11, 14, 18)
+OUT_BANKS = (("b0", "b1"), ("b2", "b3"), ("x3", "x1"), ("x2", "x0"))
+H_QUANT_STEPS = (15, 16, 18)
 
 ROOM = 8192
 TABLE0_AT = 6144
@@ -211,7 +210,7 @@ def tile_list_seawater_horner_surrogate_kernel(
 
         def matmul_x(bank, nths, order):
             if nths[0] == 0:
-                whole = psum.tile([P, NT], F32, name="x_ps", tag=f"x{bank % RING}")
+                whole = psum.tile([P, NT], F32, name="x_ps", tag=f"x{0 if bank == len(banks) - 1 else bank % RING}")
             for place, i in enumerate(banks[bank]):
                 ch, t = steps[i]
                 g, c0, c1 = chunks[ch]
@@ -322,23 +321,24 @@ def tile_list_seawater_horner_surrogate_kernel(
         cast_w1("gpsimd", 0, 1, 0, 2, 0, P)
         filled = 2
         for i in range(len(steps) - 1):
-            if i in W1_CAST_STEPS:
-                half = W1_CAST_STEPS.index(i)
-                cast_w1("scalar", 1, 1, 0, PACK, half * (P // 2), (half + 1) * (P // 2))
             if i == 0:
                 cast_w1("scalar", 0, 1, 2, PACK, 0, P)
             if i == W2_ORDER_STEP:
+                cast_w1("scalar", 1, 1, 0, 2, 0, P)
                 order_w2_words(1)
-            if i == W1_QUANT_STEP:
-                quantize_w1(0, 1, 0, 2)
-                quantize_w1(0, 1, 2, PACK)
-                quantize_w1(1, 1, 0, PACK)
-            ahead = i + LEAD if i >= W1_QUANT_STEP else min(i + LEAD, HALVES * PACK)
-            while filled < min(ahead, len(banks)):
+            if i in W1_QUANT_STEPS:
+                t0 = 2 * W1_QUANT_STEPS.index(i)
+                for a in range(PASSES):
+                    quantize_w1(a, 1, t0, t0 + 2)
+            pairs_ready = sum(i >= step for step in W1_QUANT_STEPS)
+            ahead = i + LEAD if pairs_ready == 2 else min(i + LEAD, HALVES * PACK + 2 * pairs_ready)
+            while filled < min(ahead, len(banks) - (i < 14)):
                 matmul_x(filled, (0, 1), (1, 0) if filled < PACK else (0, 1))
                 filled = filled + 1
             if i + LEAD < len(groups) * PACK:
                 make_b(i + LEAD)
+            if i == W2_ORDER_STEP + 1:
+                cast_w1("scalar", 1, 1, 2, PACK, 0, P)
             if i in H_QUANT_STEPS:
                 ch = H_QUANT_STEPS.index(i)
                 quantize_h(ch)

@@ -44,6 +44,8 @@ W1_EARLY_AT = (20480, 28672)
 B_FIRST_AT = (20480, 22528, 28672, 30720, 24576, 26624)
 TABLE1_AT = 36864
 W2_PLANES1_AT = TABLE1_AT
+W1_FIRST_AT = 47104
+W2_PLANES0_AT = 49152
 W1_SHARED_AT = 45056
 
 
@@ -109,10 +111,12 @@ def tile_list_seawater_horner_surrogate_kernel(
             src = w2_raw[b][:].bitcast(U16)
             nc.scalar.copy(w2_codes[b][:].bitcast(U16), src.rearrange("p a (m t) -> p a t m", t=PACK))
 
-        def order_w2_scales(b, planes):
+        def order_w2_scales(b, t0, t1, at):
+            planes = placed.tile([P, PASSES, t1 - t0, P], U8, name=f"w2_planes{b}{t0}", align_bytes=64, offset=at)
             src = weight_rows[:, :, b * KP : (b + 1) * KP].rearrange("p a (m t) -> p a t m", t=PACK)
-            nc.vector.tensor_copy(planes[:], src)
-            w2_planes[b] = planes
+            nc.vector.tensor_copy(planes[:], src[:, :, t0:t1])
+            for t in range(t0, t1):
+                w2_planes[b, t] = planes[:, :, t - t0, :]
 
         v_codes = {}
 
@@ -138,16 +142,17 @@ def tile_list_seawater_horner_surrogate_kernel(
         w3_codes = placed.tile([P, PASSES, N], I32, name="w3_codes", align_bytes=64, offset=LATE_AT["w3"])
         nc.sync.dma_start(w3_codes[:], w3_words.rearrange("a p c i -> p a (c i)").bitcast(I32))
         gather_words(1, 0)
-        order_w2_scales(0, keep.tile([P, PASSES, PACK, P], U8, name="w2_planes0", align_bytes=64))
+        order_w2_scales(0, 0, 3, W2_PLANES0_AT)
         gather_words(1, 1)
-        order_w2_scales(1, placed.tile([P, PASSES, PACK, P], U8, name="w2_planes1", align_bytes=64, offset=W2_PLANES1_AT))
-        load_rows(w3_scales, N)
+        order_w2_scales(1, 2, PACK, W2_PLANES1_AT)
 
         w1_codes = [keep.tile([P, PASSES, KP], U32, name=f"w1_codes{b}", align_bytes=64) for b in range(BLOCKS)]
         w1_bf16, w1_planes = {}, {}
 
         def cast_w1(engine, a, b, t0, t1, m0, m1):
-            if (a, b, t0) in ((1, 0, 2), (0, 1, 0)):
+            if (a, b, t0) == (1, 0, 0):
+                w1_bf16[a, b, t0] = placed.tile([P, 2 * KP], BF16, name="w1_bf100", align_bytes=64, offset=W1_FIRST_AT)
+            elif (a, b, t0) in ((1, 0, 2), (0, 1, 0)):
                 w1_bf16[a, b, t0] = placed.tile([P, 2 * KP], BF16, name=f"w1_bf{a}{b}{t0}", align_bytes=64, offset=W1_SHARED_AT)
             elif m0 == 0:
                 w1_bf16[a, b, t0] = keep.tile([P, (t1 - t0) * KP], BF16, name=f"w1_bf{a}{b}{t0}", align_bytes=64)
@@ -201,7 +206,7 @@ def tile_list_seawater_horner_surrogate_kernel(
             acc = psum.tile([P, NT], F32, name="b_ps", tag=f"b{u % RING}")
             for a in range(PASSES):
                 codes = w2_codes[b][:, a, t, :].bitcast(FP4X4)
-                first_stage(acc[:], codes, w2_planes[b][:, a, t, :], a, a, half * NT, (half + 1) * NT)
+                first_stage(acc[:], codes, w2_planes[b, t][:, a, :], a, a, half * NT, (half + 1) * NT)
             if u < len(B_FIRST_AT):
                 b_sb[g, t] = placed.tile([P, NT], F32, name=f"b_sb{u}", align_bytes=64, offset=B_FIRST_AT[u])
             else:
@@ -314,6 +319,9 @@ def tile_list_seawater_horner_surrogate_kernel(
         for bank in range(2):
             matmul_x(bank, (1,), (0, 1))
         cast_w1("scalar", 1, 0, 2, 4, 0, P)
+        order_w2_scales(0, 3, PACK, W1_FIRST_AT)
+        order_w2_scales(1, 0, 2, W1_FIRST_AT + 256)
+        load_rows(w3_scales, N)
         for u in range(2, LEAD):
             make_b(u)
         quantize_w1(1, 0, 2, 4)

@@ -31,11 +31,12 @@ PAIRS = PACK // 2
 LAST_CHUNKS = ((0, 256), (256, 384), (384, 512))
 NARROW = 128
 LEAD = 4
+PAIRED_CHUNKS = (2,)
 W2_ORDER_STEP = 2
 W1_QUANT_STEPS = (5, 7)
-WEAVE_STEPS = ((5, 6), (7, 8), (11, 12), (15,), (19,), (23,))
+WEAVE_STEPS = ((7, 9), (10, 11), (11,), (15,), (19,), (23,))
 OUT_BANKS = (("b0", "b1"), ("b2", "b3"), ("x3", "x1"), ("x2", "x0"))
-H_QUANT_STEPS = (15, 16, 18)
+H_QUANT_STEPS = (15, 17, 18)
 
 ROOM = 8192
 TABLE0_AT = 6144
@@ -257,7 +258,11 @@ def tile_list_seawater_horner_surrogate_kernel(
                 h_slots[ch] = keep.tile([P, PACK, c1 - c0], BF16, name=f"h_slots{ch}", align_bytes=64)
             y = ring.tile([P, c1 - c0], F32, name="y", bufs=8)
             nc.vector.tensor_tensor(y[:], inner[i][:], x_ps[i], MULT)
-            nc.gpsimd.tensor_scalar(h_slots[ch][:, t, :], y[:], 1.0, c_col[:, groups[g][0], t : t + 1], MULT, ADD)
+            if ch in PAIRED_CHUNKS:
+                slot = h_slots[ch][:].rearrange("p t n -> p (t n)").rearrange("p (u n e) -> p u n e", u=2, e=2)[:, t // 2, :, t % 2]
+            else:
+                slot = h_slots[ch][:, t, :]
+            nc.gpsimd.tensor_scalar(slot, y[:], 1.0, c_col[:, groups[g][0], t : t + 1], MULT, ADD)
 
         def weave(ch, piece):
             g, c0, c1 = chunks[ch]
@@ -268,6 +273,13 @@ def tile_list_seawater_horner_surrogate_kernel(
                 src = y_chunk[ch][:, :, cols].rearrange("p t (c i) -> p c t i", i=4)
                 c_t = c_col[:, groups[g][0], :].unsqueeze(1).unsqueeze(3).to_broadcast([P, width // 4, PACK, 4])
                 nc.vector.tensor_tensor(dst, src, c_t, ADD)
+            elif ch in PAIRED_CHUNKS:
+                words = h_slots[ch][:].rearrange("p t n -> p (t n)").bitcast(F32).rearrange("p (u n) -> p u n", u=2)
+                woven = h_woven[ch][:].rearrange("p n t -> p (n t)").bitcast(F32).rearrange("p (n u) -> p n u", u=2)
+                nc.scalar.copy(
+                    woven[:, cols, :].rearrange("p (c i) u -> p c u i", i=4),
+                    words[:, :, cols].rearrange("p u (c i) -> p c u i", i=4),
+                )
             else:
                 nc.scalar.copy(dst, h_slots[ch][:, :, cols].rearrange("p t (c i) -> p c t i", i=4))
 
@@ -343,8 +355,9 @@ def tile_list_seawater_horner_surrogate_kernel(
             while filled < min(ahead, len(banks) - (i < 14)):
                 matmul_x(filled, (0, 1), (1, 0) if filled < PACK else (0, 1))
                 filled = filled + 1
-            if i + LEAD < len(groups) * PACK:
-                make_b(i + LEAD)
+            for u in range(LEAD, len(groups) * PACK):
+                if i == (u - LEAD if u < 3 * PACK else u // 2 + 2):
+                    make_b(u)
             if i == W2_ORDER_STEP + 1:
                 cast_w1("scalar", 1, 1, 2, PACK, 0, P)
             if i in H_QUANT_STEPS:

@@ -31,10 +31,9 @@ PAIRS = PACK // 2
 LAST_CHUNKS = ((0, 256), (256, 384), (384, 512))
 NARROW = 128
 LEAD = 4
-PAIRED_CHUNKS = (2,)
 W2_ORDER_STEP = 2
 W1_QUANT_STEPS = (5, 7)
-WEAVE_STEPS = ((7, 9), (10, 11), (11,), (15,), (19,), (23,))
+WEAVE_STEPS = ((7, 9), (10, 11), (12, 13), (15,), (19,), (23,))
 OUT_BANKS = (("b0", "b1"), ("b2", "b3"), ("x3", "x1"), ("x2", "x0"))
 H_QUANT_STEPS = (15, 17, 18)
 
@@ -160,8 +159,8 @@ def tile_list_seawater_horner_surrogate_kernel(
             dst = w1_bf16[a, b, t0][:].rearrange("p (t m j) -> p m j t", t=t1 - t0, j=PACK)[:, m0:m1]
             src = w1_raw[a, b][:].rearrange("p j (m t) -> p m j t", t=PACK)[:, m0:m1, :, t0:t1]
             if engine == "gpsimd":
-                for t in range(t1 - t0):
-                    nc.gpsimd.tensor_scalar(dst[:, :, :, t], src[:, :, :, t], 1.0, 0.0, MULT, ADD)
+                by_slot = "p m j t -> p t m j"
+                nc.gpsimd.tensor_scalar(dst.rearrange(by_slot), src.rearrange(by_slot), 1.0, 0.0, MULT, ADD)
             elif engine == "scalar":
                 nc.scalar.copy(dst, src)
             else:
@@ -258,11 +257,7 @@ def tile_list_seawater_horner_surrogate_kernel(
                 h_slots[ch] = keep.tile([P, PACK, c1 - c0], BF16, name=f"h_slots{ch}", align_bytes=64)
             y = ring.tile([P, c1 - c0], F32, name="y", bufs=8)
             nc.vector.tensor_tensor(y[:], inner[i][:], x_ps[i], MULT)
-            if ch in PAIRED_CHUNKS:
-                slot = h_slots[ch][:].rearrange("p t n -> p (t n)").rearrange("p (u n e) -> p u n e", u=2, e=2)[:, t // 2, :, t % 2]
-            else:
-                slot = h_slots[ch][:, t, :]
-            nc.gpsimd.tensor_scalar(slot, y[:], 1.0, c_col[:, groups[g][0], t : t + 1], MULT, ADD)
+            nc.gpsimd.tensor_scalar(h_slots[ch][:, t, :], y[:], 1.0, c_col[:, groups[g][0], t : t + 1], MULT, ADD)
 
         def weave(ch, piece):
             g, c0, c1 = chunks[ch]
@@ -273,13 +268,6 @@ def tile_list_seawater_horner_surrogate_kernel(
                 src = y_chunk[ch][:, :, cols].rearrange("p t (c i) -> p c t i", i=4)
                 c_t = c_col[:, groups[g][0], :].unsqueeze(1).unsqueeze(3).to_broadcast([P, width // 4, PACK, 4])
                 nc.vector.tensor_tensor(dst, src, c_t, ADD)
-            elif ch in PAIRED_CHUNKS:
-                words = h_slots[ch][:].rearrange("p t n -> p (t n)").bitcast(F32).rearrange("p (u n) -> p u n", u=2)
-                woven = h_woven[ch][:].rearrange("p n t -> p (n t)").bitcast(F32).rearrange("p (n u) -> p n u", u=2)
-                nc.scalar.copy(
-                    woven[:, cols, :].rearrange("p (c i) u -> p c u i", i=4),
-                    words[:, :, cols].rearrange("p u (c i) -> p c u i", i=4),
-                )
             else:
                 nc.scalar.copy(dst, h_slots[ch][:, :, cols].rearrange("p t (c i) -> p c t i", i=4))
 

from contextlib import ExitStack

import concourse.mybir as mybir

K, T, S, H, N = 1024, 2048, 1024, 1024, 256
FLOPS = 2 * (2 * K * H * S + H * N * S)

F32 = mybir.dt.float32
BF16 = mybir.dt.bfloat16
I32 = mybir.dt.int32
U32 = mybir.dt.uint32
U16 = mybir.dt.uint16
U8 = mybir.dt.uint8
FP8X4 = mybir.dt.float8_e4m3fn_x4
FP4X4 = mybir.dt.float4_e2m1fn_x4
MULT = mybir.AluOpType.mult
ADD = mybir.AluOpType.add

P = 128
PACK = 4
KP = P * PACK
NT = 512
PASSES = K // KP
BLOCKS = H // KP
HALVES = S // NT
QUADRANTS = P // 32
RING = 4

PAIRS = PACK // 2

LAST_CHUNKS = ((0, 256), (256, 384), (384, 512))
NARROW = 128
LEAD = 4
W2_ORDER_STEP = 2
W1_QUANT_STEPS = (5, 7)
WEAVE_STEPS = ((7, 9), (10, 11), (12, 13), (15,), (19,), (23,))
OUT_BANKS = (("b0", "b1"), ("b2", "b3"), ("x3", "x1"), ("x2", "x0"))
H_QUANT_STEPS = (15, 17, 18)

ROOM = 8192
TABLE0_AT = 6144
LATE_AT = {"w1_01": 0, "w2_raw1": 8192, "w3": 10240, "w1_11": 12288}
W1_EARLY_AT = (20480, 28672)
B_FIRST_AT = (20480, 22528, 28672, 30720, 24576, 26624)
TABLE1_AT = 36864
W2_PLANES1_AT = TABLE1_AT
W1_FIRST_AT = 47104
W2_PLANES0_AT = 49152
W1_SHARED_AT = 45056


def tile_list_seawater_horner_surrogate_kernel(
    tc, tab_words, tab_scales, offs, w1, w2_words, w2_scales, quad, cons, w3_words, w3_scales, out
):
    nc = tc.nc
    with ExitStack() as ctx:
        keep = ctx.enter_context(tc.tile_pool(name="keep", bufs=1))
        ring = ctx.enter_context(tc.tile_pool(name="ring", bufs=2))
        placed = ctx.enter_context(tc.tile_pool(name="placed", bufs=1))
        psum = ctx.enter_context(tc.psum_pool(name="psum", bufs=1))

        offsets = keep.tile([P, S // 16], U16, name="offsets")
        nc.sync.dma_start(offsets[:], offs)

        q_col = keep.tile([P, BLOCKS, PACK], F32, name="q_col")
        c_col = keep.tile([P, BLOCKS, PACK], F32, name="c_col")
        w2_by_block = w2_words.bitcast(I32).rearrange("a p (b c) -> b p a c", b=BLOCKS)
        w2_raw = [keep.tile([P, PASSES, KP // 2], I32, name="w2_raw0", align_bytes=64)]
        nc.sync.dma_start(q_col[:], quad.rearrange("(b p t) -> p b t", p=P, t=PACK))
        nc.sync.dma_start(w2_raw[0][:], w2_by_block[0])
        nc.sync.dma_start(c_col[:], cons.rearrange("(b p t) -> p b t", p=P, t=PACK))

        scale_window = keep.tile([P, T], U8, name="scale_window", align_bytes=64)
        weight_rows = keep.tile([P, PASSES, H], U8, name="weight_rows", align_bytes=64)
        v_planes = keep.tile([P, PASSES, S], U8, name="v_planes", align_bytes=64)
        nc.vector.memset(scale_window[:].bitcast(I32), 0)
        nc.sync.dma_start(scale_window[0:P:4, :].bitcast(I32), tab_scales.bitcast(I32).rearrange("a q t -> q a t"))
        nc.vector.memset(weight_rows[:].rearrange("p a c -> p (a c)").bitcast(I32), 0)
        nc.vector.memset(v_planes[:].rearrange("p a c -> p (a c)").bitcast(I32), 0)

        def load_rows(src, width):
            for d in range(QUADRANTS):
                nc.sync.dma_start(
                    weight_rows[32 * d : 32 * d + 4, :, 0:width].bitcast(I32),
                    src[:, 4 * d : 4 * d + 4, :].rearrange("a r c -> r a c").bitcast(I32),
                )

        def load_table(a, at):
            window = placed.tile([P, T], I32, name=f"table{a}", align_bytes=64, offset=at)
            nc.sync.dma_start(window[:], tab_words[a].rearrange("p t i -> p (t i)").bitcast(I32))
            return window

        w1_raw = {}

        def load_w1(a, b, at):
            raw = placed.tile([P, PACK, KP], F32, name=f"w1_raw{a}{b}", align_bytes=64, offset=at)
            rows = w1[a * KP : (a + 1) * KP, b * KP : (b + 1) * KP]
            nc.sync.dma_start(raw[:], rows.rearrange("(p j) c -> p j c", j=PACK))
            w1_raw[a, b] = raw

        table = [load_table(0, TABLE0_AT)]
        load_rows(w2_scales, H)
        table.append(load_table(1, TABLE1_AT))
        load_w1(0, 0, W1_EARLY_AT[0])
        load_w1(1, 0, W1_EARLY_AT[1])

        w2_codes, w2_planes = {}, {}

        def order_w2_words(b):
            w2_codes[b] = keep.tile([P, PASSES, PACK, 2 * P], U8, name=f"w2_codes{b}", align_bytes=64)
            src = w2_raw[b][:].bitcast(U16)
            nc.scalar.copy(w2_codes[b][:].bitcast(U16), src.rearrange("p a (m t) -> p a t m", t=PACK))

        def order_w2_scales(b, t0, t1, at):
            planes = placed.tile([P, PASSES, t1 - t0, P], U8, name=f"w2_planes{b}{t0}", align_bytes=64, offset=at)
            src = weight_rows[:, :, b * KP : (b + 1) * KP].rearrange("p a (m t) -> p a t m", t=PACK)
            nc.vector.tensor_copy(planes[:], src[:, :, t0:t1])
            for t in range(t0, t1):
                w2_planes[b, t] = planes[:, :, t - t0, :]

        v_codes = {}

        def gather_words(a, half):
            lists = offsets[:, half * (NT // 16) : (half + 1) * (NT // 16)]
            v_codes[a, half] = keep.tile([P, NT], I32, name=f"v_codes{a}{half}", align_bytes=64)
            nc.vector.tensor_copy(v_codes[a, half][:].bitcast(U32), table[a][:].bitcast(U32).indirect(lists))

        order_w2_words(0)
        scales_got = keep.tile([P, S], U8, name="scales_got", align_bytes=64)
        nc.vector.tensor_copy(scales_got[:], scale_window[:].indirect(offsets[:]))
        for d in range(QUADRANTS):
            nc.scalar.dma_start(
                v_planes[32 * d : 32 * d + 4].rearrange("p a c -> p (a c)").bitcast(I32),
                scales_got[32 * d : 32 * d + 32 : 4].bitcast(I32),
            )
        gather_words(0, 0)
        gather_words(0, 1)
        load_w1(0, 1, LATE_AT["w1_01"])
        load_w1(1, 1, LATE_AT["w1_11"])
        w2_raw.append(placed.tile([P, PASSES, KP // 2], I32, name="w2_raw1", align_bytes=64, offset=LATE_AT["w2_raw1"]))
        nc.sync.dma_start(w2_raw[1][:], w2_by_block[1])
        w3_codes = placed.tile([P, PASSES, N], I32, name="w3_codes", align_bytes=64, offset=LATE_AT["w3"])
        nc.sync.dma_start(w3_codes[:], w3_words.rearrange("a p c i -> p a (c i)").bitcast(I32))
        gather_words(1, 0)
        order_w2_scales(0, 0, 3, W2_PLANES0_AT)
        gather_words(1, 1)
        order_w2_scales(1, 2, PACK, W2_PLANES1_AT)

        w1_codes = [keep.tile([P, PASSES, KP], U32, name=f"w1_codes{b}", align_bytes=64) for b in range(BLOCKS)]
        w1_bf16, w1_planes = {}, {}

        def cast_w1(engine, a, b, t0, t1, m0, m1):
            if (a, b, t0) == (1, 0, 0):
                w1_bf16[a, b, t0] = placed.tile([P, 2 * KP], BF16, name="w1_bf100", align_bytes=64, offset=W1_FIRST_AT)
            elif (a, b, t0) in ((1, 0, 2), (0, 1, 0)):
                w1_bf16[a, b, t0] = placed.tile([P, 2 * KP], BF16, name=f"w1_bf{a}{b}{t0}", align_bytes=64, offset=W1_SHARED_AT)
            elif m0 == 0:
                w1_bf16[a, b, t0] = keep.tile([P, (t1 - t0) * KP], BF16, name=f"w1_bf{a}{b}{t0}", align_bytes=64)
            dst = w1_bf16[a, b, t0][:].rearrange("p (t m j) -> p m j t", t=t1 - t0, j=PACK)[:, m0:m1]
            src = w1_raw[a, b][:].rearrange("p j (m t) -> p m j t", t=PACK)[:, m0:m1, :, t0:t1]
            if engine == "gpsimd":
                by_slot = "p m j t -> p t m j"
                nc.gpsimd.tensor_scalar(dst.rearrange(by_slot), src.rearrange(by_slot), 1.0, 0.0, MULT, ADD)
            elif engine == "scalar":
                nc.scalar.copy(dst, src)
            else:
                nc.vector.tensor_copy(dst, src)

        def quantize_w1(a, b, t0, t1):
            if (a, b, t0) == (0, 1, 0):
                plane = placed.tile([P, 2 * P], U8, name="w1_plane010", align_bytes=64, offset=B_FIRST_AT[5])
            else:
                plane = keep.tile([P, (t1 - t0) * P], U8, name=f"w1_plane{a}{b}{t0}", align_bytes=64)
            codes = w1_codes[b][:, a, t0 * P : t1 * P]
            nc.vector.quantize_mx(out=codes.bitcast(FP8X4), scales=plane[:], in_=w1_bf16[a, b, t0][:])
            for t in range(t0, t1):
                w1_planes[a, b, t] = plane[:, (t - t0) * P : (t - t0 + 1) * P]

        groups = [(b, half) for b in range(BLOCKS) for half in range(HALVES)]
        last_group = len(groups) - 1
        chunks = [(g, 0, NT) for g in range(last_group)] + [(last_group, c0, c1) for c0, c1 in LAST_CHUNKS]
        last_chunk = len(chunks) - 1
        steps = [(ch, t) for ch in range(len(chunks)) for t in range(PACK)]
        banks = []
        for i, (ch, t) in enumerate(steps):
            if t % (NT // (chunks[ch][2] - chunks[ch][1])) == 0:
                banks.append([])
            banks[-1].append(i)
        x_bank, out_ps = {}, {}
        b_sb, x_ps, inner, y_chunk, h_slots, h_woven, h_mx = {}, {}, {}, {}, {}, {}, {}

        def first_stage(acc, codes, plane, a, nth, c0, c1):
            nc.tensor.matmul_mx(
                out=acc,
                lhsT=codes,
                lhsT_scale=plane,
                rhs=v_codes[a, c0 // NT][:, c0 % NT : c0 % NT + c1 - c0].bitcast(FP8X4),
                rhs_scale=v_planes[:, a, c0:c1],
                start=(nth == 0),
                stop=(nth == PASSES - 1),
            )

        def make_b(u):
            g, t = divmod(u, PACK)
            b, half = groups[g]
            acc = psum.tile([P, NT], F32, name="b_ps", tag=f"b{u % RING}")
            for a in range(PASSES):
                codes = w2_codes[b][:, a, t, :].bitcast(FP4X4)
                first_stage(acc[:], codes, w2_planes[b, t][:, a, :], a, a, half * NT, (half + 1) * NT)
            if u < len(B_FIRST_AT):
                b_sb[g, t] = placed.tile([P, NT], F32, name=f"b_sb{u}", align_bytes=64, offset=B_FIRST_AT[u])
            else:
                b_sb[g, t] = ring.tile([P, NT], F32, name="b_sb", bufs=2 * RING)
            nc.scalar.copy(b_sb[g, t][:], acc[:])

        def matmul_x(bank, nths, order):
            if nths[0] == 0:
                whole = psum.tile([P, NT], F32, name="x_ps", tag=f"x{0 if bank == len(banks) - 1 else bank % RING}")
            for place, i in enumerate(banks[bank]):
                ch, t = steps[i]
                g, c0, c1 = chunks[ch]
                b, half = groups[g]
                if nths[0] == 0:
                    x_ps[i] = whole[:, place * (c1 - c0) : (place + 1) * (c1 - c0)]
                    x_bank[i] = whole[:]
                for nth in nths:
                    a = order[nth]
                    codes = w1_codes[b][:, a, t * P : (t + 1) * P].bitcast(FP8X4)
                    first_stage(x_ps[i], codes, w1_planes[a, b, t], a, nth, half * NT + c0, half * NT + c1)

        def is_narrow(ch):
            return ch == last_chunk

        def horner_inner(i):
            ch, t = steps[i]
            g, c0, c1 = chunks[ch]
            if is_narrow(ch):
                if t == 0:
                    inner[ch, "all"] = keep.tile([P, NT], F32, name=f"inner{ch}")
                inner[i] = inner[ch, "all"][:, t * (c1 - c0) : (t + 1) * (c1 - c0)]
            else:
                inner[i] = ring.tile([P, c1 - c0], F32, name="inner", bufs=3)
            q_t = q_col[:, groups[g][0], t : t + 1]
            nc.vector.scalar_tensor_tensor(inner[i][:], x_ps[i], q_t, b_sb[g, t][:, c0:c1], MULT, ADD)

        def horner_outer(i):
            ch, t = steps[i]
            g, c0, c1 = chunks[ch]
            if t == 0:
                h_woven[ch] = keep.tile([P, c1 - c0, PACK], BF16, name=f"h_woven{ch}", align_bytes=64)
            if is_narrow(ch):
                if t == PACK - 1:
                    y_chunk[ch] = keep.tile([P, PACK, c1 - c0], F32, name=f"y_chunk{ch}")
                    nc.vector.tensor_tensor(y_chunk[ch][:].rearrange("p t n -> p (t n)"), inner[ch, "all"][:], x_bank[i], MULT)
                return
            if t == 0:
                h_slots[ch] = keep.tile([P, PACK, c1 - c0], BF16, name=f"h_slots{ch}", align_bytes=64)
            y = ring.tile([P, c1 - c0], F32, name="y", bufs=8)
            nc.vector.tensor_tensor(y[:], inner[i][:], x_ps[i], MULT)
            nc.gpsimd.tensor_scalar(h_slots[ch][:, t, :], y[:], 1.0, c_col[:, groups[g][0], t : t + 1], MULT, ADD)

        def weave(ch, piece):
            g, c0, c1 = chunks[ch]
            width = (c1 - c0) // len(WEAVE_STEPS[ch])
            cols = slice(piece * width, (piece + 1) * width)
            dst = h_woven[ch][:, cols, :].rearrange("p (c i) t -> p c t i", i=4)
            if is_narrow(ch):
                src = y_chunk[ch][:, :, cols].rearrange("p t (c i) -> p c t i", i=4)
                c_t = c_col[:, groups[g][0], :].unsqueeze(1).unsqueeze(3).to_broadcast([P, width // 4, PACK, 4])
                nc.vector.tensor_tensor(dst, src, c_t, ADD)
            else:
                nc.scalar.copy(dst, h_slots[ch][:, :, cols].rearrange("p t (c i) -> p c t i", i=4))

        def quantize_h(ch):
            g, c0, c1 = chunks[ch]
            codes = keep.tile([P, c1 - c0], U32, name=f"h_codes{ch}", align_bytes=64)
            plane = keep.tile([P, c1 - c0], U8, name=f"h_plane{ch}", align_bytes=64)
            nc.vector.quantize_mx(
                out=codes[:].bitcast(FP8X4), scales=plane[:], in_=h_woven[ch][:].rearrange("p n t -> p (n t)")
            )
            h_mx[ch] = (codes, plane)

        def second_stage(ch):
            g, c0, c1 = chunks[ch]
            half = groups[g][1]
            first_codes, first_plane = h_mx[groups.index((0, half))]
            operands = [(first_codes[:, c0:c1], first_plane[:, c0:c1]), (h_mx[ch][0][:], h_mx[ch][1][:])]
            accs = [psum.tile([P, c1 - c0], F32, name="o_ps", tag=OUT_BANKS[ch - HALVES][n]) for n in range(N // P)]
            for b, (codes, plane) in enumerate(operands):
                for n in range(N // P):
                    nc.tensor.matmul_mx(
                        out=accs[n][:],
                        lhsT=w3_codes[:, b, n * P : (n + 1) * P].bitcast(FP8X4),
                        lhsT_scale=weight_rows[:, b, n * P : (n + 1) * P],
                        rhs=codes.bitcast(FP8X4),
                        rhs_scale=plane,
                        start=(b == 0),
                        stop=(b == BLOCKS - 1),
                    )
            out_ps[ch] = accs

        def store(ch, n, copy, queue):
            g, c0, c1 = chunks[ch]
            half = groups[g][1]
            res = keep.tile([P, c1 - c0], F32, name=f"res{ch}{n}")
            copy(res[:], out_ps[ch][n][:])
            queue.dma_start(out[n * P : (n + 1) * P, half * NT + c0 : half * NT + c1], res[:])

        cast_w1("scalar", 0, 0, 0, 2, 0, P)
        cast_w1("vector", 0, 0, 2, 4, 0, P)
        quantize_w1(0, 0, 0, 2)
        for u in range(2):
            make_b(u)
        for bank in range(2):
            matmul_x(bank, (0,), (0, 1))
        cast_w1("vector", 1, 0, 0, 2, 0, P)
        quantize_w1(0, 0, 2, 4)
        quantize_w1(1, 0, 0, 2)
        for bank in range(2):
            matmul_x(bank, (1,), (0, 1))
        cast_w1("scalar", 1, 0, 2, 4, 0, P)
        order_w2_scales(0, 3, PACK, W1_FIRST_AT)
        order_w2_scales(1, 0, 2, W1_FIRST_AT + 256)
        load_rows(w3_scales, N)
        for u in range(2, LEAD):
            make_b(u)
        quantize_w1(1, 0, 2, 4)
        horner_inner(0)
        cast_w1("gpsimd", 0, 1, 0, 2, 0, P)
        filled = 2
        for i in range(len(steps) - 1):
            if i == 0:
                cast_w1("scalar", 0, 1, 2, PACK, 0, P)
            if i == W2_ORDER_STEP:
                cast_w1("scalar", 1, 1, 0, 2, 0, P)
                order_w2_words(1)
            if i in W1_QUANT_STEPS:
                t0 = 2 * W1_QUANT_STEPS.index(i)
                for a in range(PASSES):
                    quantize_w1(a, 1, t0, t0 + 2)
            pairs_ready = sum(i >= step for step in W1_QUANT_STEPS)
            ahead = i + LEAD if pairs_ready == 2 else min(i + LEAD, HALVES * PACK + 2 * pairs_ready)
            while filled < min(ahead, len(banks) - (i < 14)):
                matmul_x(filled, (0, 1), (1, 0) if filled < PACK else (0, 1))
                filled = filled + 1
            for u in range(LEAD, len(groups) * PACK):
                if i == (u - LEAD if u < 3 * PACK else u // 2 + 2):
                    make_b(u)
            if i == W2_ORDER_STEP + 1:
                cast_w1("scalar", 1, 1, 2, PACK, 0, P)
            if i in H_QUANT_STEPS:
                ch = H_QUANT_STEPS.index(i)
                quantize_h(ch)
                if groups[chunks[ch][0]][0] == BLOCKS - 1:
                    second_stage(ch)
                    store(ch, 0, nc.scalar.copy, nc.sync)
            horner_inner(i + 1)
            horner_outer(i)
            for ch in range(last_chunk):
                if i in WEAVE_STEPS[ch]:
                    weave(ch, WEAVE_STEPS[ch].index(i))
            if i == H_QUANT_STEPS[-1] + 1:
                store(HALVES, 1, nc.scalar.copy, nc.sync)
        quantize_h(last_chunk - 2)
        second_stage(last_chunk - 2)
        store(last_chunk - 2, 0, nc.scalar.copy, nc.sync)
        horner_outer(len(steps) - 1)
        quantize_h(last_chunk - 1)
        second_stage(last_chunk - 1)
        weave(last_chunk, 0)
        store(last_chunk - 2, 1, nc.vector.tensor_copy, nc.sync)
        quantize_h(last_chunk)
        second_stage(last_chunk)
        for n in range(N // P):
            store(last_chunk - 1, n, nc.scalar.copy, nc.sync)
        store(last_chunk, 0, nc.scalar.copy, nc.scalar)
        store(last_chunk, 1, nc.vector.tensor_copy, nc.sync)
